import numpy as np, ml_dtypes
CORES = [9,25,41,57]
N = 4
BF = ml_dtypes.bfloat16
V, NF, NS, J, AM, RO = 512, 4096, 2048, 10, 255, 4
NV = N * V
def parts(rng):
    x = rng.integers(0, 256, (N, 8, 16, V)); y = rng.integers(0, 256, (N, 8, 16, NF)); f = rng.integers(0, NF, (N, 8, 16, NS))
    c = rng.integers(0, NV, (N, 8, 16, V)); e = rng.integers(0, NS, (N, 8, V))
    th = rng.integers(1180, 1440, (N, 8, 1)) + rng.integers(-60, 61, (N, 8, 16))
    return x, y, f, c, e, th
def halves(rng, n, edge, w):
    x = rng.integers(0, w, (N, 8, 16, V)); h = NF // 2; s = rng.integers(0, 2, (N, 8, h)); m = np.zeros((N, 8, NF), np.int64)
    m[..., 0::2] = s; m[..., 1::2] = 1 - s
    y = rng.integers(0, w, (N, 8, 16, NF)) + (256 - w) * m[:, :, None, :]
    r = (np.argsort(rng.random((N, 8, 16, NS)), axis=2) < n[:, :, None, :]).astype(np.int64)
    u = rng.integers(0, h, r.shape); u = np.where(rng.random(r.shape) < edge, (h - 1) * rng.integers(0, 2, r.shape), u)
    f = 2 * u + (np.take_along_axis(s, u.reshape(N, 8, -1), 2).reshape(u.shape) ^ r)
    return x, y, f
def pack(x, y, f, c, e, th):
    return {"x0": np.ascontiguousarray(x.reshape(N, 128, V)).astype(np.float32).astype(BF), "frm": np.ascontiguousarray(y.reshape(N, 128, NF)).astype(np.float32).astype(BF),
            "rol": np.ascontiguousarray(f.reshape(N, 128, NS)).astype(np.int32), "cas": np.ascontiguousarray(c.reshape(N, 128, V)).astype(np.int32),
            "sc0": np.ascontiguousarray(e).astype(np.int32), "th": np.ascontiguousarray(th.reshape(N, 128, 1)).astype(np.int32)}
def setup_inputs(rng):
    return pack(*parts(rng))
def setup_inputs_spread(rng):
    x, y, f, c, e, th = parts(rng); w = rng.choice(np.array([1.0, 2.0, 4.0]), (N, 8, 1, 1))
    x = (rng.random(x.shape) * np.exp2(rng.integers(0, 9, (N, 8, 1, V)))).astype(np.int64)
    y = (rng.random(y.shape) * np.exp2(rng.integers(0, 9, (N, 8, 1, NF)))).astype(np.int64)
    f = np.minimum((NF * rng.random(f.shape) ** w).astype(np.int64), NF - 1); c = NV - 1 - np.minimum((NV * rng.random(c.shape) ** w).astype(np.int64), NV - 1)
    e = np.minimum((NS * rng.random(e.shape) ** w[..., 0]).astype(np.int64), NS - 1)
    th = np.minimum((4080 * rng.random((N, 8, 1)) ** 2 * rng.random((N, 8, 16))).astype(np.int64), 4079)
    return pack(x, y, f, c, e, th)
def setup_inputs_ends(rng):
    x, y, f, c, e, th = parts(rng); k = np.arange(16)
    def flat(n):
        return 255 * np.where(rng.random((N, 8, 1, n)) < 0.5, rng.integers(0, 2, (N, 8, 1, n)), rng.integers(0, 2, (N, 8, 16, n)))
    x, y = flat(V), flat(NF)
    y[..., 0] = 255 * rng.integers(0, 2, (N, 8, 1)); y[..., NF - 1] = 255 - y[..., 0]
    x[0, :, :, 0] = 255 * rng.integers(0, 2, (8, 1)); x[N - 1, :, :, V - 1] = 255 * rng.integers(0, 2, (8, 1))
    f = np.where(rng.random(f.shape) < 0.85, (NF - 1) * rng.integers(0, 2, f.shape), f)
    c = np.where(rng.random(c.shape) < 0.85, (NV - 1) * rng.integers(0, 2, c.shape), c)
    e = np.where(rng.random(e.shape) < 0.85, (NS - 1) * rng.integers(0, 2, e.shape), e)
    th = 4079 * (rng.random((N, 8, 16)) < rng.choice(np.array([0.0, 0.25, 0.5, 1.0]), (N, 8, 1))).astype(np.int64)
    th[:, 7] = 4079 * ((k & 3) == 3)
    y[:, 7, :, 0] = 0; y[:, 7, :, NF - 1] = 255; x[0, 7, :, 0] = 0; x[N - 1, 7, :, V - 1] = 255; f[:, 7, :, NS - 1] = (NF - 1) * (k & 1)
    y[:, 6, :, 0] = 255; y[:, 6, :, NF - 1] = 255; x[0, 6, :, 0] = 0; x[N - 1, 6, :, V - 1] = 0; f[:, 6, :, NS - 1] = (NF - 1) * (1 - (k & 1))
    for g in (6, 7):
        c[:, g, :, V - 2:] = ((NV - 1) * ((k >> 1) & 1))[:, None]; e[:, g, V - 2:] = NS - 1
    return pack(x, y, f, c, e, th)
def setup_inputs_corners(rng):
    x, y, f, c, e, th = parts(rng); n = rng.choice(np.array([0, 1, J - 1, J, J + 1, 15, 16]), (N, 8, NS))
    n[..., 0] = J - 1; n[..., NS - 1] = J; n[..., NS - 2] = J - 1; n[::2, ::2, 0] = J; n[::2, 1::2, NS - 1] = J - 1
    x, y, f = halves(rng, n, 0.2, 8)
    e = np.where(rng.random(e.shape) < 0.5, rng.choice(np.array([0, 1, NS - 2, NS - 1]), e.shape), e)
    me = (np.arange(N)[:, None] * V + np.arange(V))[:, None, None, :]; kind = ((np.arange(N)[:, None] + np.arange(8)) & 3)[:, :, None, None]
    own = np.where(rng.random(c.shape) < 0.5, me, c); nxt = (me + 1 + np.arange(16)[:, None]) % NV; few = rng.choice(np.array([0, V - 1, NV - V, NV - 1]), c.shape)
    c = np.where(kind == 0, own, np.where(kind == 1, nxt, np.where(kind == 2, few, c)))
    return pack(x, y, f, c, e, rng.integers(300, 1600, (N, 8, 16)))
def setup_inputs_crowd(rng):
    x, y, f, c, e, th = parts(rng); a, g = np.arange(N)[:, None], np.arange(8)[None, :]
    part = ((a >= 2) & ((a & 1) == 0))[:, :, None]
    sp = rng.integers(0, NS, (N, 8, 1)); n = rng.integers(15, 17, (N, 8, NS))
    n = np.where(((a >= 2) & ((g & 1) == 1))[:, :, None], rng.integers(0, 17, n.shape), n); np.put_along_axis(n, sp, J - 1, 2)
    bit = rng.integers(0, 2, (N, 8, NS // 2)); strong = np.zeros((N, 8, NS), np.int64); strong[..., 0::2] = bit; strong[..., 1::2] = 1 - bit
    n = np.where(part, np.where(strong == 1, rng.integers(15, 17, n.shape), rng.integers(0, J, n.shape)), n)
    x, y, f = halves(rng, n, 0.1, 4)
    e = np.where((g & 1)[:, :, None] == 0, (sp + 1) & (NS - 1), (sp + 1 + rng.integers(0, NS - 1, (N, 8, V))) & (NS - 1))
    hit = rng.integers(0, 2, (N, 8, V))
    for q in range(2, N, 2):
        m = (AM + 1) * (1 + 2 * int(rng.integers(0, 2 * V // (AM + 1))))
        o = np.argsort((rng.random((8, V // 2)) + rng.random((8, 1))).reshape(-1)); z = np.zeros(4 * V, np.int64); z[o[:m]] = 1
        hit[q, :, 0::2] = z.reshape(8, V // 2)
    u = rng.integers(0, NS // 2, (N, 8, V)); e = np.where(part, 2 * u + (np.take_along_axis(bit, u, 2) ^ hit), e)
    less = rng.random((N, 8)) < 0.5; less[0] = False; less[1] = False; less[2::2] = False; less[1, rng.integers(0, 8)] = True; less[3, 7] = True
    at = 2 * rng.integers(0, V // 2, (N, 8)); at[:, 7] = V - 2
    for q in range(N):
        for j in range(8):
            if less[q, j]: e[q, j, at[q, j]:at[q, j] + 2] = sp[q, j, 0]
    three = np.take_along_axis(rng.integers(0, NV, (N, 8, 3)), rng.integers(0, 3, (N, 8, 16 * V)), 2).reshape(c.shape)
    kind = (g & 3)[:, :, None, None]; one = rng.integers(0, NV, (1, 8, 1, 1))
    c = np.where(kind == 0, one, np.where(kind == 1, three, c)); c[1::2, 0::4, 15, V - 1] = rng.integers(0, NV, c[1::2, 0::4, 15, V - 1].shape)
    loose = np.argsort(rng.random((N, 8, 16)), axis=2) < min(4, 15 - J)
    th = np.where(loose, rng.integers(4024, 4041, (N, 8, 16)), rng.integers(4080 - AM, 3984, (N, 8, 16)))
    low = (((g & 3) == 1) & (a != 1))[:, :, None]
    return pack(x, y, f, c, e, np.where(low, rng.integers(300, 1600, (N, 8, 16)), th))
def setup_inputs_ties(rng):
    x, y, f, c, e, th = parts(rng); pt = rng.integers(0, 16, (8, 16, 1))
    x = 20 * rng.integers(0, 13, (N, 8, 1, V)) + pt; y = 20 * rng.integers(0, 13, (N, 8, 1, NF)) + pt
    th = 320 * rng.integers(2, 6, (N, 8, 1)) + rng.integers(-1, 2, (N, 8, 16))
    return pack(x, y, f, c, e, th)
def check_inputs(d):
    bad = []
    for k, lo, hi in (("x0", 0, 255), ("frm", 0, 255), ("rol", 0, NF - 1), ("cas", 0, NV - 1), ("sc0", 0, NS - 1), ("th", 0, 4079)):
        v = np.asarray(d[k]).astype(np.float64)
        if not (np.min(v) >= lo and np.max(v) <= hi): bad.append("range of " + k)
        elif np.any(v != np.floor(v)): bad.append("whole numbers in " + k)
    return bad
def reference(x0, frm, rol, cas, sc0, th):
    x = x0.astype(np.float32).astype(np.int64).reshape(N, 8, 16, V); y = frm.astype(np.float32).astype(np.int64).reshape(N, 8, 16, NF)
    f = rol.astype(np.int64).reshape(N, 8, 16, NS); c = cas.astype(np.int64).reshape(N, 8, 16, V); e = sc0.astype(np.int64).reshape(N, 8, V)
    lim = th.astype(np.int64).reshape(N, 8, 16, 1); jumps = np.zeros(N, np.int64)
    for t in range(RO):
        own = np.arange(t & 1, V, 2)
        xa = np.array(x.transpose(1, 2, 0, 3)).reshape(8, 16, NV); ca = np.array(c.transpose(1, 2, 0, 3)).reshape(8, 16, NV)
        for a in range(N):
            ev = e[a][:, own]; ck = c[a][:, :, own]; fk = np.take_along_axis(f[a], ev[:, None, :], 2)
            yk = np.take_along_axis(y[a], fk.reshape(8, 1, -1), 2).reshape(8, 16, 16, -1); xk = np.take_along_axis(xa, ck.reshape(8, 1, -1), 2).reshape(8, 16, 16, -1)
            dist = np.add.reduce(np.abs(yk - xk), axis=1)
            b = np.argmin(dist, axis=1)[:, None, :]
            rej = dist > lim[a] + (jumps[a] & AM)
            jump = np.add.reduce(rej.astype(np.int64), axis=1)[:, None, :] >= J
            fb = np.take_along_axis(fk, b, 1); cb = np.take_along_axis(ck, b, 1)
            yb = np.take_along_axis(y[a], fb, 2); cc = np.take_along_axis(ca, cb, 2); xo = xa[:, :, a * V + own]
            x[a][:, :, own] = np.where(jump, (xo + yb) >> 1, np.abs(xo - yb))
            c[a][:, :, own] = np.where(rej & ~jump, cc, ck)
            e[a][:, own] = np.where(jump, fb & (NS - 1), (ev[:, None, :] + 1) & (NS - 1))[:, 0]
            jumps[a] = np.add.reduce(jump.reshape(-1).astype(np.int64))
    return {"yx": x.reshape(N, 128, V).astype(np.float32).astype(BF), "yc": c.reshape(N, 128, V).astype(np.float32), "ye": e.astype(np.float32)}

@@ -1,0 +1,398 @@
+from concourse.bass import DstId, RemoteDMATransfer
+from concourse.mybir import AluOpType, ActivationFunctionType
+
+V, NF, NS, RO = 512, 4096, 2048, 4
+H = "float16"
+MAGIC = 12582912.0
+
+SCRATCH = {
+    "XN": ("sbuf", [128, 4 * V], "bfloat16"), "cass": ("sbuf", [128, V], "int32"),
+    "frms": ("sbuf", [128, NF], "bfloat16"), "rols": ("sbuf", [128, NS], "int32"),
+    "scs": ("sbuf", [128, 32], "int32"), "sc8": ("sbuf", [128, V], "int32"), "sc8f": ("sbuf", [128, V], "float32"),
+    "ths": ("sbuf", [128, 4], "int32"),
+    "XT": ("sbuf", [128, 5 * 1024], "bfloat16"), "CT": ("sbuf", [128, 5 * 1024], "float32"),
+    "YG": ("sbuf", [128, RO * 4096], "bfloat16"), "DD": ("sbuf", [128, RO * 4096], "bfloat16"),
+    "AB": ("sbuf", [128, RO * 4096], "bfloat16"),
+    "fOff": ("sbuf", [128, RO * 256], "uint16"), "cOff": ("sbuf", [128, RO * 256], "uint16"),
+    "fJ": ("sbuf", [128, RO * 256], "float32"), "encA": ("sbuf", [128, RO * 256], "int32"),
+    "encB": ("sbuf", [128, RO * 256], "int32"), "x3": ("sbuf", [128, RO * 256], "float32"),
+    "scan": ("sbuf", [128, RO * 256], "float32"), "rs": ("sbuf", [128, RO * 256], "bfloat16"),
+    "sg": ("sbuf", [128, RO * 256], "bfloat16"), "su": ("sbuf", [128, RO * 256], "bfloat16"),
+    "hh": ("sbuf", [128, RO * 256], H), "qq": ("sbuf", [128, RO * 256], H),
+    "t1": ("sbuf", [128, RO * 256], H), "t2": ("sbuf", [128, RO * 256], H),
+    "selc": ("sbuf", [128, RO * 256], H), "slf": ("sbuf", [128, RO * 256], H),
+    "kI": ("sbuf", [128, RO * 16], "int32"), "pI": ("sbuf", [128, RO * 16], "int32"), "bI": ("sbuf", [128, RO * 16], "int32"),
+    "eA": ("sbuf", [128, RO * 16], "int32"), "eI": ("sbuf", [128, RO * 16], "int32"),
+    "pL": ("sbuf", [128, RO * 16], "uint16"), "bL": ("sbuf", [128, RO * 16], "uint16"), "cL": ("sbuf", [128, RO * 16], "uint16"),
+    "eL": ("sbuf", [128, 6 * 16], "uint16"), "eC": ("sbuf", [128, 32], "uint16"), "e1": ("sbuf", [128, RO * 16], "float32"),
+    "rsum": ("sbuf", [128, RO], "float32"), "aI": ("sbuf", [128, RO], "int32"), "aM": ("sbuf", [128, RO], "int32"),
+    "nthr": ("sbuf", [128, RO], "float32"),
+    "xout": ("sbuf", [128, V], "bfloat16"), "cout": ("sbuf", [128, V], "float32"), "eout": ("sbuf", [128, V], "float32"),
+    "ramp": ("sbuf", [128, NS], "float32"), "rmp1": ("sbuf", [128, 256], "bfloat16"),
+    "ones": ("sbuf", [128, 144], "bfloat16"), "comb": ("sbuf", [128, 144], "bfloat16"), "tmpz": ("sbuf", [128, 144], "bfloat16"),
+    "Zb": ("sbuf", [128, 144], "bfloat16"), "Zh": ("sbuf", [128, 144], H), "Zw": ("sbuf", [128, 144], "bfloat16"),
+    "Z8": ("sbuf", [128, 144], "float32"), "one8": ("sbuf", [128, 144], "float32"),
+    "tmpb": ("sbuf", [128, 128], "bfloat16"), "BD": ("sbuf", [128, 128], "bfloat16"), "Ib": ("sbuf", [128, 128], "bfloat16"),
+    "I2": ("sbuf", [128, 128], "bfloat16"), "I32": ("sbuf", [128, 128], "bfloat16"), "UW": ("sbuf", [128, 128], "bfloat16"),
+    "If": ("sbuf", [128, 128], "float32"), "I75": ("sbuf", [128, 128], H), "I25": ("sbuf", [128, 128], H),
+    "I50": ("sbuf", [128, 128], H), "w32": ("sbuf", [128, 128], "float32"), "Im": ("sbuf", [128, 128], "bfloat16"),
+    "rows": ("sbuf", [128, 128 * 3], "bfloat16"), "one1": ("sbuf", [128, 256], "bfloat16"),
+    "seg": ("sbuf", [128, 256], "float32"),
+    "ioA": ("sbuf", [128, 16], "int32"), "ioB": ("sbuf", [128, 16], "int32"), "ioC": ("sbuf", [128, 16], "int32"),
+    "ioD": ("sbuf", [128, 16], "int32"), "OH": ("sbuf", [128, 16], "bfloat16"), "turn": ("sbuf", [128, 16], "uint16"),
+    "lo256": ("sbuf", [128, 1], "float32"), "ck": ("sbuf", [128, 512], "float32"),
+    "pK": ("psum", [128, 512], "float32"), "pD": ("psum", [128, 512], "float32"), "pN": ("psum", [128, 512], "float32"),
+    "pU": ("psum", [128, 512], "float32"), "pX": ("psum", [128, 512], "float32"), "pC": ("psum", [128, 512], "float32"),
+    "pB": ("psum", [128, 512], "float32"), "pZ": ("psum", [128, 512], "float32"),
+}
+LOADS = ["x0", "sc", "cas", "rol", "frm", "th", "sc8"]
+SEMAPHORES = (["cV", "cS", "cP", "cG", "sent", "stored", "ck2", "ck3"] + ["ld_" + n for n in LOADS]
+              + ["xa%d" % t for t in range(RO)] + ["ca%d" % t for t in range(RO)])
+
+CHUNKS = [("S", 2), ("S", 2), ("V", 4), ("V", 4), ("V", 3), ("V", 1)]
+YU = 2
+ORDER = {
+    "V": "one8 ones rowa Im seg0 seg ioD rowc ioC eC1 rowb comb0 eC0 I50 OH comb w32 cs1 encA1 nthr0 s8f1 encB1 cs0 s8f0 I75 turn "
+         "encA0 cOff0 fOff0 fOff1 lo256 If encB0 Zh Zw eL01 fJ0 one1 Y0_4 Y0_14 Y0_2 e1_01 I25 X0_2 X0_3 X0_4 X0_5 Y1_10 Y1_4 scan0 "
+         "kI0 pI0 bI0 pL0 bL0 h0 q0 selc0 UW fJ1 slf0 cL0 xo aI1 t10 eA0 t20 cOff1 aM1 eI0 X1_3 X1_2 X1_4 eL2 X1_5 fJ2 encA2 fOff2 "
+         "scan1 kI1 nthr1 pI1 bI1 pL1 bL1 h1 selc1 q1 Y2_8 slf1 cL1 Y2_6 t11 aI2 t21 encB2 aM2 eA1 cOff2 eI1 encA3 X2_3 X2_2 eL3 "
+         "X2_4 fJ3 X2_5 encB3 fOff3 cOff3 scan2 nthr2 kI2 pI2 pL2 bI2 h2 q2 aI3 bL2 Y3_2 selc2 Y3_14 cL2 t12 xe t22 slf2 X3_2 X3_3 "
+         "X3_4 X3_5 aM3 e1_2 eA2 eI2 eL4 nthr3 e1_3 scan3 kI3 bI3 pI3 bL3 pL3 selc3 h3 slf3 cL3 q3 t13 t23 eA3 eI3 eL5",
+    "S": "I2 x3_0 Y0_6 Y0_8 Y0_12 Y0_0 Y0_10 X0_1 X0_0 A0_1 A0_0 A0_2 A0_3 A0_4 I32 A0_5 Y1_14 rs0 x3_1 sg0 Y1_0 xn0 Y1_6 Y1_8 su0 "
+         "Y1_2 Y1_12 cn0 X1_1 X1_0 A1_3 A1_1 A1_0 A1_2 A1_4 A1_5 x3_2 Y2_2 rs1 sg1 Y2_0 xn1 Y2_4 su1 Y2_12 Y2_10 cn1 Y2_14 X2_0 X2_1 "
+         "A2_3 A2_1 A2_2 x3_3 A2_0 A2_4 A2_5 Y3_6 rs2 sg2 Y3_0 xn2 Y3_4 Y3_10 su2 Y3_8 Y3_12 cn2 X3_0 X3_1 A3_2 A3_1 A3_0 A3_3 A3_4 "
+         "A3_5 rs3 sg3 ce su3 xn3 eo2 cn3 eo3",
+    "P": "e0 my0_1 mx0_1 my0_0 mx0_0 k0_0 k0_0a d0_0 k0_1a d0_4 k0_2a k0_3a d0_8 k0_4a k0_5a d0_12 n0 k0_1 v0_0 v2_0 v3_0 b0 a0 u0 "
+         "c0_0 zs0 zf0 c1_0 my1_1 c2_0 mx1_1 my1_0 c0_1 mx1_0 k1_3a d1_8 d1_0 v0_1 k1_0a k1_2a k1_1a k1_4a k1_5a d1_4 d1_12 n1 a1 u1 "
+         "v2_1 v3_1 b1 zs1 my2_0 zf1 k0_2 c1_1 c2_1 my2_1 mx2_1 mx2_0 k2_3a k2_1a d2_8 k2_2a d2_4 k2_0a d2_0 k2_4a k2_5a d2_12 k0_3 "
+         "v0_2 n2 v2_2 u2 a2 v3_2 c0_2 b2 c1_2 c2_2 my3_0 c0_3 zs2 v0_3 my3_1 mx3_0 mx3_1 zf2 k3_2a d3_4 k3_1a d3_0 k3_0a k3_3a k3_4a "
+         "k3_5a d3_12 d3_8 n3 b3 u3 v2_3 zs3 v3_3 zf3 c1_3 c2_3",
+}
+
+
+def build(g, core, T, topo, order_text):
+    A, F = AluOpType, ActivationFunctionType
+    q = T.rank_of(core)
+    vec, act, pe = g.vector, g.scalar, g.tensor
+    ops, order = {}, {"V": [], "S": [], "P": [], "G": [], "Y": []}
+
+    def op(eng, name, deps, fn, ext=(), alt=None):
+        fns = {eng: fn}
+        if alt is not None:
+            fns["V" if eng == "S" else "S"] = alt
+        ops[name] = (fns, list(deps), list(ext))
+        order[eng].append(name)
+
+    def mm(name, deps, calls, ext=()):
+        op("P", name, deps, lambda: [pe.matmul(*c) for c in calls][-1], ext)
+
+    def copy(eng, name, deps, out, src, ext=()):
+        fs, fv = (lambda: act.activation(out, src, F.Copy)), (lambda: vec.tensor_copy(out, src))
+        op(eng, name, deps, fs if eng == "S" else fv, ext, fv if eng == "S" else fs)
+
+    def scaled(name, deps, out, src, k, ext=()):
+        op("S", name, deps, lambda: act.activation(out, src, F.Copy, scale=k), ext, lambda: vec.tensor_scalar(out, src, k, None, A.mult))
+
+    def tt(name, deps, out, a, b, alu, ext=()):
+        op("V", name, deps, lambda: vec.tensor_tensor(out, a, b, alu), ext)
+
+    def ts(name, deps, out, a, s1, o1, s2=None, o2=None, ext=()):
+        if o2 is None:
+            op("V", name, deps, lambda: vec.tensor_scalar(out, a, s1, None, o1), ext)
+        else:
+            op("V", name, deps, lambda: vec.tensor_scalar(out, a, s1, s2, o1, o2), ext)
+
+    def tc(name, deps, out, a, ext=()):
+        op("V", name, deps, lambda: vec.tensor_copy(out, a), ext)
+
+    def fill(name, deps, out, k):
+        op("V", name, deps, lambda: vec.memset(out, k))
+
+    def ld(n):
+        return ("ld_" + n, 16)
+
+    def own(buf, slot):
+        return buf[:, slot * 1024 + q * 256: slot * 1024 + q * 256 + 256]
+
+    def r256(buf, t):
+        return buf[:, t * 256:(t + 1) * 256]
+
+    def r16(buf, t):
+        return buf[:, t * 16:(t + 1) * 16]
+
+    def turned(buf, t):
+        return r256(buf, t).indirect(T.turn[:, 0:16])
+
+    def sel(z, i):
+        return z[:, 15 - i:143 - i]
+
+    def yname(t, u):
+        return "Y%d_%d" % (t, u - u % YU)
+
+    def ygather(t):
+        for u in range(0, 16, YU):
+            copy("S", yname(t, u), ["fOff%d" % t], T.YG[:, t * 4096 + u * 256: t * 4096 + (u + YU) * 256],
+                 T.frms[:, 0:NF].indirect(T.fOff[:, t * 256 + u * 16: t * 256 + (u + YU) * 16]), [ld("frm")])
+
+    mine0 = T.XN[:, q * V:(q + 1) * V]
+
+    def ownx(t):
+        if t < 2:
+            return T.XN[:, q * V + t:(q + 1) * V:2], [], [ld("x0")]
+        return own(T.XT, t), ["xn%d" % (t - 2)], []
+    for n, dst, src in (("x0", mine0, T.x0[:]), ("sc", T.scs[:], T.sc0[:]), ("cas", T.cass[:], T.cas[:]),
+                        ("sc8", T.sc8[0:8, :], T.sc0[:]), ("th", T.ths[:, 0:1], T.th[:]),
+                        ("rol", T.rols[:], T.rol[:]), ("frm", T.frms[:], T.frm[:])):
+        op("Y", "ld_" + n, [], lambda n=n, dst=dst, src=src: g.sync.dma_start(dst, src).then_inc(T.sem["ld_" + n], 16))
+
+    fill("ones", [], T.ones[:], 1.0)
+    fill("comb0", [], T.comb[:], 0.0)
+    fill("one8", [], T.one8[0:8, :], 1.0)
+    fill("comb", ["comb0"], T.comb[:, 15:144:16], 1.0)
+    fill("seg0", [], T.seg[:], 0.0)
+    fill("w32", [], T.w32[:], 1.0 / 32)
+    fill("rowa", [], T.rows[0:1, 0:128], 1.0 / 4096)
+    fill("rowb", [], T.rows[0:1, 128:256], -0.125)
+    fill("rowc", [], T.rows[0:1, 256:384], MAGIC)
+    fill("one1", [], T.one1[0:1, :], 1.0)
+    fill("seg", ["seg0"], T.seg[:, 0:256:16], 8192.0)
+    op("G", "ioA", [], lambda: g.iota(T.ioA[:], [[1, 16]], 0, 16))
+    op("G", "ioB", [], lambda: g.iota(T.ioB[:], [[-1, 16]], 16, 1))
+    op("G", "Ib", ["ones"], lambda: g.affine_select(T.Ib[:], T.ones[:, 0:128], [[-1, 128]], A.is_equal, 0.0, 0, 1))
+    op("G", "Z8", ["one8"], lambda: g.affine_select(T.Z8[0:8, :], T.one8[0:8, :], [[-1, 144]], A.is_equal, 0.0, 15, 16))
+    op("G", "tmpz", ["comb"], lambda: g.affine_select(T.tmpz[:], T.comb[:], [[1, 144]], A.is_ge, 0.0, 0, -1))
+
+    others = [c for c in T.cores if c != core]
+    ids = [DstId(rid=topo.addr(c)[0], pnc=topo.addr(c)[1]) for c in others]
+    eng = [e for e in topo.engines(core, others[0]) if all(e in topo.engines(core, c) for c in others)]
+    half = len(eng) // 2
+    full_mask = sum(1 << e for e in eng)
+    masks = [sum(1 << e for e in eng[:half]), sum(1 << e for e in eng[half:])]
+    arrive = len(eng) * len(others)
+    sent = [0]
+
+    def send(name, dep, parts, sem, ext=()):
+        ms = [full_mask] if len(parts) == 1 else masks
+        sent[0] += len(eng)
+        op("G", name, dep, lambda: g.remote_dma_fused(
+            [RemoteDMATransfer(dst_ids=ids, dma_engine_mask=m, remote_sem=sem, srcs=[p], dsts=[p] * len(ids))
+             for p, m in zip(parts, ms)], local_sem=T.sem.sent), ext)
+
+    send("sx0", [], [mine0], T.sem.xa0, [ld("x0")])
+    copy("V", "xo", [], T.XT[:, 1024:2048], T.XN[:, 1:4 * V:2], [ld("x0"), ("xa0", arrive)])
+    for p in range(2):
+        tc("eC%d" % p, [], r16(T.eC, p), T.scs[:, p:32:2], [ld("sc")])
+    ts("ioC", ["ioA"], T.ioC[:], T.ioA[:], 255, A.bitwise_and)
+    ts("ioD", ["ioB"], T.ioD[:], T.ioB[:], 15, A.bitwise_and)
+    tc("turn", ["ioC"], T.turn[:], T.ioC[:])
+    ts("OH", ["ioD"], T.OH[:], T.ioD[:], 0.0, A.is_equal)
+    ts("lo256", ["ioD"], T.lo256[:], T.ioD[:, 0:1], 256.0, A.mult)
+    for p in range(2):
+        tc("cs%d" % p, [], own(T.CT, p), T.cass[:, p:V:2], [ld("cas")])
+    send("sc0", ["cs0", "cs1"], [own(T.CT, 0), own(T.CT, 1)], T.sem.ca0)
+    op("G", "Zb", ["tmpz"], lambda: g.affine_select(T.Zb[:], T.tmpz[:], [[-1, 144]], A.is_ge, 0.0, 15, 1))
+    op("G", "rmp1", [], lambda: g.iota(T.rmp1[0:1, :], [[1, 256]], 0, 0, allow_small_or_imprecise_dtypes=True))
+    op("G", "tmpb", ["ones"], lambda: g.affine_select(T.tmpb[:], T.ones[:, 0:128], [[16, 8], [0, 16]], A.is_ge, 0.0, 15, -1))
+    op("G", "BD", ["tmpb"], lambda: g.affine_select(T.BD[:], T.tmpb[:], [[-16, 8], [0, 16]], A.is_ge, 0.0, 0, 1))
+    op("G", "ramp", [], lambda: g.iota(T.ramp[:], [[1, NS]], 0, 0, allow_small_or_imprecise_dtypes=True))
+
+    def enc(t, dep):
+        s = str(t)
+        ts("encA" + s, [dep], r256(T.encA, t), own(T.CT, t), 1024.5, A.mult, 1024.0 * (t & 1) - 0.25, A.add)
+        ts("encB" + s, ["encA" + s], r256(T.encB, t), r256(T.encA, t), NS - 1, A.bitwise_and)
+        if t == 0:
+            tc("cOff0", ["cs0", "turn"], r256(T.cOff, 0), own(T.CT, 0).indirect(T.turn[:, 0:16]))
+        else:
+            tc("cOff" + s, ["encB" + s, "turn"], r256(T.cOff, t), turned(T.encB, t))
+
+    def fj(t, dep):
+        ts("fJ%d" % t, [dep], r256(T.fJ, t), T.rols[:, 0:NS].indirect(r16(T.eL, t)), 2048.0, A.subtract, ext=[ld("rol")])
+
+    for p in range(2):
+        tc("s8f%d" % p, [], T.sc8f[0:8, p * 256:(p + 1) * 256], T.sc8[0:8, p:V:2], [ld("sc8")])
+    mm("e0", ["s8f0", "s8f1", "Z8"],
+       [(T.pZ[:, 0:32], T.Z8[0:8, 15 - lo:143 - lo], T.sc8f[0:8, lo:V:16], lo == 0, lo == 15) for lo in range(16)])
+    enc(0, "cs0")
+    ts("I75", ["Ib"], T.I75[:], T.Ib[:], 0.75, A.mult)
+    ts("I25", ["Ib"], T.I25[:], T.Ib[:], -0.25, A.mult)
+    ts("I50", ["Ib"], T.I50[:], T.Ib[:], 0.5, A.mult)
+    scaled("I2", ["Ib"], T.I2[:], T.Ib[:], 2.0)
+    scaled("I32", ["Ib"], T.I32[:], T.Ib[:], 32.0)
+    scaled("Im", ["Ib"], T.Im[:], T.Ib[:], -1.0)
+    scaled("If", ["Ib"], T.If[:], T.Ib[:], 1.0)
+    for p in range(2):
+        scaled("x3_%d" % p, [], r256(T.x3, p), ownx(p)[0], 3.0, [ld("x0")])
+    enc(1, "cs1")
+    ts("nthr0", [], T.nthr[:, 0:1], T.ths[:, 0:1], -1.0, A.mult, -0.5, A.add, ext=[ld("th")])
+    tc("eL01", ["e0"], T.eL[:, 0:32], T.pZ[:, 0:32])
+    ts("e1_01", ["e0"], T.e1[:, 0:32], T.pZ[:, 0:32], 1.0, A.add)
+    for p in range(2):
+        tc("fOff%d" % p, ["eC%d" % p], r256(T.fOff, p), T.rols[:, 0:NS].indirect(r16(T.eC, p)), [ld("rol")])
+    fj(0, "eL01")
+    fj(1, "eL01")
+    tc("Zh", ["Zb"], T.Zh[:], T.Zb[:])
+    scaled("Zw", ["Zb"], T.Zw[:], T.Zb[:], 256.0)
+    tt("UW", ["I32", "BD"], T.UW[:], T.I32[:], T.BD[:], A.subtract)
+    ygather(0)
+
+    for t in range(RO):
+        s, pv, n1, n2 = str(t), str(t - 1), str(t + 1), str(t + 2)
+        last = t == RO - 1
+
+        def prev(*names):
+            return [n + pv for n in names] if t else []
+        xme, xdep, xext = ownx(t)
+        cdep = "cs" + s if t < 2 else "cn%d" % (t - 2)
+        tab_x = [[], ["xn0", "xo"], ["xn1"], ["xn2"]][t]
+        tab_c = ["cs0", "cs1"] if t == 0 else ["cn" + pv]
+        xa = [ld("x0")] + [("xa%d" % k, arrive) for k in range(t + 1)]
+        ca = [("ca%d" % k, arrive) for k in range(t + 1)]
+        win = slice(t * 1024, (t + 2) * 1024)
+        pK, pX, pC = T.pK[:, 0:256], T.pX[:, 0:256], T.pC[:, 0:256]
+        mm("k0_" + s, ["rowa", "rmp1"] + prev("scan"), [(pK, T.rows[0:1, 0:128], T.rmp1[0:1, :], True, False)])
+        mm("v0_" + s, ["rowb", "one1", "I2"] + xdep + prev("xn"),
+           [(pX, T.rows[0:1, 128:256], T.one1[0:1, :], True, False), (pX, T.I2[:], xme, False, False)], xext)
+        mm("c0_" + s, [cdep, "If"] + prev("cn"), [(pC, T.If[:], own(T.CT, t), True, False)])
+        u, role, done, klast = 0, [], [], "k0_" + s
+        for ci, (who, n) in enumerate(CHUNKS):
+            a, b = t * 4096 + u * 256, t * 4096 + (u + n) * 256
+            cn = "%d_%d" % (t, ci)
+            ys = sorted(set(yname(t, k) for k in range(u, u + n)))
+            gat = (T.XT[:, win] if t else T.XN[:, 0:4 * V]).indirect(T.cOff[:, a // 16:b // 16])
+            if who == "V":
+                tt("X" + cn, ["cOff" + s] + tab_x + ys, T.DD[:, a:b], gat, T.YG[:, a:b], A.subtract, xa)
+                src, dep = T.DD[:, a:b], "X" + cn
+            else:
+                src = (T.pU if ci == 0 else T.pN)[:, 0:b - a]
+                free = prev("su") if ci == 0 else (["aI" + s] if t else [])
+                copy("S", "X" + cn, ["cOff" + s] + tab_x, T.DD[:, a:b], gat, xa)
+                mm("my" + cn, ys + ["Im"] + free, [(src, T.Im[:], T.YG[:, a:b], True, False)])
+                mm("mx" + cn, ["my" + cn, "X" + cn, "Ib"], [(src, T.Ib[:], T.DD[:, a:b], False, True)])
+                dep = "mx" + cn
+            op("S", "A" + cn, [dep], lambda a=a, b=b, src=src: act.activation(T.AB[:, a:b], src, F.Abs))
+            done.append((u, u + n, "A" + cn))
+            klast = "k" + cn + "a"
+            mm(klast, ["A" + cn, "Zb", "k0_" + s] + (["k%d_%da" % (t, j) for j in range(ci)] if u + n == 16 else []),
+               [(pK, sel(T.Zb, lo), T.AB[:, t * 4096 + lo * 256:t * 4096 + lo * 256 + 256], False, lo == 15) for lo in range(u, u + n)])
+            u += n
+            while 4 * len(role) + 4 <= u:
+                u0 = 4 * len(role)
+                role.append("d%d_%d" % (t, u0))
+                mm(role[-1], [x for (i, j, x) in done if i < u0 + 4 and j > u0] + ["Zb"] + prev("rs"),
+                   [(T.pD[:, u0 * 16:u0 * 16 + 64], sel(T.Zb, k), T.AB[:, t * 4096 + u0 * 256 + k:t * 4096 + (u0 + 4) * 256:16],
+                     k == 0, k == 15) for k in range(16)])
+        alldone = [x for (i, j, x) in done]
+        op("S", "rs" + s, role + ["nthr" + s],
+           lambda t=t: act.activation(r256(T.rs, t), T.pD[:, 0:256], F.Sign, bias=T.nthr[:, t:t + 1]))
+        mm("n" + s, ["rs" + s, "BD"] + alldone + (["aI" + s] if t else []), [(T.pN[:, 0:256], T.BD[:], r256(T.rs, t), True, True)])
+        mm("u" + s, ["rs" + s, "UW"] + alldone + prev("su"), [(T.pU[:, 0:256], T.UW[:], r256(T.rs, t), True, True)])
+        acc = None if last else T.rsum[:, t:t + 1]
+        op("S", "sg" + s, ["n" + s],
+           lambda t=t, acc=acc: act.activation(r256(T.sg, t), T.pN[:, 0:256], F.Sign, bias=-3.0, accum_out=acc))
+        op("S", "su" + s, ["u" + s], lambda t=t: act.activation(r256(T.su, t), T.pU[:, 0:256], F.Sign, bias=-29.0))
+        op("V", "scan" + s, [klast, "seg"], lambda t=t, pK=pK: vec.tensor_tensor_scan(r256(T.scan, t), T.seg[:], pK, 0.0, A.add, A.min))
+        ts("kI" + s, ["scan" + s, "lo256"], r16(T.kI, t), T.scan[:, t * 256 + 15:(t + 1) * 256:16], 4096.0, A.mult, T.lo256[:, 0:1], A.add)
+        ts("pI" + s, ["kI" + s], r16(T.pI, t), r16(T.kI, t), 4095, A.bitwise_and)
+        ts("bI" + s, ["kI" + s], r16(T.bI, t), r16(T.kI, t), 15, A.bitwise_and)
+        tc("pL" + s, ["pI" + s], r16(T.pL, t), r16(T.pI, t))
+        tc("bL" + s, ["bI" + s], r16(T.bL, t), r16(T.bI, t))
+        tt("h" + s, ["pL" + s, "x3_" + s], r256(T.hh, t), T.YG[:, t * 4096:(t + 1) * 4096].indirect(r16(T.pL, t)), r256(T.x3, t), A.subtract)
+        tt("q" + s, ["h" + s, "sg" + s, "turn"], r256(T.qq, t), turned(T.sg, t), r256(T.hh, t), A.mult)
+        mm("v2_" + s, ["v0_" + s, "h" + s, "I75"], [(pX, T.I75[:], r256(T.hh, t), False, False)])
+        mm("v3_" + s, ["v2_" + s, "q" + s, "I25", "rowc"],
+           [(pX, T.I25[:], r256(T.qq, t), False, False), (pX, T.rows[0:1, 256:384], T.one1[0:1, :], False, True)])
+        xdst = T.xout[:, 1:V:2] if last else own(T.XT, t + 2)
+        op("S", "xn" + s, ["v3_" + s] + (["xe"] if last else []), lambda xdst=xdst, pX=pX: act.activation(xdst, pX, F.Abs, bias=-MAGIC))
+        if last:
+            copy("S", "xe", ["xn2"], T.xout[:, 0:V:2], own(T.XT, 4))
+            copy("S", "ce", ["cn2"], T.cout[:, 0:V:2], own(T.CT, 4))
+            op("Y", "st_x", ["xn" + s, "xe"], lambda: g.sync.dma_start(T.yx[:], T.xout[:]).then_inc(T.sem.stored, 16))
+        else:
+            send("sx" + n1, ["xn" + s], [own(T.XT, t + 2)], T.sem["xa" + n1])
+            ygather(t + 1)
+        onehot = T.OH[:, 0:16].indirect(r16(T.bL, t))
+        tt("selc" + s, ["bL" + s, "OH", "encB" + s], r256(T.selc, t), onehot, r256(T.encB, t), A.mult)
+        mm("b" + s, ["selc" + s, "Zh"] + prev("cL"),
+           [(T.pB[:, 0:16], sel(T.Zh, lo), T.selc[:, t * 256 + lo:(t + 1) * 256:16], lo == 0, lo == 15) for lo in range(16)])
+        tt("slf" + s, ["bL" + s, "OH", "fJ" + s], r256(T.slf, t), onehot, r256(T.fJ, t), A.mult)
+        mm("zs" + s, ["sg" + s, "Zw", "e1_01", "eL01"] + prev("eA"),
+           [(T.pZ[:, 0:16], sel(T.Zw, lo), T.sg[:, t * 256 + lo * 16:t * 256 + lo * 16 + 16], lo == 0, False) for lo in range(16)])
+        tc("cL" + s, ["b" + s], r16(T.cL, t), T.pB[:, 0:16])
+        mine, mext = (T.cass[:, t:V:2], [ld("cas")]) if t < 2 else (r256(T.ck, t - 2), [("ck" + s, 16)])
+        tt("t1" + s, ["cL" + s] + tab_c, r256(T.t1, t), T.CT[:, win].indirect(r16(T.cL, t)), mine, A.subtract, ca + mext)
+        tt("t2" + s, ["t1" + s, "su" + s, "turn"], r256(T.t2, t), turned(T.su, t), r256(T.t1, t), A.mult)
+        mm("zf" + s, ["zs" + s, "slf" + s, "Zh"],
+           [(T.pZ[:, 0:16], sel(T.Zh, lo), T.slf[:, t * 256 + lo:(t + 1) * 256:16], False, lo == 15) for lo in range(16)])
+        mm("c1_" + s, ["c0_" + s, "t1" + s, "I50"], [(pC, T.I50[:], r256(T.t1, t), False, False)])
+        mm("c2_" + s, ["c1_" + s, "t2" + s], [(pC, T.I50[:], r256(T.t2, t), False, True)])
+        copy("S", "cn" + s, ["c2_" + s] + (["ce"] if last else []), T.cout[:, 1:V:2] if last else own(T.CT, t + 2), pC)
+        if last:
+            op("Y", "st_c", ["cn" + s, "ce"], lambda: g.sync.dma_start(T.yc[:], T.cout[:]).then_inc(T.sem.stored, 16))
+        else:
+            send("sc" + n1, ["cn" + s], [own(T.CT, t + 2)], T.sem["ca" + n1])
+            mm("a" + s, ["sg" + s, "w32"], [(T.pN[:, 256:257], T.w32[:], T.rsum[:, t:t + 1], True, True)])
+            ts("aI" + n1, ["a" + s], T.aI[:, t:t + 1], T.pN[:, 256:257], 1024.0, A.add)
+            ts("aM" + n1, ["aI" + n1], T.aM[:, t:t + 1], T.aI[:, t:t + 1], 255, A.bitwise_and)
+            ts("nthr" + n1, ["aM" + n1, "nthr0"], T.nthr[:, t + 1:t + 2], T.aM[:, t:t + 1], -1.0, A.mult, T.nthr[:, 0:1], A.add)
+        tt("eA" + s, ["zf" + s, "e1_01" if t < 2 else "e1_" + s], r16(T.eA, t), T.pZ[:, 0:16], r16(T.e1, t), A.max)
+        ts("eI" + s, ["eA" + s], r16(T.eI, t), r16(T.eA, t), NS - 1, A.bitwise_and)
+        tc("eL" + n2, ["eI" + s], r16(T.eL, t + 2), r16(T.eI, t))
+        if t < 2:
+            op("Y", "ck" + n2, ["cn" + s],
+               lambda t=t, n2=n2: g.sync.dma_start(r256(T.ck, t), own(T.CT, t + 2)).then_inc(T.sem["ck" + n2], 16))
+            fj(t + 2, "eL" + n2)
+            ts("e1_" + n2, ["eI" + s], r16(T.e1, t + 2), r16(T.eI, t), 1.0, A.add)
+            ts("fOff" + n2, ["fJ" + n2, "turn"], r256(T.fOff, t + 2), turned(T.fJ, t + 2), 2048.0, A.add)
+            enc(t + 2, "cn" + s)
+            scaled("x3_" + n2, ["xn" + s], r256(T.x3, t + 2), own(T.XT, t + 2), 3.0)
+        else:
+            copy("S", "eo" + s, ["eL" + n2, "ramp"] + (["eo2"] if last else []), T.eout[:, (t & 1):V:2], T.ramp[:, 0:NS].indirect(r16(T.eL, t + 2)))
+    op("Y", "st_e", ["eo2", "eo3"], lambda: g.sync.dma_start(T.ye[:], T.eout[0:128:16, :]).then_inc(T.sem.stored, 16))
+    if order_text is not None:
+        had = sorted(n for e in order_text for n in order[e])
+        for e in order_text:
+            order[e] = order_text[e].split()
+        assert had == sorted(n for e in order_text for n in order[e])
+    return ops, order, sent[0]
+
+
+def emit(g, T, ops, order, sent):
+    queue = {"V": g.vector, "S": g.scalar, "P": g.tensor, "G": g, "Y": g.sync}
+    counter = {"V": "cV", "S": "cS", "P": "cP", "G": "cG"}
+    where = {n: e for e in order for n in order[e]}
+    needed = set(d for n, o in ops.items() for d in o[1] if not (where[n] == "P" and where[d] == "P"))
+    count = {}
+    for e, names in order.items():
+        k = 0
+        for name in names:
+            if name in needed:
+                k += 1
+                count[name] = k
+    for e, names in order.items():
+        seen = {}
+        for name in names:
+            fns, deps, ext = ops[name]
+            want = {}
+            for d in deps:
+                if e == "P" and where[d] == "P":
+                    assert names.index(d) < names.index(name)
+                    continue
+                k = counter[where[d]]
+                want[k] = max(want.get(k, 0), count[d])
+            for k, v in ext:
+                want[k] = max(want.get(k, 0), v)
+            for k, v in want.items():
+                if seen.get(k, 0) < v:
+                    queue[e].wait_ge(T.sem[k], v)
+                    seen[k] = v
+            ins = fns[e]()
+            if name in count:
+                ins.then_inc(T.sem[counter[e]], 1)
+    g.wait_ge(T.sem.sent, sent)
+    g.sync.wait_ge(T.sem.stored, 48)
+
+
+def rank_program(g, core, T, topo):
+    if T.rank_of(core) is None:
+        return
+    emit(g, T, *build(g, core, T, topo, ORDER))

@@ -2,96 +2,77 @@ from concourse.bass import DstId, RemoteDMATransfer
 from concourse.mybir import AluOpType, ActivationFunctionType
 
 V, NF, NS, RO = 512, 4096, 2048, 4
-H = "float16"
+H, B, F4, I4, U2 = "float16", "bfloat16", "float32", "int32", "uint16"
 MAGIC = 12582912.0
 
+
+def sb(n, dt):
+    return ("sbuf", [128, n], dt)
+
+
 SCRATCH = {
-    "XN": ("sbuf", [128, 4 * V], "bfloat16"), "cass": ("sbuf", [128, V], "int32"),
-    "frms": ("sbuf", [128, NF], "bfloat16"), "rols": ("sbuf", [128, NS], "int32"),
-    "scs": ("sbuf", [128, 32], "int32"), "sc8": ("sbuf", [128, V], "int32"), "sc8f": ("sbuf", [128, V], "float32"),
-    "ths": ("sbuf", [128, 4], "int32"),
-    "XT": ("sbuf", [128, 5 * 1024], "bfloat16"), "CT": ("sbuf", [128, 5 * 1024], "float32"),
-    "YG": ("sbuf", [128, RO * 4096], "bfloat16"), "DD": ("sbuf", [128, RO * 4096], "bfloat16"),
-    "AB": ("sbuf", [128, RO * 4096], "bfloat16"),
-    "fOff": ("sbuf", [128, RO * 256], "uint16"), "cOff": ("sbuf", [128, RO * 256], "uint16"),
-    "fJ": ("sbuf", [128, RO * 256], "float32"), "encA": ("sbuf", [128, RO * 256], "int32"),
-    "encB": ("sbuf", [128, RO * 256], "int32"), "x3": ("sbuf", [128, RO * 256], "float32"),
-    "scan": ("sbuf", [128, RO * 256], "float32"), "rs": ("sbuf", [128, RO * 256], "bfloat16"),
-    "sg": ("sbuf", [128, RO * 256], "bfloat16"), "su": ("sbuf", [128, RO * 256], "bfloat16"),
-    "hh": ("sbuf", [128, RO * 256], H), "qq": ("sbuf", [128, RO * 256], H),
-    "t1": ("sbuf", [128, RO * 256], H), "t2": ("sbuf", [128, RO * 256], H),
-    "selc": ("sbuf", [128, RO * 256], H), "slf": ("sbuf", [128, RO * 256], H),
-    "kI": ("sbuf", [128, RO * 16], "int32"), "pI": ("sbuf", [128, RO * 16], "int32"), "bI": ("sbuf", [128, RO * 16], "int32"),
-    "eA": ("sbuf", [128, RO * 16], "int32"), "eI": ("sbuf", [128, RO * 16], "int32"),
-    "pL": ("sbuf", [128, RO * 16], "uint16"), "bL": ("sbuf", [128, RO * 16], "uint16"), "cL": ("sbuf", [128, RO * 16], "uint16"),
-    "eL": ("sbuf", [128, 6 * 16], "uint16"), "eC": ("sbuf", [128, 32], "uint16"), "e1": ("sbuf", [128, RO * 16], "float32"),
-    "rsum": ("sbuf", [128, RO], "float32"), "aI": ("sbuf", [128, RO], "int32"), "aM": ("sbuf", [128, RO], "int32"),
-    "nthr": ("sbuf", [128, RO], "float32"),
-    "xout": ("sbuf", [128, V], "bfloat16"), "cout": ("sbuf", [128, V], "float32"), "eout": ("sbuf", [128, V], "float32"),
-    "ramp": ("sbuf", [128, NS], "float32"), "rmp1": ("sbuf", [128, 256], "bfloat16"),
-    "ones": ("sbuf", [128, 144], "bfloat16"), "comb": ("sbuf", [128, 144], "bfloat16"), "tmpz": ("sbuf", [128, 144], "bfloat16"),
-    "Zb": ("sbuf", [128, 144], "bfloat16"), "Zh": ("sbuf", [128, 144], H), "Zw": ("sbuf", [128, 144], "bfloat16"),
-    "Z8": ("sbuf", [128, 144], "float32"), "one8": ("sbuf", [128, 144], "float32"),
-    "tmpb": ("sbuf", [128, 128], "bfloat16"), "BD": ("sbuf", [128, 128], "bfloat16"), "Ib": ("sbuf", [128, 128], "bfloat16"),
-    "I2": ("sbuf", [128, 128], "bfloat16"), "I32": ("sbuf", [128, 128], "bfloat16"), "UW": ("sbuf", [128, 128], "bfloat16"),
-    "If": ("sbuf", [128, 128], "float32"), "I75": ("sbuf", [128, 128], H), "I25": ("sbuf", [128, 128], H),
-    "I50": ("sbuf", [128, 128], H), "w32": ("sbuf", [128, 128], "float32"), "Im": ("sbuf", [128, 128], "bfloat16"),
-    "rows": ("sbuf", [128, 128 * 3], "bfloat16"), "one1": ("sbuf", [128, 256], "bfloat16"),
-    "seg": ("sbuf", [128, 256], "float32"),
-    "ioA": ("sbuf", [128, 16], "int32"), "ioB": ("sbuf", [128, 16], "int32"), "ioC": ("sbuf", [128, 16], "int32"),
-    "ioD": ("sbuf", [128, 16], "int32"), "OH": ("sbuf", [128, 16], "bfloat16"), "turn": ("sbuf", [128, 16], "uint16"),
-    "lo256": ("sbuf", [128, 1], "float32"), "ck": ("sbuf", [128, 512], "float32"),
-    "pK": ("psum", [128, 512], "float32"), "pD": ("psum", [128, 512], "float32"), "pN": ("psum", [128, 512], "float32"),
-    "pU": ("psum", [128, 512], "float32"), "pX": ("psum", [128, 512], "float32"), "pC": ("psum", [128, 512], "float32"),
-    "pB": ("psum", [128, 512], "float32"), "pZ": ("psum", [128, 512], "float32"),
+    "XN": sb(4 * V, B), "XT": sb(4 * 1024, B), "CN": sb(V, H), "CH": sb(3 * 1024, H), "CT": sb(4 * V, I4),
+    "frms": sb(NF, B), "rols": sb(NS, I4), "scs": sb(32, I4), "sc8": sb(V, I4), "sc8h": sb(V, H), "ths": sb(4, I4), "thf": sb(1, F4),
+    "YG": sb(RO * 4096, B), "DD": sb(RO * 4096, B), "AB": sb(RO * 4096, B),
+    "fOff": sb(RO * 256, U2), "cOff": sb(RO * 256, U2), "fJ": sb(RO * 256, F4), "mh": sb(RO * 256, H), "x3": sb(RO * 256, H),
+    "turn2": sb(16, U2), "scan": sb(RO * 256, I4), "rej": sb(RO * 256, B), "rejT": sb(RO * 256, B),
+    "hh": sb(RO * 256, H), "qq": sb(RO * 256, H), "t1": sb(RO * 256, H), "t2": sb(RO * 256, H), "sel": sb(RO * 512, H),
+    "kI": sb(RO * 16, I4), "pI": sb(RO * 16, I4), "pL": sb(RO * 16, U2), "nL": sb(RO * 16, U2), "sg": sb(RO * 16, B),
+    "W": sb(RO * 32, F4), "zA": sb(RO * 32, I4), "zI": sb(RO * 32, I4), "zL": sb(RO * 32, U2), "eL": sb(32, U2), "eC": sb(32, U2),
+    "eH": sb(32, H), "rsum": sb(RO, F4), "fl": sb(RO, F4), "fr": sb(RO, F4), "lim": sb(RO * 256, F4), "Zk": sb(144, B),
+    "xout": sb(V, B), "cout": sb(V, F4), "eout": sb(V, F4),
+    "J": sb(256, B), "J16": sb(128, B), "Jm": sb(256, B), "pc": sb(4, I4), "pa": sb(4, I4), "pf": sb(12, F4), "Ga": sb(160, B),
+    "iq": sb(16, I4), "io2": sb(16, I4), "turn": sb(16, U2),
+    "Z1": sb(144, B), "Z2": sb(144, B), "Zm": sb(144, B), "Z8": sb(144, B), "G0": sb(160, B), "G1": sb(160, B),
+    "BD": sb(128, F4), "Ib": sb(128, B), "Im": sb(128, B), "I2": sb(128, B), "Ik": sb(128, B), "Imk": sb(128, B),
+    "Ia": sb(128, B), "w": sb(128, F4), "rows": sb(6 * 256, B), "seg": sb(256, B), "OH": sb(4096, B),
+    "thd": sb(256, F4), "TH": sb(256, F4), "AT": sb(32, B),
 }
+for n in ("pK", "pN", "pX", "pC", "pB", "pM", "pS0", "pS1"):
+    SCRATCH[n] = ("psum", [128, 512], F4)
 LOADS = ["x0", "sc", "cas", "rol", "frm", "th", "sc8"]
-SEMAPHORES = (["cV", "cS", "cP", "cG", "sent", "stored", "ck2", "ck3"] + ["ld_" + n for n in LOADS]
-              + ["xa%d" % t for t in range(RO)] + ["ca%d" % t for t in range(RO)])
+SEMAPHORES = (["cV", "cS", "cP", "cG", "sent", "left0", "oh", "stored"] + ["ld_" + n for n in LOADS]
+              + [k + str(t) for k in ("xa", "ha") for t in range(RO)] + ["ca%d_%d" % (t, r) for t in range(RO) for r in range(4)])
 
-CHUNKS = [("S", 2), ("S", 2), ("V", 4), ("V", 4), ("V", 3), ("V", 1)]
-YU = 2
+HELP = [0, 1, 2, 3]
+CHUNKS = [[("S", 2, "S"), ("S", 2, "S"), ("S", 2, "S"), ("V", 4, "V"), ("V", 3, "V"), ("V", 2, "V"), ("V", 1, "V")]] * 4
+YCH = [[4, 4, 4, 4], [2] * 8, [2] * 8, [2] * 8]
+YV = [[0, 1], [], [], []]
+CNE = "S"
+AND_U16 = False
 ORDER = {
-    "V": "one8 ones rowa Im seg0 seg ioD rowc ioC eC1 rowb comb0 eC0 I50 OH comb w32 cs1 encA1 nthr0 s8f1 encB1 cs0 s8f0 I75 turn "
-         "encA0 cOff0 fOff0 fOff1 lo256 If encB0 Zh Zw eL01 fJ0 one1 Y0_4 Y0_14 Y0_2 e1_01 I25 X0_2 X0_3 X0_4 X0_5 Y1_10 Y1_4 scan0 "
-         "kI0 pI0 bI0 pL0 bL0 h0 q0 selc0 UW fJ1 slf0 cL0 xo aI1 t10 eA0 t20 cOff1 aM1 eI0 X1_3 X1_2 X1_4 eL2 X1_5 fJ2 encA2 fOff2 "
-         "scan1 kI1 nthr1 pI1 bI1 pL1 bL1 h1 selc1 q1 Y2_8 slf1 cL1 Y2_6 t11 aI2 t21 encB2 aM2 eA1 cOff2 eI1 encA3 X2_3 X2_2 eL3 "
-         "X2_4 fJ3 X2_5 encB3 fOff3 cOff3 scan2 nthr2 kI2 pI2 pL2 bI2 h2 q2 aI3 bL2 Y3_2 selc2 Y3_14 cL2 t12 xe t22 slf2 X3_2 X3_3 "
-         "X3_4 X3_5 aM3 e1_2 eA2 eI2 eL4 nthr3 e1_3 scan3 kI3 bI3 pI3 bL3 pL3 selc3 h3 slf3 cL3 q3 t13 t23 eA3 eI3 eL5",
-    "S": "I2 x3_0 Y0_6 Y0_8 Y0_12 Y0_0 Y0_10 X0_1 X0_0 A0_1 A0_0 A0_2 A0_3 A0_4 I32 A0_5 Y1_14 rs0 x3_1 sg0 Y1_0 xn0 Y1_6 Y1_8 su0 "
-         "Y1_2 Y1_12 cn0 X1_1 X1_0 A1_3 A1_1 A1_0 A1_2 A1_4 A1_5 x3_2 Y2_2 rs1 sg1 Y2_0 xn1 Y2_4 su1 Y2_12 Y2_10 cn1 Y2_14 X2_0 X2_1 "
-         "A2_3 A2_1 A2_2 x3_3 A2_0 A2_4 A2_5 Y3_6 rs2 sg2 Y3_0 xn2 Y3_4 Y3_10 su2 Y3_8 Y3_12 cn2 X3_0 X3_1 A3_2 A3_1 A3_0 A3_3 A3_4 "
-         "A3_5 rs3 sg3 ce su3 xn3 eo2 cn3 eo3",
-    "P": "e0 my0_1 mx0_1 my0_0 mx0_0 k0_0 k0_0a d0_0 k0_1a d0_4 k0_2a k0_3a d0_8 k0_4a k0_5a d0_12 n0 k0_1 v0_0 v2_0 v3_0 b0 a0 u0 "
-         "c0_0 zs0 zf0 c1_0 my1_1 c2_0 mx1_1 my1_0 c0_1 mx1_0 k1_3a d1_8 d1_0 v0_1 k1_0a k1_2a k1_1a k1_4a k1_5a d1_4 d1_12 n1 a1 u1 "
-         "v2_1 v3_1 b1 zs1 my2_0 zf1 k0_2 c1_1 c2_1 my2_1 mx2_1 mx2_0 k2_3a k2_1a d2_8 k2_2a d2_4 k2_0a d2_0 k2_4a k2_5a d2_12 k0_3 "
-         "v0_2 n2 v2_2 u2 a2 v3_2 c0_2 b2 c1_2 c2_2 my3_0 c0_3 zs2 v0_3 my3_1 mx3_0 mx3_1 zf2 k3_2a d3_4 k3_1a d3_0 k3_0a k3_3a k3_4a "
-         "k3_5a d3_12 d3_8 n3 b3 u3 v2_3 zs3 v3_3 zf3 c1_3 c2_3",
+    "V": ("one seg0 pa0 pa1 pa2 pf3 pf p256 m8th magic half seg w Ib Z1 Z8 G1a AT io2 turn turn2 OH4 BD eC0 eC1 s8h0 s8h1 thf x3_0 x3_1 "
+          "cs cOff0 mh1 eL fOff0 fOff1 fJ0 Y0_0 Y0_1 fJ1 cOff1",
+          "X#_3 X#_4 A#_3 X#_5 A#_4 X#_6 A#_5 A#_6 scan# rej# kI# pI# pL# h# nL# self# q# selc# rT# cOff#@1 fl#@1 zA# zI# fr#@1 zL# "
+          "t1# eH# e1_#@2 t2# x3_#@2 fJ#@2 fOff#@2 mh#@2"),
+    "S": ("pf5 pf6 pf7 pf9 Im Imk Ia I2 Ik Zk Z2 Zm Wn0 Wn1 G1 G0 OH5 OH6 thd e1_0 e1_1 TH lim0 Y0_2 Y0_3",
+          "X#_0 X#_1 A#_0 X#_2 A#_1 A#_2 lim# Y#_7@1 Y#_5@1 Y#_2@1 Y#_0@1 sg# Y#_1@1 xn# Y#_4@1 Y#_3@1 Y#_6@1 eo# cn#"),
+    "P": ("e0 co1 thm k0 my0_0 my0_1",
+          "co#@1 mx#_0 v# mx#_1 kd#_3 ka#_0 my#_2 mx#_2 ka#_3 kd#_4 kd#_5 ka#_1 ka#_4 ka#_2 kd#_6 ka#_5 ka#_6 n# k#@1 a# vq# b# "
+          "my#_0@1 m# my#_1@1 ef# c#"),
+    "G": ("pc J iq Jm J16 sx0 sc0 xo sx1",
+          "sc#@1 cv#a@1 xe# ce# cv#b@1 cv#c@1 cv#d@1 sx#@2"),
 }
 
 
-def build(g, core, T, topo, order_text):
+def build(g, core, T, topo):
     A, F = AluOpType, ActivationFunctionType
     q = T.rank_of(core)
     vec, act, pe = g.vector, g.scalar, g.tensor
-    ops, order = {}, {"V": [], "S": [], "P": [], "G": [], "Y": []}
+    ops, bank = {}, {}
 
-    def op(eng, name, deps, fn, ext=(), alt=None):
-        fns = {eng: fn}
-        if alt is not None:
-            fns["V" if eng == "S" else "S"] = alt
-        ops[name] = (fns, list(deps), list(ext))
-        order[eng].append(name)
+    def op(eng, name, deps, fn, ext=()):
+        assert name not in ops
+        ops[name] = (eng, fn, list(deps), list(ext))
 
     def mm(name, deps, calls, ext=()):
         op("P", name, deps, lambda: [pe.matmul(*c) for c in calls][-1], ext)
 
     def copy(eng, name, deps, out, src, ext=()):
-        fs, fv = (lambda: act.activation(out, src, F.Copy)), (lambda: vec.tensor_copy(out, src))
-        op(eng, name, deps, fs if eng == "S" else fv, ext, fv if eng == "S" else fs)
+        op(eng, name, deps, (lambda: act.activation(out, src, F.Copy)) if eng == "S" else (lambda: vec.tensor_copy(out, src)), ext)
 
-    def scaled(name, deps, out, src, k, ext=()):
-        op("S", name, deps, lambda: act.activation(out, src, F.Copy, scale=k), ext, lambda: vec.tensor_scalar(out, src, k, None, A.mult))
+    def gcopy(name, deps, out, src, n, ext=()):
+        op("G", name, deps, lambda: g.affine_select(out, src, [[0, n]], A.is_ge, 0.0, 0, 0), ext)
 
     def tt(name, deps, out, a, b, alu, ext=()):
         op("V", name, deps, lambda: vec.tensor_tensor(out, a, b, alu), ext)
@@ -102,8 +83,8 @@ def build(g, core, T, topo, order_text):
         else:
             op("V", name, deps, lambda: vec.tensor_scalar(out, a, s1, s2, o1, o2), ext)
 
-    def tc(name, deps, out, a, ext=()):
-        op("V", name, deps, lambda: vec.tensor_copy(out, a), ext)
+    def lin(name, deps, out, a, scale, bias=0.0):
+        op("S", name, deps, lambda: act.activation(out, a, F.Identity, bias=bias, scale=scale))
 
     def fill(name, deps, out, k):
         op("V", name, deps, lambda: vec.memset(out, k))
@@ -111,129 +92,156 @@ def build(g, core, T, topo, order_text):
     def ld(n):
         return ("ld_" + n, 16)
 
+    def cut(buf, t, n):
+        return buf[:, t * n:(t + 1) * n]
+
     def own(buf, slot):
         return buf[:, slot * 1024 + q * 256: slot * 1024 + q * 256 + 256]
 
-    def r256(buf, t):
-        return buf[:, t * 256:(t + 1) * 256]
-
-    def r16(buf, t):
-        return buf[:, t * 16:(t + 1) * 16]
-
-    def turned(buf, t):
-        return r256(buf, t).indirect(T.turn[:, 0:16])
+    def turned(ap):
+        return ap.indirect(T.turn[:, 0:16])
 
     def sel(z, i):
         return z[:, 15 - i:143 - i]
 
-    def yname(t, u):
-        return "Y%d_%d" % (t, u - u % YU)
+    def ynames(t, a, b):
+        out, u = [], 0
+        for j, n in enumerate(YCH[t]):
+            if u < b and u + n > a:
+                out.append("Y%d_%d" % (t, j))
+            u += n
+        return out
 
     def ygather(t):
-        for u in range(0, 16, YU):
-            copy("S", yname(t, u), ["fOff%d" % t], T.YG[:, t * 4096 + u * 256: t * 4096 + (u + YU) * 256],
-                 T.frms[:, 0:NF].indirect(T.fOff[:, t * 256 + u * 16: t * 256 + (u + YU) * 16]), [ld("frm")])
+        u = 0
+        for j, n in enumerate(YCH[t]):
+            copy("V" if j in YV[t] else "S", "Y%d_%d" % (t, j), ["fOff%d" % t], T.YG[:, t * 4096 + u * 256: t * 4096 + (u + n) * 256],
+                 T.frms[:, 0:NF].indirect(T.fOff[:, t * 256 + u * 16: t * 256 + (u + n) * 16]), [ld("frm")])
+            u += n
 
-    mine0 = T.XN[:, q * V:(q + 1) * V]
-
-    def ownx(t):
-        if t < 2:
-            return T.XN[:, q * V + t:(q + 1) * V:2], [], [ld("x0")]
-        return own(T.XT, t), ["xn%d" % (t - 2)], []
-    for n, dst, src in (("x0", mine0, T.x0[:]), ("sc", T.scs[:], T.sc0[:]), ("cas", T.cass[:], T.cas[:]),
-                        ("sc8", T.sc8[0:8, :], T.sc0[:]), ("th", T.ths[:, 0:1], T.th[:]),
-                        ("rol", T.rols[:], T.rol[:]), ("frm", T.frms[:], T.frm[:])):
+    minex, minec = cut(T.XN, q, V), cut(T.CT, q, V)
+    for n, dst, src in (("x0", minex, T.x0[:]), ("sc", T.scs[:], T.sc0[:]), ("sc8", T.sc8[0:8, :], T.sc0[:]),
+                        ("th", T.ths[:, 0:1], T.th[:]), ("cas", minec, T.cas[:]), ("rol", T.rols[:], T.rol[:]), ("frm", T.frms[:], T.frm[:])):
         op("Y", "ld_" + n, [], lambda n=n, dst=dst, src=src: g.sync.dma_start(dst, src).then_inc(T.sem["ld_" + n], 16))
 
-    fill("ones", [], T.ones[:], 1.0)
-    fill("comb0", [], T.comb[:], 0.0)
-    fill("one8", [], T.one8[0:8, :], 1.0)
-    fill("comb", ["comb0"], T.comb[:, 15:144:16], 1.0)
-    fill("seg0", [], T.seg[:], 0.0)
-    fill("w32", [], T.w32[:], 1.0 / 32)
-    fill("rowa", [], T.rows[0:1, 0:128], 1.0 / 4096)
-    fill("rowb", [], T.rows[0:1, 128:256], -0.125)
-    fill("rowc", [], T.rows[0:1, 256:384], MAGIC)
-    fill("one1", [], T.one1[0:1, :], 1.0)
-    fill("seg", ["seg0"], T.seg[:, 0:256:16], 8192.0)
-    op("G", "ioA", [], lambda: g.iota(T.ioA[:], [[1, 16]], 0, 16))
-    op("G", "ioB", [], lambda: g.iota(T.ioB[:], [[-1, 16]], 16, 1))
-    op("G", "Ib", ["ones"], lambda: g.affine_select(T.Ib[:], T.ones[:, 0:128], [[-1, 128]], A.is_equal, 0.0, 0, 1))
-    op("G", "Z8", ["one8"], lambda: g.affine_select(T.Z8[0:8, :], T.one8[0:8, :], [[-1, 144]], A.is_equal, 0.0, 15, 16))
-    op("G", "tmpz", ["comb"], lambda: g.affine_select(T.tmpz[:], T.comb[:], [[1, 144]], A.is_ge, 0.0, 0, -1))
+    def ownx(t):
+        return (T.XN[:, q * V + t:(q + 1) * V:2], [], [ld("x0")]) if t < 2 else (own(T.XT, t - 1), ["xn%d" % (t - 2)], [])
 
-    others = [c for c in T.cores if c != core]
-    ids = [DstId(rid=topo.addr(c)[0], pnc=topo.addr(c)[1]) for c in others]
-    eng = [e for e in topo.engines(core, others[0]) if all(e in topo.engines(core, c) for c in others)]
-    half = len(eng) // 2
-    full_mask = sum(1 << e for e in eng)
-    masks = [sum(1 << e for e in eng[:half]), sum(1 << e for e in eng[half:])]
+    def ownc(t, a=0, step=1):
+        if t < 2:
+            return T.CN[:, t + 2 * a:V:2 * step], ["cs"]
+        return T.CH[:, (t - 2) * 1024 + q * 256 + a:(t - 2) * 1024 + q * 256 + 256:step], ["cn%d" % (t - 2)]
+
+    others = [T.cores[(q + k) % len(T.cores)] for k in range(1, len(T.cores))]
+    eng = out_engines(topo, core, others)
     arrive = len(eng) * len(others)
     sent = [0]
 
-    def send(name, dep, parts, sem, ext=()):
-        ms = [full_mask] if len(parts) == 1 else masks
-        sent[0] += len(eng)
-        op("G", name, dep, lambda: g.remote_dma_fused(
-            [RemoteDMATransfer(dst_ids=ids, dma_engine_mask=m, remote_sem=sem, srcs=[p], dsts=[p] * len(ids))
-             for p, m in zip(parts, ms)], local_sem=T.sem.sent), ext)
+    def send(name, dep, part, dsts, engs, sem, ext=()):
+        left = T.sem.left0 if name == "sc0" else T.sem.sent
+        sent[0] += 0 if name == "sc0" else len(engs)
+        op("G", name, dep, lambda: write(g, topo, part, dsts, engs, sem, left), ext)
 
-    send("sx0", [], [mine0], T.sem.xa0, [ld("x0")])
-    copy("V", "xo", [], T.XT[:, 1024:2048], T.XN[:, 1:4 * V:2], [ld("x0"), ("xa0", arrive)])
-    for p in range(2):
-        tc("eC%d" % p, [], r16(T.eC, p), T.scs[:, p:32:2], [ld("sc")])
-    ts("ioC", ["ioA"], T.ioC[:], T.ioA[:], 255, A.bitwise_and)
-    ts("ioD", ["ioB"], T.ioD[:], T.ioB[:], 15, A.bitwise_and)
-    tc("turn", ["ioC"], T.turn[:], T.ioC[:])
-    ts("OH", ["ioD"], T.OH[:], T.ioD[:], 0.0, A.is_equal)
-    ts("lo256", ["ioD"], T.lo256[:], T.ioD[:, 0:1], 256.0, A.mult)
-    for p in range(2):
-        tc("cs%d" % p, [], own(T.CT, p), T.cass[:, p:V:2], [ld("cas")])
-    send("sc0", ["cs0", "cs1"], [own(T.CT, 0), own(T.CT, 1)], T.sem.ca0)
-    op("G", "Zb", ["tmpz"], lambda: g.affine_select(T.Zb[:], T.tmpz[:], [[-1, 144]], A.is_ge, 0.0, 15, 1))
-    op("G", "rmp1", [], lambda: g.iota(T.rmp1[0:1, :], [[1, 256]], 0, 0, allow_small_or_imprecise_dtypes=True))
-    op("G", "tmpb", ["ones"], lambda: g.affine_select(T.tmpb[:], T.ones[:, 0:128], [[16, 8], [0, 16]], A.is_ge, 0.0, 15, -1))
-    op("G", "BD", ["tmpb"], lambda: g.affine_select(T.BD[:], T.tmpb[:], [[-16, 8], [0, 16]], A.is_ge, 0.0, 0, 1))
-    op("G", "ramp", [], lambda: g.iota(T.ramp[:], [[1, NS]], 0, 0, allow_small_or_imprecise_dtypes=True))
-
-    def enc(t, dep):
-        s = str(t)
-        ts("encA" + s, [dep], r256(T.encA, t), own(T.CT, t), 1024.5, A.mult, 1024.0 * (t & 1) - 0.25, A.add)
-        ts("encB" + s, ["encA" + s], r256(T.encB, t), r256(T.encA, t), NS - 1, A.bitwise_and)
-        if t == 0:
-            tc("cOff0", ["cs0", "turn"], r256(T.cOff, 0), own(T.CT, 0).indirect(T.turn[:, 0:16]))
+    def send_casts(t, dep, part, ext=()):
+        if t in HELP:
+            h = helper(topo, core)
+            send("sc%d" % t, dep, part, [h], [e for e in topo.engines(core, h) if e not in eng], T.sem["ha%d" % t], ext)
         else:
-            tc("cOff" + s, ["encB" + s, "turn"], r256(T.cOff, t), turned(T.encB, t))
+            send("sc%d" % t, dep, part, others, eng, T.sem["ca%d_%d" % (t, q)], ext)
 
-    def fj(t, dep):
-        ts("fJ%d" % t, [dep], r256(T.fJ, t), T.rols[:, 0:NS].indirect(r16(T.eL, t)), 2048.0, A.subtract, ext=[ld("rol")])
+    def widen(t, dep):
+        for k in range(len(T.cores)):
+            r = (q - k) % len(T.cores)
+            came = [("ca%d_%d" % (t, r), len(eng))] if k else [("left0", len(eng))]
+            gcopy("cv%d" % t + "abcd"[k], dep, T.CT[:, r * V + (t - 1) % 2:(r + 1) * V:2],
+                  T.CH[:, (t - 1) * 1024 + r * 256:(t - 1) * 1024 + (r + 1) * 256], 256, came)
 
+    op("G", "J", [], lambda: g.iota(T.J[:], [[1, 256]], 0, 0, allow_small_or_imprecise_dtypes=True))
+    op("G", "pc", [], lambda: g.iota(T.pc[:, 0:1], [[1, 1]], 0, 1))
+    op("G", "iq", [], lambda: g.iota(T.iq[:], [[1, 16]], 0, 16))
+    send("sx0", [], minex, others, eng, T.sem.xa0, [ld("x0")])
+    op("G", "J16", [], lambda: g.iota(T.J16[:], [[16, 8], [0, 16]], 0, 0, allow_small_or_imprecise_dtypes=True))
+    op("G", "Jm", [], lambda: g.iota(T.Jm[:], [[0, 16], [1, 16]], 0, 0, allow_small_or_imprecise_dtypes=True))
+    for j, m in enumerate((112, 15, 16)):
+        ts("pa%d" % j, ["pc"], T.pa[:, j:j + 1], T.pc[:, 0:1], m, A.bitwise_and)
+    copy("V", "pf", ["pa0", "pa1", "pa2"], T.pf[:, 0:3], T.pa[:, 0:3])
+    copy("V", "pf3", ["pc"], T.pf[:, 3:4], T.pc[:, 0:1])
+    gp, lo1, bit4, pp, lo256, p16, bit, name0 = [T.pf[:, j:j + 1] for j in range(8)]
+    lin("pf5", ["pf3"], p16, pp, 16.0)
+    lin("pf6", ["pf"], bit, bit4, 1.0 / 16)
+    lin("pf7", ["pf"], name0, lo1, 2.0, float(q * V))
+    ts("io2", ["iq"], T.io2[:], T.iq[:], 255, A.bitwise_and)
+    copy("V", "turn", ["io2"], T.turn[:], T.io2[:])
+    ts("Z1", ["J", "pf"], T.Z1[:], T.J[:, 0:144], gp, A.subtract, 15.0, A.is_equal)
+    ts("Ib", ["J", "pf3"], T.Ib[:], T.J[:, 0:128], pp, A.is_equal)
+    ts("Z8", ["J", "pf5"], T.Z8[0:8, :], T.J[0:8, 0:144], T.pf[0:8, 5:6], A.subtract, 15.0, A.is_equal)
+    for n, src, k in (("Zk", "Z1", 4096.0), ("Z2", "Z1", 8192.0), ("Zm", "Z1", -4096.0), ("Im", "Ib", -1.0), ("I2", "Ib", 2.0), ("Ik", "Ib", 4096.0),
+                      ("Imk", "Ib", -2048.0), ("Ia", "Ib", 1024.0)):
+        lin(n, [src], T[n][:], T[src][:], k)
+    ts("G1a", ["J", "pf3"], T.Ga[:], T.J[:, 0:160], pp, A.subtract, 16.0, A.is_equal)
+    lin("G1", ["G1a", "pf6"], T.G1[:], T.Ga[:], bit)
+    lin("pf9", ["pf6"], T.pf[:, 9:10], bit, -1.0, 1.0)
+    lin("G0", ["G1a", "pf9"], T.G0[:], T.Ga[:], T.pf[:, 9:10])
+    ts("BD", ["J16", "pf"], T.BD[:], T.J16[:], gp, A.is_equal)
+    ts("AT", ["J"], T.AT[:], T.J[:, 0:32], 9.5, A.is_lt, 0.5, A.max)
+    fill("w", [], T.w[:], 1.0 / 512)
+    fill("seg0", [], T.seg[:], 0.0)
+    fill("seg", ["seg0"], T.seg[:, 0:256:16], 2.0 ** 25)
+    row = {}
+    for j, (n, k, width) in enumerate((("one", 1.0, 256), ("p256", 256.0, 256), ("m8th", -0.125, 128), ("magic", MAGIC, 128),
+                                       ("half", -255.0 / 512, 128))):
+        row[n] = T.rows[0:1, j * 256:j * 256 + width]
+        fill(n, [], row[n], k)
+    ts("OH4", ["Jm", "pf"], T.OH[:, 0:256], T.Jm[:], lo1, A.is_equal)
+    for j in (4, 5):
+        copy("S", "OH%d" % (j + 1), ["OH%d" % j], T.OH[:, 16 << j:32 << j], T.OH[:, 0:16 << j])
+    for j in (1, 2, 3):
+        op("Y", "oh%d" % j, ["OH6"], lambda j=j: g.sync.dma_start(cut(T.OH, j, 1024), cut(T.OH, 0, 1024)).then_inc(T.sem.oh, 16), [ld("frm")])
+    lin("Wn0", ["J", "pf7"], T.W[:, 0:16], T.J[:, 0:16], 32.0, name0)
+    lin("Wn1", ["Wn0"], T.W[:, 32:48], T.W[:, 0:16], 1.0, 1.0)
+    copy("V", "thf", [], T.thf[:], T.ths[:, 0:1], [ld("th")])
+    lin("thd", ["thf", "OH4"], T.thd[:], T.OH[:, 0:256], T.thf[:, 0:1])
+    mm("thm", ["thd", "BD"], [(T.pM[:, 0:256], T.BD[:], T.thd[:], True, True)])
+    lin("TH", ["thm"], T.TH[:], T.pM[:, 0:256], 4096.0, 128.5 * 4096)
+    lin("lim0", ["thm"], cut(T.lim, 0, 256), T.pM[:, 0:256], 4096.0, 4096.0)
+
+    copy("V", "cs", [], T.CN[:], minec, [ld("cas")])
+    send_casts(0, [], minec, [ld("cas"), ld("frm")])
+    ts("turn2", ["io2"], T.turn2[:], T.io2[:], 2.0, A.mult)
+    copy("V", "cOff0", ["turn2"], cut(T.cOff, 0, 256), minec.indirect(T.turn2[:, 0:16]), [ld("cas")])
     for p in range(2):
-        tc("s8f%d" % p, [], T.sc8f[0:8, p * 256:(p + 1) * 256], T.sc8[0:8, p:V:2], [ld("sc8")])
-    mm("e0", ["s8f0", "s8f1", "Z8"],
-       [(T.pZ[:, 0:32], T.Z8[0:8, 15 - lo:143 - lo], T.sc8f[0:8, lo:V:16], lo == 0, lo == 15) for lo in range(16)])
-    enc(0, "cs0")
-    ts("I75", ["Ib"], T.I75[:], T.Ib[:], 0.75, A.mult)
-    ts("I25", ["Ib"], T.I25[:], T.Ib[:], -0.25, A.mult)
-    ts("I50", ["Ib"], T.I50[:], T.Ib[:], 0.5, A.mult)
-    scaled("I2", ["Ib"], T.I2[:], T.Ib[:], 2.0)
-    scaled("I32", ["Ib"], T.I32[:], T.Ib[:], 32.0)
-    scaled("Im", ["Ib"], T.Im[:], T.Ib[:], -1.0)
-    scaled("If", ["Ib"], T.If[:], T.Ib[:], 1.0)
+        copy("V", "eC%d" % p, [], cut(T.eC, p, 16), T.scs[:, p:32:2], [ld("sc")])
+        copy("V", "s8h%d" % p, [], T.sc8h[0:8, p * 256:(p + 1) * 256], T.sc8[0:8, p:V:2], [ld("sc8")])
+    mm("e0", ["s8h0", "s8h1", "Z8"], [(T.pB[:, 0:32], T.Z8[0:8, 15 - lo:143 - lo], T.sc8h[0:8, lo:V:16], lo == 0, lo == 15) for lo in range(16)])
+    copy("V", "eL", ["e0"], T.eL[:], T.pB[:, 0:32])
     for p in range(2):
-        scaled("x3_%d" % p, [], r256(T.x3, p), ownx(p)[0], 3.0, [ld("x0")])
-    enc(1, "cs1")
-    ts("nthr0", [], T.nthr[:, 0:1], T.ths[:, 0:1], -1.0, A.mult, -0.5, A.add, ext=[ld("th")])
-    tc("eL01", ["e0"], T.eL[:, 0:32], T.pZ[:, 0:32])
-    ts("e1_01", ["e0"], T.e1[:, 0:32], T.pZ[:, 0:32], 1.0, A.add)
-    for p in range(2):
-        tc("fOff%d" % p, ["eC%d" % p], r256(T.fOff, p), T.rols[:, 0:NS].indirect(r16(T.eC, p)), [ld("rol")])
-    fj(0, "eL01")
-    fj(1, "eL01")
-    tc("Zh", ["Zb"], T.Zh[:], T.Zb[:])
-    scaled("Zw", ["Zb"], T.Zw[:], T.Zb[:], 256.0)
-    tt("UW", ["I32", "BD"], T.UW[:], T.I32[:], T.BD[:], A.subtract)
+        lin("e1_%d" % p, ["eL"], T.W[:, p * 32 + 16:p * 32 + 32], T.pB[:, p * 16:p * 16 + 16], 1.0, 1.0)
+        copy("V", "fOff%d" % p, ["eC%d" % p], cut(T.fOff, p, 256), T.rols[:, 0:NS].indirect(cut(T.eC, p, 16)), [ld("rol")])
+
+    def prepare(t, free):
+        s = str(t)
+        x, xd, xe = ownx(t)
+        ts("x3_" + s, xd, cut(T.x3, t, 256), x, 3.0, A.mult, ext=xe)
+        lst, dep = (cut(T.eL, t, 16), "eL") if t < 2 else (T.zL[:, (t - 2) * 32 + 16:(t - 2) * 32 + 32], "zL%d" % (t - 2))
+        ts("fJ" + s, [dep], cut(T.fJ, t, 256), T.rols[:, 0:NS].indirect(lst), 2048.0, A.subtract, ext=[ld("rol")])
+        if t >= 2:
+            ts("fOff" + s, ["fJ" + s, "turn"], cut(T.fOff, t, 256), turned(cut(T.fJ, t, 256)), 2048.0, A.add)
+        if t:
+            c, cd = ownc(t)
+            ts("mh" + s, cd, cut(T.mh, t, 256), c, 0.5, A.mult, 1024.75, A.add)
+            calls = []
+            for lo in range(16):
+                o, m = T.pC[:, 256 + 16 * lo:272 + 16 * lo], T.mh[:, t * 256 + lo:(t + 1) * 256:16]
+                calls += [(o, T.Ia[:], ownc(t, lo, 16)[0], True, False), (o, T.Imk[:], m, False, False),
+                          (o, T.Im[:] if t % 2 else T.Ib[:], m, False, True)]
+            mm("co" + s, ["mh" + s, "Ia", "Imk", "Im", "Ib"] + cd + free, calls)
+            k = (-1.0, 1024.0 - 2049.0 * 1025) if t % 2 else (1.0, 2047.0 * 1025)
+            ts("cOff" + s, ["co" + s], cut(T.cOff, t, 256), T.pC[:, 256:512], k[0], A.mult, k[1], A.add)
+
+    prepare(0, [])
+    prepare(1, [])
     ygather(0)
+    gcopy("xo", [], cut(T.XT, 0, 1024), T.XN[:, 1:4 * V:2], 1024, [ld("x0"), ("xa0", arrive)])
 
     for t in range(RO):
         s, pv, n1, n2 = str(t), str(t - 1), str(t + 1), str(t + 2)
@@ -242,125 +250,179 @@ def build(g, core, T, topo, order_text):
         def prev(*names):
             return [n + pv for n in names] if t else []
         xme, xdep, xext = ownx(t)
-        cdep = "cs" + s if t < 2 else "cn%d" % (t - 2)
+        cme, cdep = ownc(t)
         tab_x = [[], ["xn0", "xo"], ["xn1"], ["xn2"]][t]
-        tab_c = ["cs0", "cs1"] if t == 0 else ["cn" + pv]
         xa = [ld("x0")] + [("xa%d" % k, arrive) for k in range(t + 1)]
-        ca = [("ca%d" % k, arrive) for k in range(t + 1)]
-        win = slice(t * 1024, (t + 2) * 1024)
-        pK, pX, pC = T.pK[:, 0:256], T.pX[:, 0:256], T.pC[:, 0:256]
-        mm("k0_" + s, ["rowa", "rmp1"] + prev("scan"), [(pK, T.rows[0:1, 0:128], T.rmp1[0:1, :], True, False)])
-        mm("v0_" + s, ["rowb", "one1", "I2"] + xdep + prev("xn"),
-           [(pX, T.rows[0:1, 128:256], T.one1[0:1, :], True, False), (pX, T.I2[:], xme, False, False)], xext)
-        mm("c0_" + s, [cdep, "If"] + prev("cn"), [(pC, T.If[:], own(T.CT, t), True, False)])
-        u, role, done, klast = 0, [], [], "k0_" + s
-        for ci, (who, n) in enumerate(CHUNKS):
+        pK, pX, pC, pM = T.pK[:, 0:256], T.pX[:, 0:256], T.pC[:, 0:256], T.pM[:, 0:256]
+        mm("k" + s, ["J", "Jm", "one", "p256"] + prev("scan", "rej"),
+           [(pK, T.rows[0:1, 0:128], T.J[0:1, :], True, False), (pK, T.Jm[0:1, 0:128], row["p256"], False, False)])
+        mm("v" + s, ["m8th", "one", "I2"] + xdep + prev("xn"),
+           [(pX, row["m8th"], row["one"], True, False), (pX, T.I2[:], xme, False, False)], xext)
+        u, ks, nS = 0, [], 0
+        for ci, (who, n, ab) in enumerate(CHUNKS[t]):
             a, b = t * 4096 + u * 256, t * 4096 + (u + n) * 256
             cn = "%d_%d" % (t, ci)
-            ys = sorted(set(yname(t, k) for k in range(u, u + n)))
-            gat = (T.XT[:, win] if t else T.XN[:, 0:4 * V]).indirect(T.cOff[:, a // 16:b // 16])
+            ys = ynames(t, u, u + n)
+            gat = (T.XT[:, (t - 1) * 1024:(t + 1) * 1024] if t else T.XN[:, 0:4 * V]).indirect(T.cOff[:, a // 16:b // 16])
             if who == "V":
                 tt("X" + cn, ["cOff" + s] + tab_x + ys, T.DD[:, a:b], gat, T.YG[:, a:b], A.subtract, xa)
                 src, dep = T.DD[:, a:b], "X" + cn
             else:
-                src = (T.pU if ci == 0 else T.pN)[:, 0:b - a]
-                free = prev("su") if ci == 0 else (["aI" + s] if t else [])
+                src = T["pS%d" % (nS % 2)][:, 0:b - a]
+                free = bank.get(nS % 2, [])
+                bank[nS % 2] = ["A" + cn]
+                nS += 1
                 copy("S", "X" + cn, ["cOff" + s] + tab_x, T.DD[:, a:b], gat, xa)
                 mm("my" + cn, ys + ["Im"] + free, [(src, T.Im[:], T.YG[:, a:b], True, False)])
                 mm("mx" + cn, ["my" + cn, "X" + cn, "Ib"], [(src, T.Ib[:], T.DD[:, a:b], False, True)])
                 dep = "mx" + cn
-            op("S", "A" + cn, [dep], lambda a=a, b=b, src=src: act.activation(T.AB[:, a:b], src, F.Abs))
-            done.append((u, u + n, "A" + cn))
-            klast = "k" + cn + "a"
-            mm(klast, ["A" + cn, "Zb", "k0_" + s] + (["k%d_%da" % (t, j) for j in range(ci)] if u + n == 16 else []),
-               [(pK, sel(T.Zb, lo), T.AB[:, t * 4096 + lo * 256:t * 4096 + lo * 256 + 256], False, lo == 15) for lo in range(u, u + n)])
+            end = u + n == 16
+            unit = [(lo, slice(t * 4096 + lo * 256, t * 4096 + lo * 256 + 256)) for lo in range(u, u + n)]
+            if ab == "S":
+                op("S", "A" + cn, [dep], lambda a=a, b=b, src=src: act.activation(T.AB[:, a:b], src, F.Abs))
+                z = "Zk"
+            else:
+                ts("A" + cn, [dep], T.AB[:, a:b], src, 0.0, A.max)
+                mm("kd" + cn, [dep, "Zm", "k" + s], [(pK, sel(T.Zm, lo), T.DD[:, c], False, False) for lo, c in unit])
+                ks.append("kd" + cn)
+                z = "Z2"
+            mm("ka" + cn, ["A" + cn, z, "k" + s] + (ks if end else []), [(pK, sel(T[z], lo), T.AB[:, c], False, lo == 15) for lo, c in unit])
+            ks.append("ka" + cn)
             u += n
-            while 4 * len(role) + 4 <= u:
-                u0 = 4 * len(role)
-                role.append("d%d_%d" % (t, u0))
-                mm(role[-1], [x for (i, j, x) in done if i < u0 + 4 and j > u0] + ["Zb"] + prev("rs"),
-                   [(T.pD[:, u0 * 16:u0 * 16 + 64], sel(T.Zb, k), T.AB[:, t * 4096 + u0 * 256 + k:t * 4096 + (u0 + 4) * 256:16],
-                     k == 0, k == 15) for k in range(16)])
-        alldone = [x for (i, j, x) in done]
-        op("S", "rs" + s, role + ["nthr" + s],
-           lambda t=t: act.activation(r256(T.rs, t), T.pD[:, 0:256], F.Sign, bias=T.nthr[:, t:t + 1]))
-        mm("n" + s, ["rs" + s, "BD"] + alldone + (["aI" + s] if t else []), [(T.pN[:, 0:256], T.BD[:], r256(T.rs, t), True, True)])
-        mm("u" + s, ["rs" + s, "UW"] + alldone + prev("su"), [(T.pU[:, 0:256], T.UW[:], r256(T.rs, t), True, True)])
+        key = ks[-1]
+        rej, rejT = cut(T.rej, t, 256), cut(T.rejT, t, 256)
+        tt("rej" + s, [key, "lim" + s], rej, pK, cut(T.lim, t, 256), A.is_ge)
+        mm("n" + s, ["rej" + s, "Ib"] + (["fr" + s] if t else []),
+           [(T.pN[:, 0:16], T.Ib[:], T.rej[:, t * 256 + k:(t + 1) * 256:16], k == 0, k == 15) for k in range(16)])
+        op("V", "scan" + s, [key, "seg"], lambda t=t, pK=pK: vec.tensor_tensor_scan(cut(T.scan, t, 256), T.seg[:], pK, 0.0, A.add, A.min))
+        least, dep = T.scan[:, t * 256 + 15:(t + 1) * 256:16], "scan" + s
+        if SCRATCH["scan"][2] != I4:
+            copy("V", "kI" + s, [dep], cut(T.kI, t, 16), least)
+            least, dep = cut(T.kI, t, 16), "kI" + s
+        if AND_U16:
+            ts("pL" + s, [dep], cut(T.pL, t, 16), least, NF - 1, A.bitwise_and)
+        else:
+            ts("pI" + s, [dep], cut(T.pI, t, 16), least, NF - 1, A.bitwise_and)
+            copy("V", "pL" + s, ["pI" + s], cut(T.pL, t, 16), cut(T.pI, t, 16))
+        copy("V", "nL" + s, ["n" + s], cut(T.nL, t, 16), T.pN[:, 0:16])
         acc = None if last else T.rsum[:, t:t + 1]
-        op("S", "sg" + s, ["n" + s],
-           lambda t=t, acc=acc: act.activation(r256(T.sg, t), T.pN[:, 0:256], F.Sign, bias=-3.0, accum_out=acc))
-        op("S", "su" + s, ["u" + s], lambda t=t: act.activation(r256(T.su, t), T.pU[:, 0:256], F.Sign, bias=-29.0))
-        op("V", "scan" + s, [klast, "seg"], lambda t=t, pK=pK: vec.tensor_tensor_scan(r256(T.scan, t), T.seg[:], pK, 0.0, A.add, A.min))
-        ts("kI" + s, ["scan" + s, "lo256"], r16(T.kI, t), T.scan[:, t * 256 + 15:(t + 1) * 256:16], 4096.0, A.mult, T.lo256[:, 0:1], A.add)
-        ts("pI" + s, ["kI" + s], r16(T.pI, t), r16(T.kI, t), 4095, A.bitwise_and)
-        ts("bI" + s, ["kI" + s], r16(T.bI, t), r16(T.kI, t), 15, A.bitwise_and)
-        tc("pL" + s, ["pI" + s], r16(T.pL, t), r16(T.pI, t))
-        tc("bL" + s, ["bI" + s], r16(T.bL, t), r16(T.bI, t))
-        tt("h" + s, ["pL" + s, "x3_" + s], r256(T.hh, t), T.YG[:, t * 4096:(t + 1) * 4096].indirect(r16(T.pL, t)), r256(T.x3, t), A.subtract)
-        tt("q" + s, ["h" + s, "sg" + s, "turn"], r256(T.qq, t), turned(T.sg, t), r256(T.hh, t), A.mult)
-        mm("v2_" + s, ["v0_" + s, "h" + s, "I75"], [(pX, T.I75[:], r256(T.hh, t), False, False)])
-        mm("v3_" + s, ["v2_" + s, "q" + s, "I25", "rowc"],
-           [(pX, T.I25[:], r256(T.qq, t), False, False), (pX, T.rows[0:1, 256:384], T.one1[0:1, :], False, True)])
-        xdst = T.xout[:, 1:V:2] if last else own(T.XT, t + 2)
-        op("S", "xn" + s, ["v3_" + s] + (["xe"] if last else []), lambda xdst=xdst, pX=pX: act.activation(xdst, pX, F.Abs, bias=-MAGIC))
+        op("S", "sg" + s, ["nL" + s], lambda t=t, acc=acc: act.activation(cut(T.sg, t, 16), T.pN[:, 0:16], F.Sign, bias=-9.5, accum_out=acc))
+        best = cut(T.pL, t, 16)
+        tt("h" + s, ["pL" + s, "x3_" + s], cut(T.hh, t, 256), cut(T.YG, t, 4096).indirect(best), cut(T.x3, t, 256), A.subtract)
+        tt("q" + s, ["h" + s, "nL" + s, "AT"], cut(T.qq, t, 256), T.AT[:, 0:32].indirect(cut(T.nL, t, 16)), cut(T.hh, t, 256), A.mult)
+        mm("vq" + s, ["v" + s, "q" + s, "Ib", "magic"],
+           [(pX, T.Ib[:], cut(T.qq, t, 256), False, False), (pX, row["magic"], row["one"], False, True)])
+        xdst = T.xout[:, 1:V:2] if last else own(T.XT, t + 1)
+        op("S", "xn" + s, ["vq" + s] + (["xe2"] if last else []), lambda xdst=xdst, pX=pX: act.activation(xdst, pX, F.Abs, bias=-MAGIC))
         if last:
-            copy("S", "xe", ["xn2"], T.xout[:, 0:V:2], own(T.XT, 4))
-            copy("S", "ce", ["cn2"], T.cout[:, 0:V:2], own(T.CT, 4))
-            op("Y", "st_x", ["xn" + s, "xe"], lambda: g.sync.dma_start(T.yx[:], T.xout[:]).then_inc(T.sem.stored, 16))
+            op("Y", "st_x", ["xn" + s, "xe2"], lambda: g.sync.dma_start(T.yx[:], T.xout[:]).then_inc(T.sem.stored, 16))
         else:
-            send("sx" + n1, ["xn" + s], [own(T.XT, t + 2)], T.sem["xa" + n1])
+            send("sx" + n1, ["xn" + s], own(T.XT, t + 1), others, eng, T.sem["xa" + n1])
             ygather(t + 1)
-        onehot = T.OH[:, 0:16].indirect(r16(T.bL, t))
-        tt("selc" + s, ["bL" + s, "OH", "encB" + s], r256(T.selc, t), onehot, r256(T.encB, t), A.mult)
-        mm("b" + s, ["selc" + s, "Zh"] + prev("cL"),
-           [(T.pB[:, 0:16], sel(T.Zh, lo), T.selc[:, t * 256 + lo:(t + 1) * 256:16], lo == 0, lo == 15) for lo in range(16)])
-        tt("slf" + s, ["bL" + s, "OH", "fJ" + s], r256(T.slf, t), onehot, r256(T.fJ, t), A.mult)
-        mm("zs" + s, ["sg" + s, "Zw", "e1_01", "eL01"] + prev("eA"),
-           [(T.pZ[:, 0:16], sel(T.Zw, lo), T.sg[:, t * 256 + lo * 16:t * 256 + lo * 16 + 16], lo == 0, False) for lo in range(16)])
-        tc("cL" + s, ["b" + s], r16(T.cL, t), T.pB[:, 0:16])
-        mine, mext = (T.cass[:, t:V:2], [ld("cas")]) if t < 2 else (r256(T.ck, t - 2), [("ck" + s, 16)])
-        tt("t1" + s, ["cL" + s] + tab_c, r256(T.t1, t), T.CT[:, win].indirect(r16(T.cL, t)), mine, A.subtract, ca + mext)
-        tt("t2" + s, ["t1" + s, "su" + s, "turn"], r256(T.t2, t), turned(T.su, t), r256(T.t1, t), A.mult)
-        mm("zf" + s, ["zs" + s, "slf" + s, "Zh"],
-           [(T.pZ[:, 0:16], sel(T.Zh, lo), T.slf[:, t * 256 + lo:(t + 1) * 256:16], False, lo == 15) for lo in range(16)])
-        mm("c1_" + s, ["c0_" + s, "t1" + s, "I50"], [(pC, T.I50[:], r256(T.t1, t), False, False)])
-        mm("c2_" + s, ["c1_" + s, "t2" + s], [(pC, T.I50[:], r256(T.t2, t), False, True)])
-        copy("S", "cn" + s, ["c2_" + s] + (["ce"] if last else []), T.cout[:, 1:V:2] if last else own(T.CT, t + 2), pC)
+        onehot = T.OH[:, 0:4096].indirect(best)
+        tt("selc" + s, ["pL" + s, "OH6"] + cdep, T.sel[:, t * 512:t * 512 + 256], onehot, cme, A.mult, [("oh", 48)])
+        tt("self" + s, ["pL" + s, "OH6", "fJ" + s], T.sel[:, t * 512 + 256:(t + 1) * 512], onehot, cut(T.fJ, t, 256), A.mult, [("oh", 48)])
+        bfree = ["eL", "e1_0", "e1_1"] if t == 0 else (prev("zA") if t < 3 else ["eo2"])
+        sums = [(T.pB[:, 0:32], sel(T.Z1, lo), T.sel[:, t * 512 + lo:(t + 1) * 512:16], lo == 0, lo == 15) for lo in range(16)]
+        jump = [(T.pB[:, 0:16], T.Imk[:], cut(T.sg, t, 16), False, False), (T.pB[:, 16:32], T.Ik[:], cut(T.sg, t, 16), False, False)]
+        mm("b" + s, ["selc" + s, "self" + s, "Z1", "sg" + s, "Ik", "Imk"] + bfree, sums[:15] + jump + sums[15:])
+        tt("zA" + s, ["b" + s, "Wn%d" % (t & 1), "e1_" + s], cut(T.zA, t, 32), T.pB[:, 0:32], cut(T.W, t & 1, 32), A.max)
+        if AND_U16:
+            ts("zL" + s, ["zA" + s], cut(T.zL, t, 32), cut(T.zA, t, 32), NS - 1, A.bitwise_and)
+            scene, sdep = T.zL[:, t * 32 + 16:(t + 1) * 32], "zL" + s
+        else:
+            ts("zI" + s, ["zA" + s], cut(T.zI, t, 32), cut(T.zA, t, 32), NS - 1, A.bitwise_and)
+            copy("V", "zL" + s, ["zI" + s], cut(T.zL, t, 32), cut(T.zI, t, 32))
+            scene, sdep = T.zI[:, t * 32 + 16:(t + 1) * 32], "zI" + s
+        op("V", "rT" + s, ["rej" + s], lambda rej=rej, rejT=rejT: vec.transpose(rejT, rej))
+        calls = []
+        for hi in range(16):
+            for w in range(2):
+                blk, half = hi // 2, hi % 2
+                off = 16 + 16 * (half - w)
+                calls.append((T.pM[:, 16 * hi:16 * hi + 16], T["G%d" % half][:, off:off + 128],
+                              T.rejT[:, t * 256 + 32 * blk + 16 * w:t * 256 + 32 * blk + 16 * w + 16], w == 0, w == 1))
+        mm("m" + s, ["rT" + s, "G0", "G1"] + (prev("t2") if t else ["TH", "lim0"]), calls)
+        conv = ["cv" + s + k for k in "abcd"] if t else []
+        came = [] if t else [ld("cas")] + [("ca0_%d" % r, len(eng)) for r in range(len(T.cores)) if r != q]
+        tt("t1" + s, ["zL" + s] + conv + cdep, cut(T.t1, t, 256), T.CT[:, 0:4 * V].indirect(T.zL[:, t * 32:t * 32 + 16]), cme, A.subtract, came)
+        tt("t2" + s, ["t1" + s, "m" + s], cut(T.t2, t, 256), pM, cut(T.t1, t, 256), A.mult)
+        mm("c" + s, ["t2" + s, "Ib"] + cdep + [["cOff1"], ["cOff2"], ["cOff3"], ["cn2"]][t],
+           [(pC, T.Ib[:], cme, True, False), (pC, T.Ib[:], cut(T.t2, t, 256), False, True)])
         if last:
-            op("Y", "st_c", ["cn" + s, "ce"], lambda: g.sync.dma_start(T.yc[:], T.cout[:]).then_inc(T.sem.stored, 16))
+            copy("S", "cn" + s, ["c" + s, "ce2"], T.cout[:, 1:V:2], pC)
+            op("Y", "st_c", ["cn" + s, "ce2"], lambda: g.sync.dma_start(T.yc[:], T.cout[:]).then_inc(T.sem.stored, 16))
         else:
-            send("sc" + n1, ["cn" + s], [own(T.CT, t + 2)], T.sem["ca" + n1])
-            mm("a" + s, ["sg" + s, "w32"], [(T.pN[:, 256:257], T.w32[:], T.rsum[:, t:t + 1], True, True)])
-            ts("aI" + n1, ["a" + s], T.aI[:, t:t + 1], T.pN[:, 256:257], 1024.0, A.add)
-            ts("aM" + n1, ["aI" + n1], T.aM[:, t:t + 1], T.aI[:, t:t + 1], 255, A.bitwise_and)
-            ts("nthr" + n1, ["aM" + n1, "nthr0"], T.nthr[:, t + 1:t + 2], T.aM[:, t:t + 1], -1.0, A.mult, T.nthr[:, 0:1], A.add)
-        tt("eA" + s, ["zf" + s, "e1_01" if t < 2 else "e1_" + s], r16(T.eA, t), T.pZ[:, 0:16], r16(T.e1, t), A.max)
-        ts("eI" + s, ["eA" + s], r16(T.eI, t), r16(T.eA, t), NS - 1, A.bitwise_and)
-        tc("eL" + n2, ["eI" + s], r16(T.eL, t + 2), r16(T.eI, t))
+            copy(CNE, "cn" + s, ["c" + s], own(T.CH, t), pC)
+            send_casts(t + 1, ["cn" + s], own(T.CH, t))
+            widen(t + 1, ["cn" + s, "t1" + s])
+            pA = T.pN[:, 128:129]
+            mm("a" + s, ["sg" + s, "w", "one", "half"],
+               [(pA, T.w[:], T.rsum[:, t:t + 1], True, False), (pA, row["half"], T.rows[0:1, 0:1], False, True)])
+            ts("fl" + n1, ["a" + s], T.fl[:, t:t + 1], pA, MAGIC, A.add, MAGIC, A.subtract)
+            ts("fr" + n1, ["fl" + n1], T.fr[:, t:t + 1], pA, T.fl[:, t:t + 1], A.subtract, 256.0 * 4096, A.mult)
+            lin("lim" + n1, ["fr" + n1, "TH"], cut(T.lim, t + 1, 256), T.TH[:], 1.0, T.fr[:, t:t + 1])
         if t < 2:
-            op("Y", "ck" + n2, ["cn" + s],
-               lambda t=t, n2=n2: g.sync.dma_start(r256(T.ck, t), own(T.CT, t + 2)).then_inc(T.sem["ck" + n2], 16))
-            fj(t + 2, "eL" + n2)
-            ts("e1_" + n2, ["eI" + s], r16(T.e1, t + 2), r16(T.eI, t), 1.0, A.add)
-            ts("fOff" + n2, ["fJ" + n2, "turn"], r256(T.fOff, t + 2), turned(T.fJ, t + 2), 2048.0, A.add)
-            enc(t + 2, "cn" + s)
-            scaled("x3_" + n2, ["xn" + s], r256(T.x3, t + 2), own(T.XT, t + 2), 3.0)
+            ts("e1_" + n2, [sdep], T.W[:, t * 32 + 16:(t + 1) * 32], scene, 1.0, A.add)
+            prepare(t + 2, ["cn" + s])
         else:
-            copy("S", "eo" + s, ["eL" + n2, "ramp"] + (["eo2"] if last else []), T.eout[:, (t & 1):V:2], T.ramp[:, 0:NS].indirect(r16(T.eL, t + 2)))
-    op("Y", "st_e", ["eo2", "eo3"], lambda: g.sync.dma_start(T.ye[:], T.eout[0:128:16, :]).then_inc(T.sem.stored, 16))
-    if order_text is not None:
-        had = sorted(n for e in order_text for n in order[e])
-        for e in order_text:
-            order[e] = order_text[e].split()
-        assert had == sorted(n for e in order_text for n in order[e])
-    return ops, order, sent[0]
+            p = t & 1
+            ts("eH" + s, [sdep], cut(T.eH, p, 16), scene, 1.0, A.mult)
+            mm("ef" + s, ["eH" + s, "zA" + s, "Ib"],
+               [(T.pB[0:8, 256 + lo:512:16], T.Ib[:, lo:128:16], cut(T.eH, p, 16), True, True) for lo in range(16)])
+            copy("S", "eo" + s, ["ef" + s] + (["eo2"] if last else []), T.eout[0:8, p:V:2], T.pB[0:8, 256:512])
+        if t == 2:
+            gcopy("xe2", ["xn2"], T.xout[:, 0:V:2], own(T.XT, 3), 256)
+            gcopy("ce2", ["cn2"], T.cout[:, 0:V:2], own(T.CH, 2), 256)
+    op("Y", "st_e", ["eo2", "eo3"], lambda: g.sync.dma_start(T.ye[:], T.eout[0:8, :]).then_inc(T.sem.stored, 16))
+    return ops, sent[0]
+
+
+def out_engines(topo, core, dsts):
+    return [e for e in topo.engines(core, dsts[0]) if all(e in topo.engines(core, c) for c in dsts)]
+
+
+def helper(topo, core):
+    return [c for c in topo.cores_of(core) if topo.die(c) != topo.die(core)][0]
+
+
+def write(g, topo, part, dsts, engs, sem, left):
+    ids = [DstId(rid=topo.addr(c)[0], pnc=topo.addr(c)[1]) for c in dsts]
+    return g.remote_dma_fused([RemoteDMATransfer(dst_ids=ids, dma_engine_mask=sum(1 << e for e in engs), remote_sem=sem,
+                                                 srcs=[part], dsts=[part] * len(ids))], local_sem=left)
+
+
+def hand_on(g, core, rank_core, T, topo):
+    q = T.rank_of(rank_core)
+    others = [T.cores[(q + k) % len(T.cores)] for k in range(1, len(T.cores))]
+    eng = out_engines(topo, core, others)
+    came = len([e for e in topo.engines(rank_core, core) if e not in out_engines(topo, rank_core, others)])
+    for t in HELP:
+        g.wait_ge(T.sem["ha%d" % t], came)
+        a = (t - 1) * 1024 + q * 256
+        write(g, topo, T.CH[:, a:a + 256] if t else T.CT[:, q * V:(q + 1) * V], others, eng, T.sem["ca%d_%d" % (t, q)], T.sem.sent)
+    g.wait_ge(T.sem.sent, len(HELP) * len(eng))
+
+
+def arrange(ops):
+    order = {e: [n for n in ops if ops[n][0] == e] for e in "VSPGY"}
+    for e, (first, each) in (ORDER or {}).items():
+        names = first.split()
+        for r in range(RO + 2):
+            for tok in each.split():
+                n, d = (tok + "@0").split("@")[:2]
+                n = n.replace("#", str(r + int(d)))
+                if n in order[e] and n not in names:
+                    names.append(n)
+        assert sorted(names) == sorted(order[e]), (e, sorted(set(names) ^ set(order[e])))
+        order[e] = names
+    return order
 
 
 def emit(g, T, ops, order, sent):
     queue = {"V": g.vector, "S": g.scalar, "P": g.tensor, "G": g, "Y": g.sync}
     counter = {"V": "cV", "S": "cS", "P": "cP", "G": "cG"}
-    where = {n: e for e in order for n in order[e]}
-    needed = set(d for n, o in ops.items() for d in o[1] if not (where[n] == "P" and where[d] == "P"))
+    needed = set(d for o in ops.values() for d in o[2] if not (o[0] == "P" and ops[d][0] == "P"))
     count = {}
     for e, names in order.items():
         k = 0
@@ -371,13 +433,13 @@ def emit(g, T, ops, order, sent):
     for e, names in order.items():
         seen = {}
         for name in names:
-            fns, deps, ext = ops[name]
+            _, fn, deps, ext = ops[name]
             want = {}
             for d in deps:
-                if e == "P" and where[d] == "P":
+                if e == "P" and ops[d][0] == "P":
                     assert names.index(d) < names.index(name)
                     continue
-                k = counter[where[d]]
+                k = counter[ops[d][0]]
                 want[k] = max(want.get(k, 0), count[d])
             for k, v in ext:
                 want[k] = max(want.get(k, 0), v)
@@ -385,7 +447,7 @@ def emit(g, T, ops, order, sent):
                 if seen.get(k, 0) < v:
                     queue[e].wait_ge(T.sem[k], v)
                     seen[k] = v
-            ins = fns[e]()
+            ins = fn()
             if name in count:
                 ins.then_inc(T.sem[counter[e]], 1)
     g.wait_ge(T.sem.sent, sent)
@@ -393,6 +455,10 @@ def emit(g, T, ops, order, sent):
 
 
 def rank_program(g, core, T, topo):
-    if T.rank_of(core) is None:
-        return
-    emit(g, T, *build(g, core, T, topo, ORDER))
+    if T.rank_of(core) is not None:
+        ops, sent = build(g, core, T, topo)
+        emit(g, T, ops, arrange(ops), sent)
+    elif HELP:
+        for c in T.cores:
+            if helper(topo, c) == core:
+                hand_on(g, core, c, T, topo)

@@ -11,10 +11,10 @@ def sb(n, dt):
 
 
 SCRATCH = {
-    "XN": sb(4 * V, B), "XT": sb(4 * 1024, B), "CN": sb(V, H), "CH": sb(3 * 1024, H), "CT": sb(4 * V, I4),
+    "XN": sb(4 * V, B), "XT": sb(4 * 1024, B), "CN": sb(V, H), "CH": sb(3 * 1024, H), "CT": sb(4 * V + 256, I4), "Wc": sb(16, F4), "zc": sb(16, F4),
     "frms": sb(NF, B), "rols": sb(NS, I4), "scs": sb(32, I4), "sc8": sb(V, I4), "sc8h": sb(V, H), "ths": sb(4, I4), "thf": sb(1, F4),
     "YG": sb(RO * 4096, B), "DD": sb(RO * 4096, B), "AB": sb(RO * 4096, B),
-    "fOff": sb(RO * 256, U2), "cOff": sb(RO * 256, U2), "fJ": sb(RO * 256, F4), "mh": sb(RO * 256, H), "x3": sb(RO * 256, H),
+    "fOff": sb(RO * 256, U2), "cOff": sb(RO * 256, U2), "fJ": sb(RO * 256, H), "mh": sb(RO * 256, H), "x3": sb(RO * 256, H),
     "turn2": sb(16, U2), "scan": sb(RO * 256, I4), "rej": sb(RO * 256, B), "rejT": sb(RO * 256, B),
     "hh": sb(RO * 256, H), "qq": sb(RO * 256, H), "t1": sb(RO * 256, H), "t2": sb(RO * 256, H), "sel": sb(RO * 512, H),
     "kI": sb(RO * 16, I4), "pI": sb(RO * 16, I4), "pL": sb(RO * 16, U2), "nL": sb(RO * 16, U2), "sg": sb(RO * 16, B),
@@ -23,8 +23,8 @@ SCRATCH = {
     "xout": sb(V, B), "cout": sb(V, F4), "eout": sb(V, F4),
     "J": sb(256, B), "J16": sb(128, B), "Jm": sb(256, B), "pc": sb(4, I4), "pa": sb(4, I4), "pf": sb(12, F4), "Ga": sb(160, B),
     "iq": sb(16, I4), "io2": sb(16, I4), "turn": sb(16, U2),
-    "Z1": sb(144, B), "Z2": sb(144, B), "Zm": sb(144, B), "Z8": sb(144, B), "G0": sb(160, B), "G1": sb(160, B),
-    "BD": sb(128, F4), "Ib": sb(128, B), "Im": sb(128, B), "I2": sb(128, B), "Ik": sb(128, B), "Imk": sb(128, B),
+    "Z1": sb(144, B), "Zm": sb(144, B), "Z8": sb(144, B), "G0": sb(160, B), "G1": sb(160, B),
+    "BD": sb(128, F4), "Ib": sb(128, B), "Im": sb(128, B), "Ik": sb(128, B), "Imk": sb(128, B),
     "Ia": sb(128, B), "w": sb(128, F4), "rows": sb(6 * 256, B), "seg": sb(256, B), "OH": sb(4096, B),
     "thd": sb(256, F4), "TH": sb(256, F4), "AT": sb(32, B),
 }
@@ -32,26 +32,30 @@ for n in ("pK", "pN", "pX", "pC", "pB", "pM", "pS0", "pS1"):
     SCRATCH[n] = ("psum", [128, 512], F4)
 LOADS = ["x0", "sc", "cas", "rol", "frm", "th", "sc8"]
 SEMAPHORES = (["cV", "cS", "cP", "cG", "sent", "left0", "oh", "stored"] + ["ld_" + n for n in LOADS]
-              + [k + str(t) for k in ("xa", "ha") for t in range(RO)] + ["ca%d_%d" % (t, r) for t in range(RO) for r in range(4)])
+              + ["handed"] + ["xa%d" % t for t in range(RO)] + ["ca%d_%d" % (t, r) for t in range(RO) for r in range(4)])
 
-HELP = [0, 1, 2, 3]
-CHUNKS = [[("S", 2, "S"), ("S", 2, "S"), ("S", 2, "S"), ("V", 4, "V"), ("V", 3, "V"), ("V", 2, "V"), ("V", 1, "V")]] * 4
-YCH = [[4, 4, 4, 4], [2] * 8, [2] * 8, [2] * 8]
-YV = [[0, 1], [], [], []]
-CNE = "S"
-AND_U16 = False
+DIRECT = 1
+CHUNKS = [[("S", 2, "S"), ("S", 2, "S"), ("S", 2, "S"), ("S", 1, "S"), ("V", 4, "V"), ("V", 3, "V"), ("V", 1, "V"), ("V", 1, "V")]] * 4
+YCH = [[4, 4, 4, 4]] + [[3, 3, 3, 3, 2, 2]] * 3
+YV = [[0, 1], [5], [5], [5]]
+ON_S = ["x3_2", "x3_3"]
+PARTS = [[128, 128]] * 3 + [[256]]
 ORDER = {
-    "V": ("one seg0 pa0 pa1 pa2 pf3 pf p256 m8th magic half seg w Ib Z1 Z8 G1a AT io2 turn turn2 OH4 BD eC0 eC1 s8h0 s8h1 thf x3_0 x3_1 "
-          "cs cOff0 mh1 eL fOff0 fOff1 fJ0 Y0_0 Y0_1 fJ1 cOff1",
-          "X#_3 X#_4 A#_3 X#_5 A#_4 X#_6 A#_5 A#_6 scan# rej# kI# pI# pL# h# nL# self# q# selc# rT# cOff#@1 fl#@1 zA# zI# fr#@1 zL# "
-          "t1# eH# e1_#@2 t2# x3_#@2 fJ#@2 fOff#@2 mh#@2"),
-    "S": ("pf5 pf6 pf7 pf9 Im Imk Ia I2 Ik Zk Z2 Zm Wn0 Wn1 G1 G0 OH5 OH6 thd e1_0 e1_1 TH lim0 Y0_2 Y0_3",
-          "X#_0 X#_1 A#_0 X#_2 A#_1 A#_2 lim# Y#_7@1 Y#_5@1 Y#_2@1 Y#_0@1 sg# Y#_1@1 xn# Y#_4@1 Y#_3@1 Y#_6@1 eo# cn#"),
-    "P": ("e0 co1 thm k0 my0_0 my0_1",
-          "co#@1 mx#_0 v# mx#_1 kd#_3 ka#_0 my#_2 mx#_2 ka#_3 kd#_4 kd#_5 ka#_1 ka#_4 ka#_2 kd#_6 ka#_5 ka#_6 n# k#@1 a# vq# b# "
-          "my#_0@1 m# my#_1@1 ef# c#"),
-    "G": ("pc J iq Jm J16 sx0 sc0 xo sx1",
-          "sc#@1 cv#a@1 xe# ce# cv#b@1 cv#c@1 cv#d@1 sx#@2"),
+    "V": ("one seg0 magic half pa2 pf3 pa0 pa1 m8th p256 pf G1a Ib Z8 AT w seg io2 Z1 OH4 s8h1 thf s8h0 turn2 eC0 x3_1 cOff0 BD turn eL "
+          "cs eC1 fOff0 fOff1 mh1 fJ0 x3_0 Y0_1 Y0_0",
+          "X#_4 X#_5 A#_4 A#_5 X#_6 fOff#@1 X#_7 A#_6 A#_7 e1_#@1 scan# rej# pI# mh#@1 pL# rT# h#a nL# h#b q#a q#b selc# self# Y#_5@1 "
+          "zA# fl#@1 zI# cOff#@1 zL# fr#@1 t1# fJ#@1 eH# t2# fJ#@2 cn#",
+          "X#_4 X#_5 A#_4 X#_6 A#_5 X#_7 A#_6 A#_7 scan# rej# pI# pL# rT# selc# nL# self# h#a zA# q#a zE# zL# zI# t1# eH# t2# cn#"),
+    "S": ("pf5 pf7 pf6 Ik pf9 Ia Wn0 Imk Wn1 Zm Zk G0 thd e1_0 Wc e1_1 Im G1 lim0 TH Y0_2 Y0_3",
+          "x3_#@1 lim# X#_0 X#_1 A#_0 X#_2 A#_1 X#_3 A#_2 A#_3 Y#_4@1 Y#_0@1 Y#_1@1 sg# xn#a xn#b Y#_2@1 Y#_3@1 eo#",
+          "X#_0 X#_1 A#_0 X#_2 A#_1 X#_3 A#_2 A#_3 lim# sg# xn#a eo#"),
+    "P": ("k0 e0 thm co1 my0_1 my0_0",
+          "ft#@1 v#a mx#_0 mx#_1 kd#_4 my#_2 ka#_0 kd#_5 mx#_2 ka#_4 my#_3 ka#_1 mx#_3 kd#_6 ka#_5 ka#_2 kd#_7 ka#_6 ka#_3 ka#_7 "
+          "n# co#@1 vq#a v#b vq#b b# a# my#_1@1 m# my#_0@1 k#@1 ef#",
+          "v#a mx#_0 kd#_4 mx#_1 ka#_0 my#_2 kd#_5 mx#_2 ka#_4 my#_3 ka#_1 mx#_3 kd#_6 ka#_5 kd#_7 ka#_2 ka#_6 ka#_3 ka#_7 "
+          "n# bc# bcj# be# bej# m# vq#a ef#"),
+    "G": ("pc J iq Jm J16 sx0 sc0 OH5 OH6 sd0 xo sx1a sx1b",
+          "sc#@1 cv#a@1 cc#@1 xe# ce# cv#b@1 cv#c@1 cv#d@1 sx#a@2 sx#b@2", ""),
 }
 
 
@@ -83,8 +87,8 @@ def build(g, core, T, topo):
         else:
             op("V", name, deps, lambda: vec.tensor_scalar(out, a, s1, s2, o1, o2), ext)
 
-    def lin(name, deps, out, a, scale, bias=0.0):
-        op("S", name, deps, lambda: act.activation(out, a, F.Identity, bias=bias, scale=scale))
+    def lin(name, deps, out, a, scale, bias=0.0, ext=()):
+        op("S", name, deps, lambda: act.activation(out, a, F.Identity, bias=bias, scale=scale), ext)
 
     def fill(name, deps, out, k):
         op("V", name, deps, lambda: vec.memset(out, k))
@@ -124,8 +128,11 @@ def build(g, core, T, topo):
                         ("th", T.ths[:, 0:1], T.th[:]), ("cas", minec, T.cas[:]), ("rol", T.rols[:], T.rol[:]), ("frm", T.frms[:], T.frm[:])):
         op("Y", "ld_" + n, [], lambda n=n, dst=dst, src=src: g.sync.dma_start(dst, src).then_inc(T.sem["ld_" + n], 16))
 
+    def xnames(t):
+        return ["xn%d" % t + "ab"[j] for j in range(len(PARTS[t]))] if t >= 0 else []
+
     def ownx(t):
-        return (T.XN[:, q * V + t:(q + 1) * V:2], [], [ld("x0")]) if t < 2 else (own(T.XT, t - 1), ["xn%d" % (t - 2)], [])
+        return (T.XN[:, q * V + t:(q + 1) * V:2], [], [ld("x0")]) if t < 2 else (own(T.XT, t - 1), xnames(t - 2), [])
 
     def ownc(t, a=0, step=1):
         if t < 2:
@@ -138,21 +145,22 @@ def build(g, core, T, topo):
     sent = [0]
 
     def send(name, dep, part, dsts, engs, sem, ext=()):
-        left = T.sem.left0 if name == "sc0" else T.sem.sent
-        sent[0] += 0 if name == "sc0" else len(engs)
-        op("G", name, dep, lambda: write(g, topo, part, dsts, engs, sem, left), ext)
+        first = name in ("sc0", "sd0")
+        sent[0] += 0 if first else len(engs)
+        op("G", name, dep, lambda: write(g, topo, part, dsts, engs, sem, T.sem.left0 if first else T.sem.sent), ext)
 
     def send_casts(t, dep, part, ext=()):
-        if t in HELP:
-            h = helper(topo, core)
-            send("sc%d" % t, dep, part, [h], [e for e in topo.engines(core, h) if e not in eng], T.sem["ha%d" % t], ext)
-        else:
+        if t:
             send("sc%d" % t, dep, part, others, eng, T.sem["ca%d_%d" % (t, q)], ext)
+        else:
+            h = helper(topo, core)
+            send("sc0", dep, part, [h], [e for e in topo.engines(core, h) if e not in eng], T.sem.handed, ext)
+            send("sd0", dep, part, others[:DIRECT], eng, T.sem["ca0_%d" % q], list(ext) + [("sent", len(eng))])
 
     def widen(t, dep):
         for k in range(len(T.cores)):
             r = (q - k) % len(T.cores)
-            came = [("ca%d_%d" % (t, r), len(eng))] if k else [("left0", len(eng))]
+            came = [("ca%d_%d" % (t, r), len(eng))] if k else [("left0", 2 * len(eng))]
             gcopy("cv%d" % t + "abcd"[k], dep, T.CT[:, r * V + (t - 1) % 2:(r + 1) * V:2],
                   T.CH[:, (t - 1) * 1024 + r * 256:(t - 1) * 1024 + (r + 1) * 256], 256, came)
 
@@ -175,7 +183,7 @@ def build(g, core, T, topo):
     ts("Z1", ["J", "pf"], T.Z1[:], T.J[:, 0:144], gp, A.subtract, 15.0, A.is_equal)
     ts("Ib", ["J", "pf3"], T.Ib[:], T.J[:, 0:128], pp, A.is_equal)
     ts("Z8", ["J", "pf5"], T.Z8[0:8, :], T.J[0:8, 0:144], T.pf[0:8, 5:6], A.subtract, 15.0, A.is_equal)
-    for n, src, k in (("Zk", "Z1", 4096.0), ("Z2", "Z1", 8192.0), ("Zm", "Z1", -4096.0), ("Im", "Ib", -1.0), ("I2", "Ib", 2.0), ("Ik", "Ib", 4096.0),
+    for n, src, k in (("Zk", "Z1", 4096.0), ("Zm", "Z1", -4096.0), ("Im", "Ib", -1.0), ("Ik", "Ib", 4096.0),
                       ("Imk", "Ib", -2048.0), ("Ia", "Ib", 1024.0)):
         lin(n, [src], T[n][:], T[src][:], k)
     ts("G1a", ["J", "pf3"], T.Ga[:], T.J[:, 0:160], pp, A.subtract, 16.0, A.is_equal)
@@ -194,7 +202,7 @@ def build(g, core, T, topo):
         fill(n, [], row[n], k)
     ts("OH4", ["Jm", "pf"], T.OH[:, 0:256], T.Jm[:], lo1, A.is_equal)
     for j in (4, 5):
-        copy("S", "OH%d" % (j + 1), ["OH%d" % j], T.OH[:, 16 << j:32 << j], T.OH[:, 0:16 << j])
+        gcopy("OH%d" % (j + 1), ["OH%d" % j], T.OH[:, 16 << j:32 << j], T.OH[:, 0:16 << j], 16 << j)
     for j in (1, 2, 3):
         op("Y", "oh%d" % j, ["OH6"], lambda j=j: g.sync.dma_start(cut(T.OH, j, 1024), cut(T.OH, 0, 1024)).then_inc(T.sem.oh, 16), [ld("frm")])
     lin("Wn0", ["J", "pf7"], T.W[:, 0:16], T.J[:, 0:16], 32.0, name0)
@@ -206,7 +214,7 @@ def build(g, core, T, topo):
     lin("lim0", ["thm"], cut(T.lim, 0, 256), T.pM[:, 0:256], 4096.0, 4096.0)
 
     copy("V", "cs", [], T.CN[:], minec, [ld("cas")])
-    send_casts(0, [], minec, [ld("cas"), ld("frm")])
+    send_casts(0, [], minec, [ld("cas")])
     ts("turn2", ["io2"], T.turn2[:], T.io2[:], 2.0, A.mult)
     copy("V", "cOff0", ["turn2"], cut(T.cOff, 0, 256), minec.indirect(T.turn2[:, 0:16]), [ld("cas")])
     for p in range(2):
@@ -221,14 +229,22 @@ def build(g, core, T, topo):
     def prepare(t, free):
         s = str(t)
         x, xd, xe = ownx(t)
-        ts("x3_" + s, xd, cut(T.x3, t, 256), x, 3.0, A.mult, ext=xe)
+        if "x3_" + s in ON_S:
+            lin("x3_" + s, xd, cut(T.x3, t, 256), x, 3.0, ext=xe)
+        else:
+            ts("x3_" + s, xd, cut(T.x3, t, 256), x, 3.0, A.mult, ext=xe)
         lst, dep = (cut(T.eL, t, 16), "eL") if t < 2 else (T.zL[:, (t - 2) * 32 + 16:(t - 2) * 32 + 32], "zL%d" % (t - 2))
         ts("fJ" + s, [dep], cut(T.fJ, t, 256), T.rols[:, 0:NS].indirect(lst), 2048.0, A.subtract, ext=[ld("rol")])
         if t >= 2:
-            ts("fOff" + s, ["fJ" + s, "turn"], cut(T.fOff, t, 256), turned(cut(T.fJ, t, 256)), 2048.0, A.add)
+            mm("ft" + s, ["fJ" + s, "Ib", "t2%d" % (t - 2)],
+               [(T.pM[:, 256 + 16 * lo:272 + 16 * lo], T.Ib[:], T.fJ[:, t * 256 + lo:(t + 1) * 256:16], True, True) for lo in range(16)])
+            ts("fOff" + s, ["ft" + s], cut(T.fOff, t, 256), T.pM[:, 256:512], 2048.0, A.add)
         if t:
             c, cd = ownc(t)
-            ts("mh" + s, cd, cut(T.mh, t, 256), c, 0.5, A.mult, 1024.75, A.add)
+            if "mh" + s in ON_S:
+                lin("mh" + s, cd, cut(T.mh, t, 256), c, 0.5, 1024.75)
+            else:
+                ts("mh" + s, cd, cut(T.mh, t, 256), c, 0.5, A.mult, 1024.75, A.add)
             calls = []
             for lo in range(16):
                 o, m = T.pC[:, 256 + 16 * lo:272 + 16 * lo], T.mh[:, t * 256 + lo:(t + 1) * 256:16]
@@ -251,13 +267,11 @@ def build(g, core, T, topo):
             return [n + pv for n in names] if t else []
         xme, xdep, xext = ownx(t)
         cme, cdep = ownc(t)
-        tab_x = [[], ["xn0", "xo"], ["xn1"], ["xn2"]][t]
-        xa = [ld("x0")] + [("xa%d" % k, arrive) for k in range(t + 1)]
+        tab_x = xnames(t - 1) + (["xo"] if t == 1 else [])
+        xa = [ld("x0")] + [("xa%d" % k, arrive * (len(PARTS[k - 1]) if k else 1)) for k in range(t + 1)]
         pK, pX, pC, pM = T.pK[:, 0:256], T.pX[:, 0:256], T.pC[:, 0:256], T.pM[:, 0:256]
         mm("k" + s, ["J", "Jm", "one", "p256"] + prev("scan", "rej"),
            [(pK, T.rows[0:1, 0:128], T.J[0:1, :], True, False), (pK, T.Jm[0:1, 0:128], row["p256"], False, False)])
-        mm("v" + s, ["m8th", "one", "I2"] + xdep + prev("xn"),
-           [(pX, row["m8th"], row["one"], True, False), (pX, T.I2[:], xme, False, False)], xext)
         u, ks, nS = 0, [], 0
         for ci, (who, n, ab) in enumerate(CHUNKS[t]):
             a, b = t * 4096 + u * 256, t * 4096 + (u + n) * 256
@@ -280,13 +294,11 @@ def build(g, core, T, topo):
             unit = [(lo, slice(t * 4096 + lo * 256, t * 4096 + lo * 256 + 256)) for lo in range(u, u + n)]
             if ab == "S":
                 op("S", "A" + cn, [dep], lambda a=a, b=b, src=src: act.activation(T.AB[:, a:b], src, F.Abs))
-                z = "Zk"
             else:
-                ts("A" + cn, [dep], T.AB[:, a:b], src, 0.0, A.max)
+                ts("A" + cn, [dep], T.AB[:, a:b], src, 0.0, A.max, 2.0, A.mult)
                 mm("kd" + cn, [dep, "Zm", "k" + s], [(pK, sel(T.Zm, lo), T.DD[:, c], False, False) for lo, c in unit])
                 ks.append("kd" + cn)
-                z = "Z2"
-            mm("ka" + cn, ["A" + cn, z, "k" + s] + (ks if end else []), [(pK, sel(T[z], lo), T.AB[:, c], False, lo == 15) for lo, c in unit])
+            mm("ka" + cn, ["A" + cn, "Zk", "k" + s] + (ks if end else []), [(pK, sel(T.Zk, lo), T.AB[:, c], False, lo == 15) for lo, c in unit])
             ks.append("ka" + cn)
             u += n
         key = ks[-1]
@@ -295,45 +307,54 @@ def build(g, core, T, topo):
         mm("n" + s, ["rej" + s, "Ib"] + (["fr" + s] if t else []),
            [(T.pN[:, 0:16], T.Ib[:], T.rej[:, t * 256 + k:(t + 1) * 256:16], k == 0, k == 15) for k in range(16)])
         op("V", "scan" + s, [key, "seg"], lambda t=t, pK=pK: vec.tensor_tensor_scan(cut(T.scan, t, 256), T.seg[:], pK, 0.0, A.add, A.min))
-        least, dep = T.scan[:, t * 256 + 15:(t + 1) * 256:16], "scan" + s
-        if SCRATCH["scan"][2] != I4:
-            copy("V", "kI" + s, [dep], cut(T.kI, t, 16), least)
-            least, dep = cut(T.kI, t, 16), "kI" + s
-        if AND_U16:
-            ts("pL" + s, [dep], cut(T.pL, t, 16), least, NF - 1, A.bitwise_and)
-        else:
-            ts("pI" + s, [dep], cut(T.pI, t, 16), least, NF - 1, A.bitwise_and)
-            copy("V", "pL" + s, ["pI" + s], cut(T.pL, t, 16), cut(T.pI, t, 16))
+        ts("pI" + s, ["scan" + s], cut(T.pI, t, 16), T.scan[:, t * 256 + 15:(t + 1) * 256:16], NF - 1, A.bitwise_and)
+        copy("V", "pL" + s, ["pI" + s], cut(T.pL, t, 16), cut(T.pI, t, 16))
         copy("V", "nL" + s, ["n" + s], cut(T.nL, t, 16), T.pN[:, 0:16])
         acc = None if last else T.rsum[:, t:t + 1]
         op("S", "sg" + s, ["nL" + s], lambda t=t, acc=acc: act.activation(cut(T.sg, t, 16), T.pN[:, 0:16], F.Sign, bias=-9.5, accum_out=acc))
         best = cut(T.pL, t, 16)
-        tt("h" + s, ["pL" + s, "x3_" + s], cut(T.hh, t, 256), cut(T.YG, t, 4096).indirect(best), cut(T.x3, t, 256), A.subtract)
-        tt("q" + s, ["h" + s, "nL" + s, "AT"], cut(T.qq, t, 256), T.AT[:, 0:32].indirect(cut(T.nL, t, 16)), cut(T.hh, t, 256), A.mult)
-        mm("vq" + s, ["v" + s, "q" + s, "Ib", "magic"],
-           [(pX, T.Ib[:], cut(T.qq, t, 256), False, False), (pX, row["magic"], row["one"], False, True)])
-        xdst = T.xout[:, 1:V:2] if last else own(T.XT, t + 1)
-        op("S", "xn" + s, ["vq" + s] + (["xe2"] if last else []), lambda xdst=xdst, pX=pX: act.activation(xdst, pX, F.Abs, bias=-MAGIC))
+        parts = PARTS[t]
+        for j, n in enumerate(parts):
+            a, p = sum(parts[:j]), s + "ab"[j]
+            cols, lists = slice(t * 256 + a, t * 256 + a + n), slice(t * 16 + a // 16, t * 16 + (a + n) // 16)
+            pv_ = (T.pS1 if j else T.pX)[:, 0:n]
+            xme = T.XN[:, q * V + t + 2 * a:q * V + t + 2 * (a + n) - 1:2] if t < 2 else T.XT[:, (t - 1) * 1024 + q * 256 + a:(t - 1) * 1024 + q * 256 + a + n]
+            mm("v" + p, ["m8th", "one", "Ib"] + xdep + (bank[1] if j else xnames(t - 1)[:1]),
+               [(pv_, row["m8th"], T.rows[0:1, 0:n], True, False)] + [(pv_, T.Ib[:], xme, False, False)] * 2, xext)
+            tt("h" + p, ["pL" + s, "x3_" + s], T.hh[:, cols], cut(T.YG, t, 4096).indirect(T.pL[:, lists]), T.x3[:, cols], A.subtract)
+            tt("q" + p, ["h" + p, "nL" + s, "AT"], T.qq[:, cols], T.AT[:, 0:32].indirect(T.nL[:, lists]), T.hh[:, cols], A.mult)
+            mm("vq" + p, ["v" + p, "q" + p, "Ib", "magic"],
+               [(pv_, T.Ib[:], T.qq[:, cols], False, False), (pv_, row["magic"], T.rows[0:1, 0:n], False, True)])
+            xdst = T.xout[:, 1:V:2] if last else T.XT[:, (t + 1) * 1024 + q * 256 + a:(t + 1) * 1024 + q * 256 + a + n]
+            op("S", "xn" + p, ["vq" + p] + (["xe2"] if last else []), lambda xdst=xdst, pv_=pv_: act.activation(xdst, pv_, F.Abs, bias=-MAGIC))
+            if j:
+                bank[1] = ["xn" + p]
+            if not last:
+                send("sx" + n1 + "ab"[j], ["xn" + p], xdst, others, eng, T.sem["xa" + n1])
         if last:
-            op("Y", "st_x", ["xn" + s, "xe2"], lambda: g.sync.dma_start(T.yx[:], T.xout[:]).then_inc(T.sem.stored, 16))
+            op("Y", "st_x", xnames(t) + ["xe2"], lambda: g.sync.dma_start(T.yx[:], T.xout[:]).then_inc(T.sem.stored, 16))
         else:
-            send("sx" + n1, ["xn" + s], own(T.XT, t + 1), others, eng, T.sem["xa" + n1])
             ygather(t + 1)
         onehot = T.OH[:, 0:4096].indirect(best)
         tt("selc" + s, ["pL" + s, "OH6"] + cdep, T.sel[:, t * 512:t * 512 + 256], onehot, cme, A.mult, [("oh", 48)])
         tt("self" + s, ["pL" + s, "OH6", "fJ" + s], T.sel[:, t * 512 + 256:(t + 1) * 512], onehot, cut(T.fJ, t, 256), A.mult, [("oh", 48)])
-        bfree = ["eL", "e1_0", "e1_1"] if t == 0 else (prev("zA") if t < 3 else ["eo2"])
-        sums = [(T.pB[:, 0:32], sel(T.Z1, lo), T.sel[:, t * 512 + lo:(t + 1) * 512:16], lo == 0, lo == 15) for lo in range(16)]
-        jump = [(T.pB[:, 0:16], T.Imk[:], cut(T.sg, t, 16), False, False), (T.pB[:, 16:32], T.Ik[:], cut(T.sg, t, 16), False, False)]
-        mm("b" + s, ["selc" + s, "self" + s, "Z1", "sg" + s, "Ik", "Imk"] + bfree, sums[:15] + jump + sums[15:])
-        tt("zA" + s, ["b" + s, "Wn%d" % (t & 1), "e1_" + s], cut(T.zA, t, 32), T.pB[:, 0:32], cut(T.W, t & 1, 32), A.max)
-        if AND_U16:
-            ts("zL" + s, ["zA" + s], cut(T.zL, t, 32), cut(T.zA, t, 32), NS - 1, A.bitwise_and)
-            scene, sdep = T.zL[:, t * 32 + 16:(t + 1) * 32], "zL" + s
+        scene, sdep, sg = T.zI[:, t * 32 + 16:(t + 1) * 32], "zI" + s, cut(T.sg, t, 16)
+        if last:
+            for n, out, a in (("bc", T.pB[:, 0:16], 0), ("be", T.pK[:, 256:272], 256)):
+                mm(n + s, ["selc" + s, "eo2"] if a == 0 else ["self" + s, "scan" + s, "rej" + s],
+                   [(out, sel(T.Z1, lo), T.sel[:, t * 512 + a + lo:t * 512 + a + 256:16], lo == 0, False) for lo in range(16)])
+                mm(n + "j" + s, [n + s, "sg" + s], [(out, T.Ik[:], sg, False, True)])
+            tt("zA" + s, ["bcj" + s, "Wc"], T.zc[:], T.pB[:, 0:16], T.Wc[:], A.min)
+            ts("zL" + s, ["zA" + s], T.zL[:, t * 32:t * 32 + 16], T.zc[:], 4096.0, A.add)
+            tt("zE" + s, ["bej" + s, "e1_" + s], T.zA[:, t * 32 + 16:(t + 1) * 32], T.pK[:, 256:272], T.W[:, 48:64], A.max)
+            ts("zI" + s, ["zE" + s], scene, T.zA[:, t * 32 + 16:(t + 1) * 32], NS - 1, A.bitwise_and)
         else:
+            sums = [(T.pB[:, 0:32], sel(T.Z1, lo), T.sel[:, t * 512 + lo:(t + 1) * 512:16], lo == 0, lo == 15) for lo in range(16)]
+            jump = [(T.pB[:, 0:16], T.Imk[:], sg, False, False), (T.pB[:, 16:32], T.Ik[:], sg, False, False)]
+            mm("b" + s, ["selc" + s, "self" + s, "Z1", "sg" + s, "Ik", "Imk"] + (prev("zA") or ["eL", "e1_0", "e1_1"]), sums[:15] + jump + sums[15:])
+            tt("zA" + s, ["b" + s, "Wn%d" % (t & 1), "e1_" + s], cut(T.zA, t, 32), T.pB[:, 0:32], cut(T.W, t & 1, 32), A.max)
             ts("zI" + s, ["zA" + s], cut(T.zI, t, 32), cut(T.zA, t, 32), NS - 1, A.bitwise_and)
             copy("V", "zL" + s, ["zI" + s], cut(T.zL, t, 32), cut(T.zI, t, 32))
-            scene, sdep = T.zI[:, t * 32 + 16:(t + 1) * 32], "zI" + s
         op("V", "rT" + s, ["rej" + s], lambda rej=rej, rejT=rejT: vec.transpose(rejT, rej))
         calls = []
         for hi in range(16):
@@ -342,18 +363,16 @@ def build(g, core, T, topo):
                 off = 16 + 16 * (half - w)
                 calls.append((T.pM[:, 16 * hi:16 * hi + 16], T["G%d" % half][:, off:off + 128],
                               T.rejT[:, t * 256 + 32 * blk + 16 * w:t * 256 + 32 * blk + 16 * w + 16], w == 0, w == 1))
-        mm("m" + s, ["rT" + s, "G0", "G1"] + (prev("t2") if t else ["TH", "lim0"]), calls)
+        mm("m" + s, ["rT" + s, "G0", "G1"] + [["TH", "lim0"], ["fOff2"], ["fOff3"], ["t22"]][t], calls)
         conv = ["cv" + s + k for k in "abcd"] if t else []
         came = [] if t else [ld("cas")] + [("ca0_%d" % r, len(eng)) for r in range(len(T.cores)) if r != q]
-        tt("t1" + s, ["zL" + s] + conv + cdep, cut(T.t1, t, 256), T.CT[:, 0:4 * V].indirect(T.zL[:, t * 32:t * 32 + 16]), cme, A.subtract, came)
-        tt("t2" + s, ["t1" + s, "m" + s], cut(T.t2, t, 256), pM, cut(T.t1, t, 256), A.mult)
-        mm("c" + s, ["t2" + s, "Ib"] + cdep + [["cOff1"], ["cOff2"], ["cOff3"], ["cn2"]][t],
-           [(pC, T.Ib[:], cme, True, False), (pC, T.Ib[:], cut(T.t2, t, 256), False, True)])
+        table, conv = (T.CT[:, 0:4 * V + 256], conv + ["cc2"]) if last else (T.CT[:, 0:4 * V], conv)
+        tt("t1" + s, ["zL" + s] + conv + cdep, cut(T.t1, t, 256), table.indirect(T.zL[:, t * 32:t * 32 + 16]), cme, A.subtract, came)
+        tt("t2" + s, ["t1" + s, "m" + s] + prev("cn") + ([] if last else ["cOff" + n1]), pC, pM, cut(T.t1, t, 256), A.mult)
+        tt("cn" + s, ["t2" + s] + (["ce2"] if last else []), T.cout[:, 1:V:2] if last else own(T.CH, t), pC, cme, A.add)
         if last:
-            copy("S", "cn" + s, ["c" + s, "ce2"], T.cout[:, 1:V:2], pC)
             op("Y", "st_c", ["cn" + s, "ce2"], lambda: g.sync.dma_start(T.yc[:], T.cout[:]).then_inc(T.sem.stored, 16))
         else:
-            copy(CNE, "cn" + s, ["c" + s], own(T.CH, t), pC)
             send_casts(t + 1, ["cn" + s], own(T.CH, t))
             widen(t + 1, ["cn" + s, "t1" + s])
             pA = T.pN[:, 128:129]
@@ -372,8 +391,10 @@ def build(g, core, T, topo):
                [(T.pB[0:8, 256 + lo:512:16], T.Ib[:, lo:128:16], cut(T.eH, p, 16), True, True) for lo in range(16)])
             copy("S", "eo" + s, ["ef" + s] + (["eo2"] if last else []), T.eout[0:8, p:V:2], T.pB[0:8, 256:512])
         if t == 2:
-            gcopy("xe2", ["xn2"], T.xout[:, 0:V:2], own(T.XT, 3), 256)
+            gcopy("xe2", xnames(2), T.xout[:, 0:V:2], own(T.XT, 3), 256)
             gcopy("ce2", ["cn2"], T.cout[:, 0:V:2], own(T.CH, 2), 256)
+            gcopy("cc2", ["cn1"], T.CT[:, 4 * V:4 * V + 256], own(T.CH, 1), 256)
+            lin("Wc", ["Wn0"], T.Wc[:], T.W[:, 0:16], 0.5, -2048.0 - q * 256)
     op("Y", "st_e", ["eo2", "eo3"], lambda: g.sync.dma_start(T.ye[:], T.eout[0:8, :]).then_inc(T.sem.stored, 16))
     return ops, sent[0]
 
@@ -397,19 +418,17 @@ def hand_on(g, core, rank_core, T, topo):
     others = [T.cores[(q + k) % len(T.cores)] for k in range(1, len(T.cores))]
     eng = out_engines(topo, core, others)
     came = len([e for e in topo.engines(rank_core, core) if e not in out_engines(topo, rank_core, others)])
-    for t in HELP:
-        g.wait_ge(T.sem["ha%d" % t], came)
-        a = (t - 1) * 1024 + q * 256
-        write(g, topo, T.CH[:, a:a + 256] if t else T.CT[:, q * V:(q + 1) * V], others, eng, T.sem["ca%d_%d" % (t, q)], T.sem.sent)
-    g.wait_ge(T.sem.sent, len(HELP) * len(eng))
+    g.wait_ge(T.sem.handed, came)
+    write(g, topo, T.CT[:, q * V:(q + 1) * V], others[DIRECT:], eng, T.sem["ca0_%d" % q], T.sem.sent)
+    g.wait_ge(T.sem.sent, len(eng))
 
 
 def arrange(ops):
     order = {e: [n for n in ops if ops[n][0] == e] for e in "VSPGY"}
-    for e, (first, each) in (ORDER or {}).items():
+    for e, (first, each, final) in (ORDER or {}).items():
         names = first.split()
-        for r in range(RO + 2):
-            for tok in each.split():
+        for r in range(RO):
+            for tok in (final if r == RO - 1 else each).split():
                 n, d = (tok + "@0").split("@")[:2]
                 n = n.replace("#", str(r + int(d)))
                 if n in order[e] and n not in names:
@@ -458,7 +477,7 @@ def rank_program(g, core, T, topo):
     if T.rank_of(core) is not None:
         ops, sent = build(g, core, T, topo)
         emit(g, T, ops, arrange(ops), sent)
-    elif HELP:
+    else:
         for c in T.cores:
             if helper(topo, c) == core:
                 hand_on(g, core, c, T, topo)

@@ -12,83 +12,237 @@ def sb(n, dt):
 
 SCRATCH = {
     "XN": sb(4 * V, B), "XT": sb(4 * 1024, B), "CN": sb(V, H), "CH": sb(3 * 1024, H), "CT": sb(4 * V + 256, I4), "Wc": sb(16, F4), "zc": sb(16, F4),
-    "frms": sb(NF, B), "rols": sb(NS, I4), "scs": sb(32, I4), "sc8": sb(V, I4), "sc8h": sb(V, H), "ths": sb(4, I4), "thf": sb(1, F4),
+    "frms": sb(NF, B), "rols": sb(NS + 16, I4), "selF": sb(V, H), "eU": sb(32, F4), "sT": sb(32, B), "Gk0": sb(160, B), "Gk1": sb(160, B), "scs": sb(32, I4), "sc8": sb(V, I4), "sc8h": sb(V, H), "ths": sb(4, I4), "thf": sb(1, F4),
     "YG": sb(RO * 4096, B), "DD": sb(RO * 4096, B), "AB": sb(RO * 4096, B),
     "fOff": sb(RO * 256, U2), "cOff": sb(RO * 256, U2), "fJ": sb(RO * 256, H), "mh": sb(RO * 256, H), "x3": sb(RO * 256, H),
-    "turn2": sb(16, U2), "scan": sb(RO * 256, I4), "rej": sb(RO * 256, B), "rejT": sb(RO * 256, B),
-    "hh": sb(RO * 256, H), "qq": sb(RO * 256, H), "t1": sb(RO * 256, H), "t2": sb(RO * 256, H), "sel": sb(RO * 512, H),
-    "kI": sb(RO * 16, I4), "pI": sb(RO * 16, I4), "pL": sb(RO * 16, U2), "nL": sb(RO * 16, U2), "sg": sb(RO * 16, B),
-    "W": sb(RO * 32, F4), "zA": sb(RO * 32, I4), "zI": sb(RO * 32, I4), "zL": sb(RO * 32, U2), "eL": sb(32, U2), "eC": sb(32, U2),
-    "eH": sb(32, H), "rsum": sb(RO, F4), "fl": sb(RO, F4), "fr": sb(RO, F4), "lim": sb(RO * 256, F4), "Zk": sb(144, B),
-    "xout": sb(V, B), "cout": sb(V, F4), "eout": sb(V, F4),
-    "J": sb(256, B), "J16": sb(128, B), "Jm": sb(256, B), "pc": sb(4, I4), "pa": sb(4, I4), "pf": sb(12, F4), "Ga": sb(160, B),
-    "iq": sb(16, I4), "io2": sb(16, I4), "turn": sb(16, U2),
-    "Z1": sb(144, B), "Zm": sb(144, B), "Z8": sb(144, B), "G0": sb(160, B), "G1": sb(160, B),
-    "BD": sb(128, F4), "Ib": sb(128, B), "Im": sb(128, B), "Ik": sb(128, B), "Imk": sb(128, B),
-    "Ia": sb(128, B), "w": sb(128, F4), "rows": sb(6 * 256, B), "seg": sb(256, B), "OH": sb(4096, B),
-    "thd": sb(256, F4), "TH": sb(256, F4), "AT": sb(32, B),
+    "turn": sb(16, U2), "scan": sb(RO * 256, I4), "rej": sb(RO * 256, B), "rejT": ("sbuf", [128, RO * 8, 2, 16], B),
+    "hh": sb(RO * 256, H), "qq": sb(RO * 256, H), "t1": sb(RO * 256, H), "mk": sb(RO * 256, H), "sel": ("sbuf", [128, RO, 2, 256], H),
+    "pI": sb(RO * 16, I4), "pL": sb(RO * 16, U2), "nL": sb(RO * 16, U2), "sg": sb(RO * 16, B),
+    "W": sb(64, F4), "zA": sb(RO * 32, I4), "zI": ("sbuf", [128, 2, 2, 16], I4), "zL": sb(RO * 32, U2), "eL": sb(32, U2), "eC": sb(32, H), "eD": sb(32, H), "PT": sb(32, B), "Ihalf": sb(128, B), "uu": sb(256, H),
+    "eH": sb(32, H), "eT": sb(32, I4), "rsum": sb(2 * RO, F4), "fl": sb(RO, F4), "c1": sb(RO, F4),
+    "xout": sb(V, B), "cout": sb(V, F4), "eout": sb(32, F4),
+    "J": sb(256, B), "J16": sb(160, B), "Gb": sb(160, B), "Gc": sb(160, B), "Ik2": sb(128, B), "Jm": sb(256, B), "pc": sb(4, I4), "pa": sb(4, I4), "pf": sb(12, F4), "Ga": sb(160, B),
+    "iq": sb(16, I4), "io2": sb(16, I4), "Zk": sb(144, B),
+    "Z1": sb(144, B), "Zm": sb(144, B), "Z8": sb(144, B), "G0": sb(160, B), "G1": sb(160, B), "Gm0": sb(160, B), "Gm1": sb(160, B),
+    "BD": sb(128, B), "Ib": sb(128, B), "Im": sb(128, B), "Ik": sb(128, B), "Imk": sb(128, B), "Ih": sb(128, H),
+    "Ia": sb(128, B), "w": sb(128, F4), "wk": sb(1, F4), "rows": sb(5 * 256, B), "seg": sb(256, F4), "OH": sb(4096, B),
+    "thd": sb(256, H), "TH": sb(256, F4), "AT": sb(32, B),
+    "pM": ("psum", [128, 16, 2, 16], F4), "pL2": ("psum", [128, 4, 16, 8], F4),
 }
-for n in ("pK", "pN", "pX", "pC", "pB", "pM", "pS0", "pS1"):
+for n in ("pK0", "pK1", "pN", "pX", "pS0", "pS1"):
     SCRATCH[n] = ("psum", [128, 512], F4)
-LOADS = ["x0", "sc", "cas", "rol", "frm", "th", "sc8"]
-SEMAPHORES = (["cV", "cS", "cP", "cG", "sent", "left0", "oh", "stored"] + ["ld_" + n for n in LOADS]
+LOADS = ["x0", "sc", "th", "end", "cas", "rol", "frm"]
+SEMAPHORES = (["cV", "cS", "cP", "cG", "sent", "left0", "stored"] + ["ld_" + n for n in LOADS]
               + ["handed"] + ["xa%d" % t for t in range(RO)] + ["ca%d_%d" % (t, r) for t in range(RO) for r in range(4)])
 
+STORES = ["st_ca", "st_xa", "st_e"]
 DIRECT = 1
-CHUNKS = [[("S", 2, "S"), ("S", 2, "S"), ("S", 2, "S"), ("S", 1, "S"), ("V", 4, "V"), ("V", 3, "V"), ("V", 1, "V"), ("V", 1, "V")]] * 4
-YCH = [[4, 4, 4, 4]] + [[3, 3, 3, 3, 2, 2]] * 3
-YV = [[0, 1], [5], [5], [5]]
+KEYS = [1, 1, 1, 1]
+FEATS = [2, 2, 2, 1]
+CASTS = [1, 1, 1, 1]
+CHUNKS = [["S2 S2 S2 S1 V4 V3 V1 V1"]] * 4
+YCH = ["V4 V4 S4 S4"] + ["S3 S3 S3 S3 S2 V2"] * 3
 ON_S = ["x3_2", "x3_3"]
-PARTS = [[128, 128]] * 3 + [[256]]
 ORDER = {
-    "V": ("one seg0 magic half pa2 pf3 pa0 pa1 m8th p256 pf G1a Ib Z8 AT w seg io2 Z1 OH4 s8h1 thf s8h0 turn2 eC0 x3_1 cOff0 BD turn eL "
-          "cs eC1 fOff0 fOff1 mh1 fJ0 x3_0 Y0_1 Y0_0",
-          "X#_4 X#_5 A#_4 A#_5 X#_6 fOff#@1 X#_7 A#_6 A#_7 e1_#@1 scan# rej# pI# mh#@1 pL# rT# h#a nL# h#b q#a q#b selc# self# Y#_5@1 "
-          "zA# fl#@1 zI# cOff#@1 zL# fr#@1 t1# fJ#@1 eH# t2# fJ#@2 cn#",
-          "X#_4 X#_5 A#_4 X#_6 A#_5 X#_7 A#_6 A#_7 scan# rej# pI# pL# rT# selc# nL# self# h#a zA# q#a zE# zL# zI# t1# eH# t2# cn#"),
-    "S": ("pf5 pf7 pf6 Ik pf9 Ia Wn0 Imk Wn1 Zm Zk G0 thd e1_0 Wc e1_1 Im G1 lim0 TH Y0_2 Y0_3",
-          "x3_#@1 lim# X#_0 X#_1 A#_0 X#_2 A#_1 X#_3 A#_2 A#_3 Y#_4@1 Y#_0@1 Y#_1@1 sg# xn#a xn#b Y#_2@1 Y#_3@1 eo#",
-          "X#_0 X#_1 A#_0 X#_2 A#_1 X#_3 A#_2 A#_3 lim# sg# xn#a eo#"),
-    "P": ("k0 e0 thm co1 my0_1 my0_0",
-          "ft#@1 v#a mx#_0 mx#_1 kd#_4 my#_2 ka#_0 kd#_5 mx#_2 ka#_4 my#_3 ka#_1 mx#_3 kd#_6 ka#_5 ka#_2 kd#_7 ka#_6 ka#_3 ka#_7 "
-          "n# co#@1 vq#a v#b vq#b b# a# my#_1@1 m# my#_0@1 k#@1 ef#",
-          "v#a mx#_0 kd#_4 mx#_1 ka#_0 my#_2 kd#_5 mx#_2 ka#_4 my#_3 ka#_1 mx#_3 kd#_6 ka#_5 kd#_7 ka#_2 ka#_6 ka#_3 ka#_7 "
-          "n# bc# bcj# be# bej# m# vq#a ef#"),
-    "G": ("pc J iq Jm J16 sx0 sc0 OH5 OH6 sd0 xo sx1a sx1b",
+    "V": ("one pa2 pa0 m8th pa1 pf3 pf w Z1 G1a wk io2 magic Z8 turn AT Ib x3_1 s8h0 thf eC1 s8h1 BD cs x3_0 OH4 eC0 mh1 cOff0 eL fOff1 fOff0 seg0 fJ0 seg Y0_1 Y0_0",
+          "X#a4 X#a5 A#a4 A#a5 X#a6 X#a7 mh#@1 fOff#@1 A#a6 A#a7 scan#a rej#a pI#a rT#a pL#a h#a nL#a h#b q#a q#b e1_#@1 self#a selc#a Y#_5@1 cOff#@1 zA#a zI#a fJ#@1 zL#a fl#@1 t1#a fJ#@2 cn#a",
+          "X#a4 X#a5 A#a4 A#a5 X#a6 X#a7 A#a7 A#a6 rej#a scan#a rT#a pI#a pL#a nL#a selc#a self#a h#a zA#a q#a zE#a zL#a zI#a t1#a eT# cn#a eH#"),
+    "S": ("pf5 Im pf6 Ia Ih Zm pf9 Ik G0 thd TH G1 Gm0 e1_0 Imk pf7 Wn0 Zk pf8 Wn1 Gm1 e1_1 Wc pf4 Y0_2 Y0_3",
+          "X#a0 X#a1 A#a0 X#a3 X#a2 x3_#@1 A#a1 A#a2 A#a3 Y#_1@1 Y#_0@1 sg#a xn#a xn#b mk#a Y#_3@1 Y#_2@1 Y#_4@1",
+          "X#a0 X#a1 A#a0 X#a2 A#a1 X#a3 A#a2 A#a3 sg#a mk#a xn#a eo#"),
+    "P": ("e0 thm k0a co1 my0a0 my0a2 my0a3 my0a1",
+          "ft#@1 mx#a0 kd#a4 mx#a1 ka#a0 kd#a5 mx#a3 ka#a4 mx#a2 ka#a5 ka#a1 kd#a7 kd#a6 ka#a2 ka#a6 ka#a3 ka#a7 v#b v#a n#a m#a vq#a vq#b co#@1 b#a a# my#a1@1 my#a2@1 my#a3@1 my#a0@1 k#a@1",
+          "mx#a0 kd#a4 mx#a1 ka#a0 kd#a5 mx#a2 ka#a4 ka#a5 mx#a3 ka#a1 kd#a6 kd#a7 ka#a2 ka#a3 ka#a6 ka#a7 v#a n#a m#a bc#a bcj#a be#a bej#a vq#a ef#"),
+    "G": ("pc J iq Jm J16 sx0 sc0 OH5 OH6 oh1 sd0 oh2 oh3 xo sx1a sx1b",
           "sc#@1 cv#a@1 cc#@1 xe# ce# cv#b@1 cv#c@1 cv#d@1 sx#a@2 sx#b@2", ""),
 }
+
+
+CHUNKS2 = [["S2 S2 S1 V2 M2 V3 M2 V1 V1"]] * 4
+YCH2 = ["V4 V4 S4 S4"] + ["S4 S4 S4 S3 V1"] * 3
+ORDER2 = dict({
+    "V": ("m8th pf3 magic wk one pa0 pa1 pa2 pf G1a io2 Ib turn Z1 w Z8 OH4 s8h1 x3_0 thf BD eC1 cs s8h0 AT mh1 cOff0 x3_1 eL seg0 eC0 fOff1 fOff0 seg fJ0 Y0_1 Y0_0",
+          "e1_#@1 X#a3 X#a4 A#a3 X#a5 X#a6 A#a5 fOff#@1 X#a7 X#a8 A#a7 A#a8 mh#@1 rej#a scan#a pI#a rT#a pL#a nL#a h#a q#a h#b q#b self#a selc#a fJ#@1 Y#_4@1 zA#a zI#a zL#a fl#@1 t1#a fJ#@2 cn#a cOff#@1",
+          "X#a3 X#a5 A#a3 A#a5 X#a4 X#a6 X#a8 X#a7 A#a7 A#a8 rej#a scan#a rT#a pI#a pL#a nL#a selc#a self#a h#a q#a zA#a zE#a zL#a zI#a t1#a eT# cn#a eH#"),
+    "S": ("pf5 pf6 pf7 Zk Wn0 Ih Ik G1 Imk pf9 Zm thd TH G0 Wc Gm0 Im pf8 Ia Wn1 e1_1 Gm1 e1_0 pf4 Y0_2 Y0_3",
+          "x3_#@1 X#a0 X#a2 X#a1 A#a0 A#a1 A#a4 A#a2 A#a6 Y#_0@1 Y#_1@1 xn#a mk#a sg#a xn#b Y#_3@1 Y#_2@1",
+          "X#a0 X#a2 X#a1 A#a0 A#a1 A#a2 A#a4 A#a6 sg#a mk#a xn#a eo#"),
+    "P": ("thm e0 co1 k0a my0a2 my0a1 my0a0",
+          "ft#@1 mx#a0 kd#a3 mx#a1 mx#a2 ka#a3 ka#a0 kd#a5 ka#a1 ka#a4 ka#a5 ka#a2 kd#a7 ka#a6 kd#a8 ka#a7 ka#a8 v#a n#a m#a vq#a v#b my#a0@1 vq#b a# b#a co#@1 my#a2@1 my#a1@1 k#a@1",
+          "mx#a0 kd#a3 mx#a2 mx#a1 kd#a5 ka#a5 ka#a1 ka#a2 ka#a3 ka#a0 ka#a4 kd#a8 ka#a6 kd#a7 ka#a7 ka#a8 v#a n#a m#a bc#a bcj#a be#a bej#a vq#a ef#"),
+})
+YCH = ["V4 V4 S4 S4"] + ["S4 S3 S3 S3 V1 V1 V1"] * 3
+ORDER.update({
+    "V": ("magic m8th kilo w wk pf3 pa1 pa2 pa0 pf G1a one io2 Ib Z1 Z8 AT turn OH4 x3_0 thf s8h1 BD Gb Gc s8h0 eC0 cOff0 eC1 cs seg0 fOff0 fOff1 eL mh1 x3_1 fJ0 seg Y0_1 Y0_0",
+          "X#a4 X#a5 A#a4 A#a5 X#a6 fOff#@1 X#a7 A#a6 A#a7 Y#_6@1 scan#a rej#a pI#a rT#a pL#a mh#@1 h#a nL#a h#b q#a q#b self#a selc#a Y#_5@1 Y#_4@1 zL#a zE#a fl#@1 zI#a fJ#@1 t1#a zS#@2 e1_#@2 cOff#@1 cn#a fJ#@2",
+          "X#a4 X#a5 A#a4 X#a7 A#a5 A#a7 X#a6 A#a6 rej#a scan#a rT#a pI#a pL#a nL#a selc#a self#a h#a zL#a q#a zE#a t1#a zI#a eT# cn#a eH#"),
+    "S": ("pf5 pf6 G1 pf8 pf9 Im pf7 Ik G0 thd Gm1 TH Zk pf4 Zm Ih Ik2 Imk Gm0 e1_1 e1_0 Ia Y0_2 Y0_3",
+          "X#a0 X#a1 A#a0 X#a3 X#a2 A#a3 A#a1 A#a2 Y#_1@1 Y#_0@1 sg#a x3_#@1 mk#a xn#a xn#b Y#_3@1 Y#_2@1",
+          "X#a0 X#a1 A#a0 X#a2 X#a3 A#a1 A#a2 A#a3 sg#a mk#a xn#a eo#"),
+    "P": ("thm k0a e0 co1 my0a2 my0a0 my0a3 my0a1",
+          "ft#@1 mx#a0 kd#a4 mx#a1 ka#a0 kd#a5 mx#a3 ka#a4 mx#a2 kd#a6 ka#a3 ka#a5 ka#a1 kd#a7 ka#a6 ka#a2 ka#a7 v#a v#b n#a m#a vq#a a# vq#b b#a mc#a co#@1 my#a3@1 my#a2@1 k#a@1 my#a1@1 my#a0@1",
+          "mx#a0 kd#a4 mx#a1 ka#a0 kd#a5 mx#a2 ka#a4 kd#a7 mx#a3 ka#a5 ka#a1 ka#a2 kd#a6 ka#a6 ka#a3 ka#a7 v#a n#a m#a bc#a b#a mc#a vq#a ef#"),
+})
+CHUNKS = [["S2 S2 S2 V3 M1 V3 V2 V1"]] * 4
+YCH = ["V4 V4 S4 S4"] + ["S4 S4 S3 S3 V1 V1"] * 3
+ON_S = ["x3_2", "x3_3", "fJ1", "fJ2", "fJ3"]
+ORDER.update({
+    "V": ("magic m8th kilo w wk pf3 pa1 pa2 pa0 pf G1a one io2 Ib Z1 Z8 AT turn OH4 x3_0 thf s8h1 BD Gb Gc s8h0 eC0 cOff0 eC1 cs seg0 fOff0 fOff1 eL mh1 x3_1 fJ0 seg Y0_1 Y0_0",
+          "X#a3 X#a4 A#a3 X#a5 X#a6 fOff#@1 A#a5 X#a7 A#a6 A#a7 mh#@1 scan#a rej#a pI#a pL#a rT#a h#a nL#a h#b q#a q#b self#a selc#a Y#_4@1 Y#_5@1 zE#a zL#a fl#@1 zI#a t1#a e1_#@2 zS#@2 cOff#@1 cn#a",
+          "X#a3 X#a4 A#a3 X#a5 X#a6 A#a5 X#a7 A#a6 A#a7 rej#a scan#a rT#a pI#a pL#a nL#a selc#a self#a h#a zL#a q#a zE#a t1#a zI#a eT# cn#a eH#"),
+    "S": ("pf5 pf6 G1 pf8 pf9 Im pf7 Ik G0 thd Gm1 TH Zk pf4 Zm Ih Ik2 Imk Gm0 e1_1 e1_0 Ia Y0_2 Y0_3",
+          "X#a0 X#a1 A#a0 X#a2 A#a1 A#a4 A#a2 Y#_0@1 fJ#@1 Y#_1@1 sg#a mk#a xn#a xn#b Y#_2@1 Y#_3@1 fJ#@2 x3_#@1",
+          "X#a0 X#a1 A#a0 X#a2 A#a1 A#a4 A#a2 mk#a sg#a xn#a eo#"),
+    "P": ("thm k0a e0 co1 my0a0 my0a1 my0a2",
+          "ft#@1 mx#a0 kd#a3 mx#a1 ka#a0 ka#a3 mx#a2 kd#a5 ka#a1 ka#a4 kd#a6 ka#a2 ka#a5 kd#a7 ka#a6 ka#a7 v#a v#b n#a k#a@1 m#a vq#a vq#b mc#a a# b#a co#@1 my#a0@1 my#a2@1 my#a1@1",
+          "mx#a0 kd#a3 mx#a1 ka#a0 ka#a3 mx#a2 kd#a5 ka#a1 ka#a4 kd#a6 ka#a5 ka#a2 kd#a7 ka#a6 ka#a7 n#a m#a v#a bc#a b#a mc#a vq#a ef#"),
+})
+CHUNKS = [["S2 S2 S2 V3 M1 V3 V2 V1"]] * 3 + [["S2 S2 S2 S1 V3 V3 V2 V1"]]
+ON_S = ["x3_2", "x3_3", "fJ0", "fJ1", "fJ2", "fJ3", "cs", "s8h0", "s8h1"]
+ORDER.update({
+    "V": ("magic pa2 pa0 pa1 pf3 pf Ib G1a w io2 Z1 one turn x3_0 Z8 thf OH4 m8th Gb BD cOff0 wk x3_1 Gc AT eC1 eC0 eL mh1 fOff0 kilo seg0 fOff1 seg Y0_1 Y0_0",
+          "X#a3 X#a4 A#a3 X#a5 X#a6 fOff#@1 A#a5 X#a7 A#a6 A#a7 scan#a rej#a pI#a mh#@1 pL#a rT#a h#a nL#a h#b q#a q#b selc#a self#a Y#_4@1 Y#_5@1 zE#a zL#a fl#@1 zI#a t1#a e1_#@2 zS#@2 cOff#@1 cn#a",
+          "X#a4 X#a5 A#a4 A#a5 X#a6 X#a7 A#a6 A#a7 rej#a scan#a rT#a pI#a pL#a nL#a selc#a self#a h#a zL#a q#a zE#a t1#a zI#a eT# cn#a eH#"),
+    "S": ("pf5 pf6 pf8 pf4 pf7 Ih Ik Imk Ia Ik2 Zk s8h1 s8h0 thd pf9 cs G0 TH Zm Im Gm1 e1_0 e1_1 G1 fJ0 Gm0 Y0_2 Y0_3",
+          "X#a0 X#a1 X#a2 A#a0 A#a1 A#a4 A#a2 fJ#@1 Y#_0@1 Y#_1@1 sg#a mk#a xn#a xn#b Y#_2@1 Y#_3@1 fJ#@2 x3_#@1",
+          "X#a0 X#a1 A#a0 X#a2 X#a3 A#a1 A#a3 A#a2 mk#a sg#a xn#a eo#"),
+    "P": ("e0 thm co1 my0a2 k0a my0a0 my0a1",
+          "ft#@1 mx#a0 kd#a3 mx#a1 ka#a3 mx#a2 ka#a0 kd#a5 ka#a1 kd#a6 ka#a4 ka#a2 ka#a5 kd#a7 ka#a6 ka#a7 v#a n#a v#b m#a my#a0@1 vq#a vq#b a# mc#a b#a co#@1 my#a1@1 my#a2@1 k#a@1 my#a3@1",
+          "mx#a0 kd#a4 mx#a1 ka#a0 kd#a5 ka#a4 mx#a2 mx#a3 ka#a5 ka#a1 kd#a6 kd#a7 ka#a3 ka#a6 ka#a2 ka#a7 v#a n#a m#a bc#a b#a mc#a vq#a ef#"),
+})
+KEYS = [2, 2, 2, 1]
+CHUNKS = [["S4 S3 V5 V4", "S4 S3 V4 V3 V2"]] * 3 + [["S2 S2 S2 S1 V3 V3 V2 V1"]]
+ON_S = ["x3_2", "x3_3", "cs", "s8h0", "s8h1"]
+ORDER.update({
+    "V": ("pa0 pa1 pa2 pf3 pf Ib io2 wk kilo OH4 thf w x3_1 magic Z8 AT Z1 G1a eC0 BD one m8th Gb turn x3_0 Gc eL eC1 mh1 fJ0 seg0 fJ1 fOff0 seg Y0_0 cOff0 Y0_1 fOff1",
+          "X#a2 X#a3 A#a2 A#a3 X#b2 X#b3 rej#a fOff#@1 scan#a X#b4 pI#a A#b2 pL#a A#b3 nL#a h#a A#b4 q#a scan#b rej#b pI#b pL#b rT#a h#b nL#b mh#@1 q#b self#a selc#a Y#_4@1 Y#_5@1 zE#a zL#a fl#@1 zI#a t1#a zS#@2 e1_#@2 fJ#@2 cOff#@1 cn#a",
+          "X#a4 X#a5 A#a4 A#a5 X#a6 X#a7 A#a6 A#a7 rej#a scan#a rT#a pI#a pL#a nL#a selc#a self#a h#a zL#a q#a zE#a t1#a zI#a eT# cn#a eH#"),
+    "S": ("pf5 pf7 pf8 Ik2 pf6 Ia Imk pf9 s8h0 s8h1 Im thd cs pf4 TH G0 Zm e1_1 Zk Gm1 Ik Gm0 G1 Ih e1_0 Y0_3 Y0_2",
+          "x3_#@1 X#a0 X#a1 A#a0 A#a1 X#b0 X#b1 A#b0 A#b1 Y#_0@1 sg#a xn#a Y#_1@1 sg#b xn#b mk#a Y#_2@1 c1_#@1 Y#_3@1",
+          "X#a0 X#a1 A#a0 X#a2 X#a3 A#a1 A#a3 A#a2 mk#a sg#a xn#a eo#"),
+    "P": ("e0 thm k0a ft0 co0 my0a0 ft1 my0a1 k0b my0b0",
+          "ft#@1 mx#a0 kd#a2 mx#a1 kd#a3 ka#a2 ka#a0 ka#a1 ka#a3 my#b1 mx#b0 kd#b2 mx#b1 kd#b3 n#a ka#b0 ka#b2 ka#b1 ka#b3 kd#b4 ka#b4 v#a vq#a n#b m#a my#a0@1 v#b vq#b k#a@1 a# b#a co#@1 mc#a my#a3@1 my#b0@1 k#b@1 my#a1@1 my#a2@1",
+          "mx#a0 kd#a4 mx#a1 ka#a0 kd#a5 ka#a4 mx#a2 mx#a3 ka#a5 ka#a1 kd#a6 kd#a7 ka#a3 ka#a6 ka#a2 ka#a7 v#a n#a m#a bc#a b#a mc#a vq#a ef#"),
+})
+YCH = ["V4 V4 S4 S4"] + ["S4 S3 S3 S3 V1 V2"] * 3
+ORDER.update({
+    "V": ("pa0 pa2 pa1 pf3 pf w Ib kilo io2 Z8 turn wk G1a m8th Gb OH4 x3_0 thf BD eC0 Gc Z1 one x3_1 eL eC1 magic AT fJ0 seg0 fJ1 seg fOff0 mh1 cOff0 Y0_0 Y0_1 fOff1",
+          "X#a2 X#a3 A#a2 A#a3 fOff#@1 X#b2 X#b3 rej#a scan#a X#b4 pI#a A#b2 pL#a A#b3 A#b4 h#a nL#a q#a scan#b rej#b pI#b mh#@1 pL#b rT#a h#b nL#b q#b selc#a self#a Y#_5@1 Y#_4@1 zE#a zL#a fl#@1 zI#a t1#a zS#@2 e1_#@2 cOff#@1 fJ#@2 cn#a",
+          "X#a4 X#a5 A#a4 A#a5 X#a6 X#a7 A#a6 A#a7 rej#a scan#a pI#a rT#a pL#a nL#a selc#a self#a h#a zL#a q#a zE#a t1#a zI#a eT# cn#a eH#"),
+    "S": ("pf5 pf8 pf7 pf6 Ia Ih pf9 Ik s8h0 s8h1 Im Imk thd cs Ik2 TH G1 pf4 G0 e1_0 Gm0 Gm1 Zk Zm e1_1 Y0_2 Y0_3",
+          "x3_#@1 X#a0 X#a1 A#a0 A#a1 X#b0 X#b1 A#b0 A#b1 Y#_0@1 sg#a xn#a Y#_1@1 sg#b xn#b mk#a Y#_2@1 Y#_3@1 c1_#@1",
+          "X#a0 X#a1 A#a0 X#a2 X#a3 A#a1 A#a3 A#a2 sg#a mk#a xn#a eo#"),
+    "P": ("e0 thm ft0 co0 k0b my0b0 ft1 k0a my0a0 my0a1",
+          "ft#@1 mx#a0 kd#a2 mx#a1 kd#a3 my#b1 ka#a2 ka#a0 ka#a1 ka#a3 mx#b0 kd#b2 mx#b1 kd#b3 n#a kd#b4 ka#b0 ka#b2 ka#b1 ka#b3 ka#b4 v#a vq#a n#b m#a v#b vq#b k#a@1 a# b#a co#@1 mc#a my#a1@1 my#a0@1 my#a3@1 my#b0@1 my#a2@1 k#b@1",
+          "mx#a0 kd#a4 mx#a1 ka#a0 kd#a5 ka#a4 mx#a2 mx#a3 ka#a5 kd#a6 ka#a1 kd#a7 ka#a3 ka#a6 ka#a2 ka#a7 n#a v#a m#a bc#a b#a mc#a vq#a ef#"),
+})
+ON_S = ["cs"]
+ORDER.update({
+    "V": ("pa0 pa2 pa1 pf3 pf w Ib G1a kilo wk eC0 eC1 m8th eD Gb OH4 x3_0 thf BD Gc Z1 one x3_1 eL magic back AT PT fJ0 seg0 fJ1 seg fOff0 mh1 Y0_0 cOff0 Y0_1 fOff1",
+          "X#a2 X#a3 A#a2 A#a3 fOff#@1 X#b2 X#b3 rej#a scan#a X#b4 pI#a A#b2 pL#a A#b3 A#b4 h#a nL#a q#a scan#b rej#b pI#b mh#@1 pL#b rT#a h#b nL#b q#b selc#a self#a Y#_5@1 Y#_4@1 zE#a zL#a fl#@1 zI#a c1_#@1 t1#a zS#@2 e1_#@2 cOff#@1 fJ#@2 cn#a x3_#@1",
+          "X#a4 X#a5 A#a4 A#a5 X#a6 X#a7 A#a6 A#a7 rej#a scan#a pI#a rT#a pL#a nL#a selc#a self#a zL#a zE#a t1#a zI#a xn#a eT# cn#a eH#"),
+    "S": ("pf8 pf7 pf6 pf9 G1 G0 Ia Ih Ik Im Imk thd cs Ik2 TH pf4 e1_0 Gm0 Gm1 Zk Zm e1_1 Ihalf Y0_2 Y0_3",
+          "X#a0 X#a1 A#a0 A#a1 X#b0 X#b1 A#b0 A#b1 Y#_0@1 sg#a xn#a Y#_1@1 sg#b xn#b mk#a Y#_2@1 Y#_3@1",
+          "X#a0 X#a1 A#a0 X#a2 X#a3 A#a1 A#a3 A#a2 h#a sg#a q#a mk#a xu#a eo#"),
+    "P": ("e0 thm ft0 co0 k0b my0b0 ft1 k0a my0a0 my0a1",
+          "ft#@1 mx#a0 kd#a2 mx#a1 kd#a3 my#b1 ka#a2 ka#a0 ka#a1 ka#a3 mx#b0 kd#b2 mx#b1 kd#b3 n#a kd#b4 ka#b0 ka#b2 ka#b1 ka#b3 ka#b4 v#a vq#a n#b m#a v#b vq#b k#a@1 a# b#a co#@1 mc#a my#a1@1 my#a0@1 my#a3@1 my#b0@1 my#a2@1 k#b@1",
+          "mx#a0 kd#a4 mx#a1 ka#a0 kd#a5 ka#a4 mx#a2 mx#a3 ka#a5 kd#a6 ka#a1 kd#a7 ka#a3 ka#a6 ka#a2 ka#a7 u#a n#a v#a m#a bc#a uh#a vh#a b#a uq#a vq#a mc#a ef#"),
+    "G": ("pc J Jm J16 sx0 sc0 OH5 OH6 oh1 sd0 oh2 oh3 xo sx1a sx1b",
+          "sc#@1 cv#a@1 xe# ce# cv#b@1 cv#c@1 cv#d@1 sx#a@2 sx#b@2", ""),
+})
+ORDER.update({
+    "V": ("kilo m8th pa2 pa0 pa1 pf magic wk pf3 Ib G1a eC0 thf PT AT x3_0 w eC1 Z1 back x3_1 OH4 eD one Gb eL BD mh1 Gc fJ0 seg0 fJ1 seg fOff0 Y0_0 cOff0 Y0_1 fOff1",
+          "X#a2 X#a3 A#a2 A#a3 X#b2 X#b3 rej#a fOff#@1 scan#a A#b3 pI#a A#b2 pL#a X#b4 h#a nL#a A#b4 q#a x3_#@1 scan#b rej#b pI#b rT#a pL#b mh#@1 h#b nL#b q#b selc#a self#a Y#_5@1 zL#a zE#a Y#_4@1 zI#a fl#@1 t1#a zS#@2 c1_#@1 e1_#@2 cOff#@1 fJ#@2 cn#a",
+          "X#a4 X#a5 A#a4 A#a5 X#a6 A#a6 X#a7 A#a7 scan#a rej#a pI#a pL#a rT#a selc#a nL#a self#a zL#a t1#a zE#a zI#a eT# xn#a eH# cn#a"),
+    "S": ("pf6 pf7 pf4 pf9 Ik G1 G0 Ih Im Ik2 cs thd Imk Zm TH Ihalf Gm1 Zk pf8 Gm0 e1_0 Ia e1_1 Y0_3 Y0_2",
+          "X#a0 X#a1 A#a0 A#a1 X#b0 X#b1 A#b0 A#b1 Y#_0@1 sg#a xn#a Y#_1@1 sg#b xn#b Y#_2@1 mk#a Y#_3@1",
+          "X#a1 X#a3 X#a0 X#a2 A#a0 A#a1 A#a2 A#a3 h#a sg#a mk#a q#a xu#a eo#"),
+    "P": ("e0 thm ft0 co0 ft1 my0a1 my0a0 my0b0 k0a k0b",
+          "ft#@1 mx#a0 kd#a2 mx#a1 kd#a3 ka#a0 ka#a2 my#b1 ka#a1 ka#a3 mx#b0 kd#b2 mx#b1 kd#b3 n#a ka#b0 ka#b3 ka#b1 kd#b4 ka#b2 ka#b4 v#a vq#a n#b m#a v#b vq#b k#a@1 a# b#a co#@1 mc#a my#a1@1 my#a0@1 my#b0@1 my#a2@1 k#b@1 my#a3@1",
+          "mx#a1 mx#a3 kd#a4 mx#a0 kd#a5 ka#a4 mx#a2 ka#a5 ka#a0 kd#a6 ka#a1 ka#a6 ka#a2 kd#a7 ka#a3 ka#a7 v#a u#a n#a m#a bc#a uh#a b#a uq#a vh#a vq#a mc#a ef#"),
+})
+ON_S = ["cs", "x3_2", "fJ2", "fJ3", "eo3"]
+CHUNKS = [["S4 S3 V5 V4", "S4 S3 V5 V4"]] * 3 + [["S2 S2 S2 S1 V3 V3 V2 V1"]]
+ORDER.update({
+    "V": ("back magic one pf3 w pa0 pa1 Ib pa2 wk pf G1a Z1 kilo OH4 x3_1 eC0 AT eC1 Gb m8th eD thf x3_0 BD Gc eL PT cOff0 fJ0 fJ1 seg0 mh1 seg fOff0 Y0_0 Y0_1",
+          "X#a2 X#a3 A#a2 A#a3 eT#@-1 X#b2 eH#@-1 X#b3 fOff#@1 rej#a scan#a A#b2 pI#a A#b3 pL#a nL#a h#a q#a scan#b rej#b pI#b mh#@1 pL#b rT#a h#b nL#b q#b selc#a self#a Y#_4@1 zE#a fl#@1 zI#a Y#_5@1 zL#a cOff#@1 t1#a cn#a",
+          "X#a4 X#a5 A#a4 A#a5 X#a6 A#a6 X#a7 A#a7 scan#a rej#a pI#a pL#a rT#a selc#a nL#a self#a zL#a sT# t1#a zE#a cn#a zI#a xn#a"),
+    "S": ("Ia Imk Ik pf6 Ik2 pf9 G1 Ih G0 pf8 cs Zm Zk thd pf7 Gm1 TH Im W0 e1_0 Gm0 Ihalf pf4 e1_1 Y0_3 Y0_2",
+          "X#a0 X#a1 A#a0 A#a1 eu#@-1 X#b0 X#b1 A#b0 A#b1 Y#_0@1 sg#a x3_#@1 xn#a Y#_1@1 sg#b xn#b Y#_2@1 mk#a Y#_3@1 c1_#@1 fJ#@2",
+          "X#a3 X#a1 X#a0 X#a2 A#a3 A#a0 A#a1 A#a2 Gk0 Gk1 h#a sg#a mk#a q#a xu#a eo#"),
+    "P": ("e0 co0 thm k0a ft0 ft1 k0b my0b0 my0a1 my0a0",
+          "ft#@1 mx#a0 kd#a2 mx#a1 kd#a3 ka#a0 ef#@-1 ka#a2 ka#a1 my#b1 ka#a3 mx#b0 kd#b2 mx#b1 kd#b3 n#a ka#b0 ka#b1 ka#b2 ka#b3 v#a vq#a n#b v#b m#a my#a0@1 vq#b a# b#a co#@1 mc#a my#a3@1 k#b@1 my#a2@1 my#b0@1 k#a@1 my#a1@1",
+          "mx#a3 mx#a1 kd#a4 mx#a0 kd#a5 ka#a4 mx#a2 ka#a3 ka#a5 ka#a0 kd#a6 ka#a1 ka#a6 ka#a2 kd#a7 ka#a7 u#a v#a n#a m#a b#a uh#a mc#a be# uq#a vh#a vq#a"),
+})
+ORDER.update({
+    "V": ("m8th w pa1 pa0 pa2 pf3 pf Ib AT PT G1a kilo Z1 one eC0 eC1 Gb eD thf BD back OH4 Gc wk mh1 eL cOff0 magic x3_0 fJ0 fJ1 seg0 fOff0 x3_1 seg Y0_0 fOff1 Y0_1",
+          "eT#@-1 X#a2 eH#@-1 X#a3 A#a2 A#a3 X#b2 X#b3 fOff#@1 rej#a scan#a A#b3 pI#a A#b2 pL#a nL#a h#a mh#@1 q#a scan#b rej#b pI#b pL#b rT#a h#b nL#b q#b selc#a self#a Y#_5@1 zE#a fl#@1 zI#a zL#a Y#_4@1 t1#a cOff#@1 cn#a",
+          "X#a4 X#a5 A#a4 A#a5 X#a6 X#a7 A#a6 A#a7 scan#a rej#a pI#a rT#a pL#a selc#a nL#a self#a zL#a sT# t1#a cn#a zE#a xn#a zI#a"),
+    "S": ("pf6 pf9 Im G1 Zk G0 cs W0 pf7 Ik thd Imk pf4 Gm0 Gm1 pf8 TH Zm e1_1 e1_0 Ik2 Ih Ia Ihalf Y0_3 Y0_2",
+          "X#a0 X#a1 A#a0 eu#@-1 A#a1 X#b0 X#b1 A#b0 A#b1 Y#_0@1 sg#a x3_#@1 xn#a Y#_1@1 sg#b xn#b mk#a Y#_2@1 Y#_3@1 fJ#@2 c1_#@1",
+          "X#a3 X#a1 X#a0 X#a2 A#a0 A#a3 A#a1 A#a2 Gk0 Gk1 h#a sg#a mk#a q#a xu#a eo#"),
+    "P": ("e0 co0 k0a thm ft0 ft1 my0a1 my0a0 my0b0 k0b",
+          "ft#@1 mx#a0 ef#@-1 kd#a2 mx#a1 kd#a3 ka#a0 ka#a2 my#b1 ka#a1 ka#a3 mx#b0 kd#b2 mx#b1 kd#b3 n#a ka#b0 ka#b1 ka#b2 ka#b3 v#a vq#a n#b m#a v#b my#a1@1 vq#b a# b#a co#@1 mc#a my#b0@1 k#a@1 my#a0@1 my#a3@1 my#a2@1 k#b@1",
+          "mx#a3 kd#a4 mx#a1 mx#a0 kd#a5 ka#a4 mx#a2 ka#a5 ka#a0 kd#a6 ka#a3 ka#a1 kd#a7 ka#a6 ka#a2 ka#a7 v#a u#a mb#a n#a m#a b#a uh#a mc#a be# vh#a uq#a vq#a"),
+})
+ORDER.update({
+    "V": ("kilo one pa1 pa0 pa2 wk pf m8th pf3 Z1 back G1a w Ib OH4 magic thf eC1 eC0 Gb eD AT Gc BD x3_0 eL x3_1 PT mh1 cOff0 fJ0 fJ1 seg0 fOff0 seg Y0_0 Y0_1 fOff1",
+          "eT#@-1 X#a2 X#a3 A#a2 eH#@-1 A#a3 X#b2 X#b3 rej#a fOff#@1 scan#a A#b3 pI#a A#b2 pL#a nL#a h#a q#a scan#b rej#b pI#b pL#b rT#a h#b nL#b mh#@1 q#b selc#a self#a Y#_5@1 zE#a zI#a Y#_4@1 zL#a fl#@1 t1#a cOff#@1 cn#a",
+          "X#a4 X#a5 A#a4 A#a5 X#a6 A#a6 X#a7 A#a7 scan#a rej#a pI#a pL#a rT#a selc#a nL#a self#a zL#a sT# t1#a cn#a xn#a zE#a zI#a"),
+    "S": ("W0 pf6 pf7 Zm pf9 pf8 G0 Ik2 G1 cs Imk thd Zk Ihalf e1_1 Im Ih TH e1_0 Gm1 Gm0 Ik Ia pf4 Y0_2 Y0_3",
+          "X#a0 X#a1 A#a0 A#a1 X#b0 X#b1 eu#@-1 A#b0 A#b1 Y#_0@1 sg#a x3_#@1 xn#a Y#_1@1 sg#b xn#b mk#a Y#_2@1 Y#_3@1 c1_#@1 fJ#@2",
+          "X#a1 X#a3 X#a0 A#a3 X#a2 A#a0 A#a1 A#a2 Gk1 Gk0 h#a mk#a sg#a q#a xu#a eo#"),
+    "P": ("e0 co0 thm ft0 k0b my0a0 ft1 my0b0 my0a1 k0a",
+          "ft#@1 mx#a0 kd#a2 mx#a1 kd#a3 my#b1 ka#a2 ka#a1 ef#@-1 ka#a0 ka#a3 mx#b0 kd#b2 mx#b1 kd#b3 n#a ka#b0 ka#b1 ka#b2 ka#b3 v#a vq#a n#b m#a my#a1@1 v#b vq#b a# b#a co#@1 mc#a my#b0@1 k#b@1 my#a2@1 my#a0@1 my#a3@1 k#a@1",
+          "mx#a1 mx#a3 kd#a4 mx#a0 kd#a5 ka#a3 ka#a4 mx#a2 ka#a5 ka#a0 kd#a6 ka#a1 ka#a6 ka#a2 kd#a7 ka#a7 v#a mb#a u#a n#a m#a b#a uh#a vh#a uq#a mc#a vq#a be#"),
+})
+
+
+def pieces(n):
+    return [(j, "ab"[j], 16 // n * j, 16 // n) for j in range(n)]
 
 
 def build(g, core, T, topo):
     A, F = AluOpType, ActivationFunctionType
     q = T.rank_of(core)
     vec, act, pe = g.vector, g.scalar, g.tensor
-    ops, bank = {}, {}
+    ops, turn = {}, {}
 
-    def op(eng, name, deps, fn, ext=()):
+    def op(eng, name, deps, fn, ext=(), bank=None):
         assert name not in ops
-        ops[name] = (eng, fn, list(deps), list(ext))
+        deps = list(deps)
+        if bank:
+            who, now, before = turn.get(bank, (eng, [], []))
+            turn[bank] = (eng, now + [name], before) if who == eng else (eng, [name], now)
+            deps += turn[bank][2]
+        ops[name] = (eng, fn, deps, list(ext))
 
     def mm(name, deps, calls, ext=()):
-        op("P", name, deps, lambda: [pe.matmul(*c) for c in calls][-1], ext)
+        op("P", name, deps, lambda: [pe.matmul(*c) for c in calls[1:]][-1], ext, calls[0])
 
-    def copy(eng, name, deps, out, src, ext=()):
-        op(eng, name, deps, (lambda: act.activation(out, src, F.Copy)) if eng == "S" else (lambda: vec.tensor_copy(out, src)), ext)
+    def copy(eng, name, deps, out, src, ext=(), bank=None):
+        op(eng, name, deps, (lambda: act.activation(out, src, F.Copy)) if eng == "S" else (lambda: vec.tensor_copy(out, src)), ext, bank)
 
     def gcopy(name, deps, out, src, n, ext=()):
         op("G", name, deps, lambda: g.affine_select(out, src, [[0, n]], A.is_ge, 0.0, 0, 0), ext)
 
-    def tt(name, deps, out, a, b, alu, ext=()):
-        op("V", name, deps, lambda: vec.tensor_tensor(out, a, b, alu), ext)
+    def tt(name, deps, out, a, b, alu, ext=(), bank=None):
+        op("V", name, deps, lambda: vec.tensor_tensor(out, a, b, alu), ext, bank)
 
-    def ts(name, deps, out, a, s1, o1, s2=None, o2=None, ext=()):
+    def ts(name, deps, out, a, s1, o1, s2=None, o2=None, ext=(), bank=None):
         if o2 is None:
-            op("V", name, deps, lambda: vec.tensor_scalar(out, a, s1, None, o1), ext)
+            op("V", name, deps, lambda: vec.tensor_scalar(out, a, s1, None, o1), ext, bank)
         else:
-            op("V", name, deps, lambda: vec.tensor_scalar(out, a, s1, s2, o1, o2), ext)
+            op("V", name, deps, lambda: vec.tensor_scalar(out, a, s1, s2, o1, o2), ext, bank)
 
-    def lin(name, deps, out, a, scale, bias=0.0, ext=()):
-        op("S", name, deps, lambda: act.activation(out, a, F.Identity, bias=bias, scale=scale), ext)
+    def lin(name, deps, out, a, scale, bias=0.0, ext=(), bank=None):
+        op("S", name, deps, lambda: act.activation(out, a, F.Identity, bias=bias, scale=scale), ext, bank)
+
+    def scale(name, deps, out, a, k, bias=0.0, ext=()):
+        if name in ON_S:
+            lin(name, deps, out, a, k, bias, ext)
+        else:
+            ts(name, deps, out, a, k, A.mult, bias, A.add, ext)
 
     def fill(name, deps, out, k):
         op("V", name, deps, lambda: vec.memset(out, k))
@@ -96,48 +250,55 @@ def build(g, core, T, topo):
     def ld(n):
         return ("ld_" + n, 16)
 
-    def cut(buf, t, n):
-        return buf[:, t * n:(t + 1) * n]
+    def cut(buf, t, n, a=0, m=None):
+        return buf[:, t * n + a:t * n + (n if m is None else a + m)]
 
-    def own(buf, slot):
-        return buf[:, slot * 1024 + q * 256: slot * 1024 + q * 256 + 256]
-
-    def turned(ap):
-        return ap.indirect(T.turn[:, 0:16])
+    def own(buf, slot, a=0, m=256):
+        return cut(buf, 4 * slot + q, 256, a, m)
 
     def sel(z, i):
         return z[:, 15 - i:143 - i]
 
+    def shift(G, h, w):
+        return T[G + str(h)][:, 16 + 16 * (h - w):144 + 16 * (h - w)]
+
+    def listed(t, use, lo):
+        return T.pL2[:, 2 * use:2 * use + 2, lo, :] if KEYS[t] == 2 else T.pL2[:, 2 * use + lo // 8, 2 * (lo % 8):2 * (lo % 8) + 2, :]
+
+    def letters(n, t, table):
+        return [n + str(t) + p[1] for p in pieces(table[t])] if t >= 0 else []
+
     def ynames(t, a, b):
         out, u = [], 0
-        for j, n in enumerate(YCH[t]):
-            if u < b and u + n > a:
+        for j, c in enumerate(YCH[t].split()):
+            if u < b and u + 256 * int(c[1:]) > a:
                 out.append("Y%d_%d" % (t, j))
-            u += n
+            u += 256 * int(c[1:])
         return out
 
     def ygather(t):
         u = 0
-        for j, n in enumerate(YCH[t]):
-            copy("V" if j in YV[t] else "S", "Y%d_%d" % (t, j), ["fOff%d" % t], T.YG[:, t * 4096 + u * 256: t * 4096 + (u + n) * 256],
-                 T.frms[:, 0:NF].indirect(T.fOff[:, t * 256 + u * 16: t * 256 + (u + n) * 16]), [ld("frm")])
+        for j, c in enumerate(YCH[t].split()):
+            n = int(c[1:])
+            copy(c[0], "Y%d_%d" % (t, j), ["fOff%d" % t], cut(T.YG, t, 4096, u * 256, n * 256),
+                 T.frms[:, 0:NF].indirect(cut(T.fOff, t, 256, u * 16, n * 16)), [ld("frm")])
             u += n
 
     minex, minec = cut(T.XN, q, V), cut(T.CT, q, V)
-    for n, dst, src in (("x0", minex, T.x0[:]), ("sc", T.scs[:], T.sc0[:]), ("sc8", T.sc8[0:8, :], T.sc0[:]),
-                        ("th", T.ths[:, 0:1], T.th[:]), ("cas", minec, T.cas[:]), ("rol", T.rols[:], T.rol[:]), ("frm", T.frms[:], T.frm[:])):
-        op("Y", "ld_" + n, [], lambda n=n, dst=dst, src=src: g.sync.dma_start(dst, src).then_inc(T.sem["ld_" + n], 16))
+    into = {"x0": (minex, T.x0[:]), "sc": (T.scs[:], T.sc0[:]), "th": (T.ths[:, 0:1], T.th[:]),
+            "cas": (minec, T.cas[:]), "rol": (T.rols[:, 9:9 + NS], T.rol[:]), "end": (T.rols[:, 7:9], T.rol[:, NS - 2:NS]), "frm": (T.frms[:], T.frm[:])}
+    for n in LOADS:
+        op("Y", "ld_" + n, [], lambda n=n: g.sync.dma_start(*into[n]).then_inc(T.sem["ld_" + n], 16))
 
-    def xnames(t):
-        return ["xn%d" % t + "ab"[j] for j in range(len(PARTS[t]))] if t >= 0 else []
-
-    def ownx(t):
-        return (T.XN[:, q * V + t:(q + 1) * V:2], [], [ld("x0")]) if t < 2 else (own(T.XT, t - 1), xnames(t - 2), [])
-
-    def ownc(t, a=0, step=1):
+    def ownx(t, a=0, m=256):
         if t < 2:
-            return T.CN[:, t + 2 * a:V:2 * step], ["cs"]
-        return T.CH[:, (t - 2) * 1024 + q * 256 + a:(t - 2) * 1024 + q * 256 + 256:step], ["cn%d" % (t - 2)]
+            return T.XN[:, q * V + t + 2 * a:q * V + t + 2 * (a + m) - 1:2], [], [ld("x0")]
+        return own(T.XT, 4 - t, a, m), letters("xn", t - 2, FEATS), []
+
+    def ownc(t, a=0, m=256, step=1):
+        if t < 2:
+            return T.CN[:, t + 2 * a:t + 2 * (a + m) - 1:2 * step], ["cs"]
+        return T.CH[:, (t - 2) * 1024 + q * 256 + a:(t - 2) * 1024 + q * 256 + a + m:step], letters("cn", t - 2, CASTS)
 
     others = [T.cores[(q + k) % len(T.cores)] for k in range(1, len(T.cores))]
     eng = out_engines(topo, core, others)
@@ -161,241 +322,258 @@ def build(g, core, T, topo):
         for k in range(len(T.cores)):
             r = (q - k) % len(T.cores)
             came = [("ca%d_%d" % (t, r), len(eng))] if k else [("left0", 2 * len(eng))]
-            gcopy("cv%d" % t + "abcd"[k], dep, T.CT[:, r * V + (t - 1) % 2:(r + 1) * V:2],
-                  T.CH[:, (t - 1) * 1024 + r * 256:(t - 1) * 1024 + (r + 1) * 256], 256, came)
+            gcopy("cv%d" % t + "abcd"[k], dep, T.CT[:, r * V + (t - 1) % 2:(r + 1) * V:2], cut(T.CH, 4 * (t - 1) + r, 256), 256, came)
 
     op("G", "J", [], lambda: g.iota(T.J[:], [[1, 256]], 0, 0, allow_small_or_imprecise_dtypes=True))
     op("G", "pc", [], lambda: g.iota(T.pc[:, 0:1], [[1, 1]], 0, 1))
-    op("G", "iq", [], lambda: g.iota(T.iq[:], [[1, 16]], 0, 16))
     send("sx0", [], minex, others, eng, T.sem.xa0, [ld("x0")])
-    op("G", "J16", [], lambda: g.iota(T.J16[:], [[16, 8], [0, 16]], 0, 0, allow_small_or_imprecise_dtypes=True))
+    op("G", "J16", [], lambda: g.iota(T.J16[:], [[16, 10], [0, 16]], -16, 0, allow_small_or_imprecise_dtypes=True))
     op("G", "Jm", [], lambda: g.iota(T.Jm[:], [[0, 16], [1, 16]], 0, 0, allow_small_or_imprecise_dtypes=True))
     for j, m in enumerate((112, 15, 16)):
         ts("pa%d" % j, ["pc"], T.pa[:, j:j + 1], T.pc[:, 0:1], m, A.bitwise_and)
     copy("V", "pf", ["pa0", "pa1", "pa2"], T.pf[:, 0:3], T.pa[:, 0:3])
     copy("V", "pf3", ["pc"], T.pf[:, 3:4], T.pc[:, 0:1])
-    gp, lo1, bit4, pp, lo256, p16, bit, name0 = [T.pf[:, j:j + 1] for j in range(8)]
-    lin("pf5", ["pf3"], p16, pp, 16.0)
+    gp, lo1, bit4, pp, lo256, p16, bit, nobit4, lo128, nobit = [T.pf[:, j:j + 1] for j in range(10)]
+    lin("pf4", ["pf"], lo256, lo1, 256.0)
     lin("pf6", ["pf"], bit, bit4, 1.0 / 16)
-    lin("pf7", ["pf"], name0, lo1, 2.0, float(q * V))
-    ts("io2", ["iq"], T.io2[:], T.iq[:], 255, A.bitwise_and)
-    copy("V", "turn", ["io2"], T.turn[:], T.io2[:])
+    lin("pf8", ["pf"], lo128, lo1, 128.0)
+    lin("pf9", ["pf6"], nobit, bit, -1.0, 1.0)
     ts("Z1", ["J", "pf"], T.Z1[:], T.J[:, 0:144], gp, A.subtract, 15.0, A.is_equal)
     ts("Ib", ["J", "pf3"], T.Ib[:], T.J[:, 0:128], pp, A.is_equal)
-    ts("Z8", ["J", "pf5"], T.Z8[0:8, :], T.J[0:8, 0:144], T.pf[0:8, 5:6], A.subtract, 15.0, A.is_equal)
-    for n, src, k in (("Zk", "Z1", 4096.0), ("Zm", "Z1", -4096.0), ("Im", "Ib", -1.0), ("Ik", "Ib", 4096.0),
-                      ("Imk", "Ib", -2048.0), ("Ia", "Ib", 1024.0)):
-        lin(n, [src], T[n][:], T[src][:], k)
     ts("G1a", ["J", "pf3"], T.Ga[:], T.J[:, 0:160], pp, A.subtract, 16.0, A.is_equal)
     lin("G1", ["G1a", "pf6"], T.G1[:], T.Ga[:], bit)
-    lin("pf9", ["pf6"], T.pf[:, 9:10], bit, -1.0, 1.0)
-    lin("G0", ["G1a", "pf9"], T.G0[:], T.Ga[:], T.pf[:, 9:10])
-    ts("BD", ["J16", "pf"], T.BD[:], T.J16[:], gp, A.is_equal)
+    lin("G0", ["G1a", "pf9"], T.G0[:], T.Ga[:], nobit)
+    for n, src, k in (("Zk", "Z1", 256.0), ("Zm", "Z1", -256.0), ("Im", "Ib", -1.0), ("Ik", "Ib", 4096.0),
+                      ("Imk", "Ib", -2048.0), ("Ia", "Ib", 1024.0), ("Ih", "Ib", -2047.0), ("Ik2", "Ib", -1024.0), ("Ihalf", "Ib", 0.5),
+                      ("Gk0", "G0", 4096.0), ("Gk1", "G1", 4096.0)):
+        lin(n, [src], T[n][:], T[src][:], k)
+    ts("BD", ["J16", "pf"], T.BD[:], T.J16[:, 16:144], gp, A.is_equal, -256.0, A.mult)
+    ts("Gb", ["J16", "pf"], T.Gb[:], T.J16[:], gp, A.is_equal, 1.0 / 16, A.mult)
+    tt("Gc", ["Gb", "G1a"], T.Gc[:], T.Ga[:], T.Gb[:], A.subtract)
+    lin("Gm1", ["Gc", "pf"], T.Gm1[:], T.Gc[:], bit4)
+    lin("pf7", ["pf"], nobit4, bit4, -1.0, 16.0)
+    lin("Gm0", ["Gc", "pf7"], T.Gm0[:], T.Gc[:], nobit4)
     ts("AT", ["J"], T.AT[:], T.J[:, 0:32], 9.5, A.is_lt, 0.5, A.max)
-    fill("w", [], T.w[:], 1.0 / 512)
-    fill("seg0", [], T.seg[:], 0.0)
-    fill("seg", ["seg0"], T.seg[:, 0:256:16], 2.0 ** 25)
+    ts("PT", ["J"], T.PT[:], T.J[:, 0:32], 9.5, A.is_lt, 1024.0, A.mult)
+    fill("w", [], T.w[:], 128.0)
+    fill("wk", [], T.wk[:], 2048.0 + 2.0 * 2049 - 1.0 / 256)
     row = {}
-    for j, (n, k, width) in enumerate((("one", 1.0, 256), ("p256", 256.0, 256), ("m8th", -0.125, 128), ("magic", MAGIC, 128),
-                                       ("half", -255.0 / 512, 128))):
+    for j, (n, k, width) in enumerate((("one", 1.0, 256), ("m8th", -0.125, 128), ("magic", MAGIC, 128), ("kilo", -1024.0, 128), ("back", -MAGIC, 128))):
         row[n] = T.rows[0:1, j * 256:j * 256 + width]
         fill(n, [], row[n], k)
     ts("OH4", ["Jm", "pf"], T.OH[:, 0:256], T.Jm[:], lo1, A.is_equal)
     for j in (4, 5):
         gcopy("OH%d" % (j + 1), ["OH%d" % j], T.OH[:, 16 << j:32 << j], T.OH[:, 0:16 << j], 16 << j)
     for j in (1, 2, 3):
-        op("Y", "oh%d" % j, ["OH6"], lambda j=j: g.sync.dma_start(cut(T.OH, j, 1024), cut(T.OH, 0, 1024)).then_inc(T.sem.oh, 16), [ld("frm")])
-    lin("Wn0", ["J", "pf7"], T.W[:, 0:16], T.J[:, 0:16], 32.0, name0)
-    lin("Wn1", ["Wn0"], T.W[:, 32:48], T.W[:, 0:16], 1.0, 1.0)
-    copy("V", "thf", [], T.thf[:], T.ths[:, 0:1], [ld("th")])
+        gcopy("oh%d" % j, ["OH6"], cut(T.OH, j, 1024), cut(T.OH, 0, 1024), 1024)
+    ts("thf", [], T.thf[:], T.ths[:, 0:1], 2048.0, A.subtract, ext=[ld("th")])
     lin("thd", ["thf", "OH4"], T.thd[:], T.OH[:, 0:256], T.thf[:, 0:1])
-    mm("thm", ["thd", "BD"], [(T.pM[:, 0:256], T.BD[:], T.thd[:], True, True)])
-    lin("TH", ["thm"], T.TH[:], T.pM[:, 0:256], 4096.0, 128.5 * 4096)
-    lin("lim0", ["thm"], cut(T.lim, 0, 256), T.pM[:, 0:256], 4096.0, 4096.0)
+    mm("thm", ["thd", "BD"], ["pK1", (T.pK1[:, 0:256], T.BD[:], T.thd[:], True, True)])
+    copy("S", "TH", ["thm"], T.TH[:], T.pK1[:, 0:256], bank="pK1")
+    tt("seg0", ["TH"], T.seg[:, 1:256], T.pK1[:, 1:256], T.TH[:, 0:255], A.subtract, bank="pK1")
+    fill("seg", ["seg0"], T.seg[:, 0:256:16], 2.0 ** 25)
 
-    copy("V", "cs", [], T.CN[:], minec, [ld("cas")])
+    scale("cs", [], T.CN[:], minec, 1.0, ext=[ld("cas")])
     send_casts(0, [], minec, [ld("cas")])
-    ts("turn2", ["io2"], T.turn2[:], T.io2[:], 2.0, A.mult)
-    copy("V", "cOff0", ["turn2"], cut(T.cOff, 0, 256), minec.indirect(T.turn2[:, 0:16]), [ld("cas")])
     for p in range(2):
         copy("V", "eC%d" % p, [], cut(T.eC, p, 16), T.scs[:, p:32:2], [ld("sc")])
-        copy("V", "s8h%d" % p, [], T.sc8h[0:8, p * 256:(p + 1) * 256], T.sc8[0:8, p:V:2], [ld("sc8")])
-    mm("e0", ["s8h0", "s8h1", "Z8"], [(T.pB[:, 0:32], T.Z8[0:8, 15 - lo:143 - lo], T.sc8h[0:8, lo:V:16], lo == 0, lo == 15) for lo in range(16)])
-    copy("V", "eL", ["e0"], T.eL[:], T.pB[:, 0:32])
+    op("V", "eD", ["eC0", "eC1"], lambda: vec.transpose(T.eD[:], T.eC[:]))
+    mm("e0", ["eD", "G0", "G1"], ["pN"] + [(cut(T.pN, p, 16), shift("G", p, w), cut(T.eD, w, 16), w == 0, w == 1) for p in range(2) for w in range(2)])
+    ts("eL", ["e0"], T.eL[:], T.pN[:, 0:32], 1.0, A.add, bank="pN")
+    lin("W0", ["J"], T.W[:], T.J[:, 0:64], 0.0)
     for p in range(2):
-        lin("e1_%d" % p, ["eL"], T.W[:, p * 32 + 16:p * 32 + 32], T.pB[:, p * 16:p * 16 + 16], 1.0, 1.0)
-        copy("V", "fOff%d" % p, ["eC%d" % p], cut(T.fOff, p, 256), T.rols[:, 0:NS].indirect(cut(T.eC, p, 16)), [ld("rol")])
+        lin("e1_%d" % p, ["W0"], cut(T.W, p, 32, 16), cut(T.pN, p, 16), 1.0, 2.0, bank="pN")
+    mm("co0", ["Ib", "cs"], ["pL2"] + [(listed(0, 1, lo), T.Ib[:], ownc(0, lo, 256 - lo, 16)[0], True, True) for lo in range(16)])
+    copy("V", "cOff0", ["co0"], cut(T.cOff, 0, 256), T.pL2[:, 2:4, :, :], bank="pL2")
 
-    def prepare(t, free):
+    def frames(t, ts_):
+        for r in ts_:
+            lst, dep = (cut(T.eL, r, 16), ["eL"]) if r < 2 else (cut(T.zL, r - 2, 32, 16), ["zL%da" % (r - 2)])
+            scale("fJ%d" % r, dep, cut(T.fJ, r, 256), T.rols[:, 8:9 + NS].indirect(lst), 1.0, -2047.0 - r // 2, ext=[ld("rol"), ld("end")])
+        for r in ts_:
+            mm("ft%d" % r, ["fJ%d" % r, "Ib"], ["pL2"] + [(listed(r, r - t, lo), T.Ib[:], T.fJ[:, r * 256 + lo:(r + 1) * 256:16], True, True) for lo in range(16)])
+        ts("fOff%d" % t, [], T.fOff[:, t * 256:(t + len(ts_)) * 256], T.pL2[:, 0:2 * len(ts_), :, :], 2047.0 + t // 2, A.add, bank="pL2")
+
+    def prepare(t):
         s = str(t)
         x, xd, xe = ownx(t)
-        if "x3_" + s in ON_S:
-            lin("x3_" + s, xd, cut(T.x3, t, 256), x, 3.0, ext=xe)
-        else:
-            ts("x3_" + s, xd, cut(T.x3, t, 256), x, 3.0, A.mult, ext=xe)
-        lst, dep = (cut(T.eL, t, 16), "eL") if t < 2 else (T.zL[:, (t - 2) * 32 + 16:(t - 2) * 32 + 32], "zL%d" % (t - 2))
-        ts("fJ" + s, [dep], cut(T.fJ, t, 256), T.rols[:, 0:NS].indirect(lst), 2048.0, A.subtract, ext=[ld("rol")])
-        if t >= 2:
-            mm("ft" + s, ["fJ" + s, "Ib", "t2%d" % (t - 2)],
-               [(T.pM[:, 256 + 16 * lo:272 + 16 * lo], T.Ib[:], T.fJ[:, t * 256 + lo:(t + 1) * 256:16], True, True) for lo in range(16)])
-            ts("fOff" + s, ["ft" + s], cut(T.fOff, t, 256), T.pM[:, 256:512], 2048.0, A.add)
+        if t < RO - 1:
+            scale("x3_" + s, xd, cut(T.x3, t, 256), x, 3.0, ext=xe)
+        frames(t, [t])
+        c, cd = ownc(t)
         if t:
-            c, cd = ownc(t)
-            if "mh" + s in ON_S:
-                lin("mh" + s, cd, cut(T.mh, t, 256), c, 0.5, 1024.75)
-            else:
-                ts("mh" + s, cd, cut(T.mh, t, 256), c, 0.5, A.mult, 1024.75, A.add)
-            calls = []
+            scale("mh" + s, cd, cut(T.mh, t, 256), c, 0.5, 1024.75)
+            calls = ["pL2"]
             for lo in range(16):
-                o, m = T.pC[:, 256 + 16 * lo:272 + 16 * lo], T.mh[:, t * 256 + lo:(t + 1) * 256:16]
-                calls += [(o, T.Ia[:], ownc(t, lo, 16)[0], True, False), (o, T.Imk[:], m, False, False),
-                          (o, T.Im[:] if t % 2 else T.Ib[:], m, False, True)]
-            mm("co" + s, ["mh" + s, "Ia", "Imk", "Im", "Ib"] + cd + free, calls)
-            k = (-1.0, 1024.0 - 2049.0 * 1025) if t % 2 else (1.0, 2047.0 * 1025)
-            ts("cOff" + s, ["co" + s], cut(T.cOff, t, 256), T.pC[:, 256:512], k[0], A.mult, k[1], A.add)
+                o, m = listed(t, 1, lo), T.mh[:, t * 256 + lo:(t + 1) * 256:16]
+                calls += [(o, T.Ia[:], ownc(t, lo, 256 - lo, 16)[0], True, False)]
+                calls += [(o, T.Ih[:], m, False, True)] if t % 2 else [(o, T.Imk[:], m, False, False), (o, T.Im[:], m, False, True)]
+            mm("co" + s, ["mh" + s, "Ia", "Imk", "Im", "Ih"] + cd, calls)
+            k = (1.0, 2047.0 * 1025) if t % 2 else (-1.0, 1024.0 - 2049.0 * 1025)
+            ts("cOff" + s, ["co" + s], cut(T.cOff, t, 256), T.pL2[:, 2:4, :, :], k[0], A.mult, k[1], A.add, bank="pL2")
 
-    prepare(0, [])
-    prepare(1, [])
+    prepare(0)
+    prepare(1)
     ygather(0)
-    gcopy("xo", [], cut(T.XT, 0, 1024), T.XN[:, 1:4 * V:2], 1024, [ld("x0"), ("xa0", arrive)])
+    gcopy("xo", [], cut(T.XT, 3, 1024), T.XN[:, 1:4 * V:2], 1024, [ld("x0"), ("xa0", arrive)])
 
     for t in range(RO):
-        s, pv, n1, n2 = str(t), str(t - 1), str(t + 1), str(t + 2)
+        s, n1, n2 = str(t), str(t + 1), str(t + 2)
+        nS, spare = [0], ["pS0", "pS1"] + (["pK1", "pX"] if KEYS[t] == 1 else ["pX"])
         last = t == RO - 1
+        tab_x = letters("xn", t - 1, FEATS) + (["xo"] if t == 1 else [])
+        xa = [ld("x0")] + [("xa%d" % k, arrive * (FEATS[k - 1] if k else 1)) for k in range(t + 1)]
+        table = T.XT[:, (3 - t) * 1024:(5 - t) * 1024] if t else T.XN[:, 0:4 * V]
 
-        def prev(*names):
-            return [n + pv for n in names] if t else []
-        xme, xdep, xext = ownx(t)
-        cme, cdep = ownc(t)
-        tab_x = xnames(t - 1) + (["xo"] if t == 1 else [])
-        xa = [ld("x0")] + [("xa%d" % k, arrive * (len(PARTS[k - 1]) if k else 1)) for k in range(t + 1)]
-        pK, pX, pC, pM = T.pK[:, 0:256], T.pX[:, 0:256], T.pC[:, 0:256], T.pM[:, 0:256]
-        mm("k" + s, ["J", "Jm", "one", "p256"] + prev("scan", "rej"),
-           [(pK, T.rows[0:1, 0:128], T.J[0:1, :], True, False), (pK, T.Jm[0:1, 0:128], row["p256"], False, False)])
-        u, ks, nS = 0, [], 0
-        for ci, (who, n, ab) in enumerate(CHUNKS[t]):
-            a, b = t * 4096 + u * 256, t * 4096 + (u + n) * 256
-            cn = "%d_%d" % (t, ci)
-            ys = ynames(t, u, u + n)
-            gat = (T.XT[:, (t - 1) * 1024:(t + 1) * 1024] if t else T.XN[:, 0:4 * V]).indirect(T.cOff[:, a // 16:b // 16])
-            if who == "V":
-                tt("X" + cn, ["cOff" + s] + tab_x + ys, T.DD[:, a:b], gat, T.YG[:, a:b], A.subtract, xa)
-                src, dep = T.DD[:, a:b], "X" + cn
+        def keys(p, sp, h0, nh, t=t):
+            e, uw, bank = s + sp, 16 * nh, "pK%d" % p
+            pK = T[bank][:, 0:uw]
+            mm("k" + e, ["J", "one", "BD", "thd"], [bank, (pK, T.rows[0:1, 0:128], T.J[0:1, 16 * h0:16 * h0 + uw], True, False), (pK, T.BD[:], T.thd[:, 0:uw], False, False)])
+            u, ks = 0, []
+            for ci, c in enumerate(CHUNKS[t][p].split()):
+                n, cn = int(c[1:]), e + str(ci)
+                a, m = 256 * h0 + u * uw, n * uw
+                ys, dd, ab, yg = ynames(t, a, a + m), cut(T.DD, t, 4096, a, m), cut(T.AB, t, 4096, a, m), cut(T.YG, t, 4096, a, m)
+                gat = table.indirect(cut(T.cOff, t, 256, a // 16, m // 16))
+                unit = [(lo, a + (lo - u) * uw) for lo in range(u, u + n)]
+                if c[0] == "M":
+                    tt("X" + cn, ["cOff" + s] + tab_x + ys, dd, gat, yg, A.subtract, xa)
+                    op("S", "A" + cn, ["X" + cn], lambda ab=ab, dd=dd: act.activation(ab, dd, F.Abs))
+                elif c[0] == "V":
+                    tt("X" + cn, ["cOff" + s] + tab_x + ys, dd, gat, yg, A.subtract, xa)
+                    ts("A" + cn, ["X" + cn], ab, dd, 0.0, A.max, 2.0, A.mult)
+                    mm("kd" + cn, ["X" + cn, "Zm", "k" + e], [bank] + [(pK, sel(T.Zm, lo), cut(T.DD, t, 4096, b, uw), False, False) for lo, b in unit])
+                    ks.append("kd" + cn)
+                else:
+                    pS = spare[nS[0] % len(spare)]
+                    nS[0] += 1
+                    copy("S", "X" + cn, ["cOff" + s] + tab_x, dd, gat, xa)
+                    mm("my" + cn, ys + ["Im"], [pS, (T[pS][:, 0:m], T.Im[:], yg, True, False)])
+                    mm("mx" + cn, ["my" + cn, "X" + cn, "Ib"], [pS, (T[pS][:, 0:m], T.Ib[:], dd, False, True)])
+                    op("S", "A" + cn, ["mx" + cn], lambda ab=ab, src=T[pS][:, 0:m]: act.activation(ab, src, F.Abs), bank=pS)
+                mm("ka" + cn, ["A" + cn, "Zk", "k" + e] + (ks if u + n == 16 else []),
+                   [bank] + [(pK, sel(T.Zk, lo), cut(T.AB, t, 4096, b, uw), False, lo == 15) for lo, b in unit])
+                ks.append("ka" + cn)
+                u += n
+            rej = cut(T.rej, t, 256, 16 * h0, uw)
+            op("V", "scan" + e, ["seg"], lambda: vec.tensor_tensor_scan(cut(T.scan, t, 256, 16 * h0, uw), T.seg[:, 0:uw], pK, 0.0, A.add, A.min), bank=bank)
+            if t:
+                limit, dep = (T.c1[:, t:t + 1], ["c1_" + s]) if KEYS[t] == 2 else (T.pN[:, 128:129], [])
+                ts("rej" + e, ["fl" + s] + dep, rej, pK, T.fl[:, t:t + 1], A.add, limit, A.is_ge, bank=bank)
             else:
-                src = T["pS%d" % (nS % 2)][:, 0:b - a]
-                free = bank.get(nS % 2, [])
-                bank[nS % 2] = ["A" + cn]
-                nS += 1
-                copy("S", "X" + cn, ["cOff" + s] + tab_x, T.DD[:, a:b], gat, xa)
-                mm("my" + cn, ys + ["Im"] + free, [(src, T.Im[:], T.YG[:, a:b], True, False)])
-                mm("mx" + cn, ["my" + cn, "X" + cn, "Ib"], [(src, T.Ib[:], T.DD[:, a:b], False, True)])
-                dep = "mx" + cn
-            end = u + n == 16
-            unit = [(lo, slice(t * 4096 + lo * 256, t * 4096 + lo * 256 + 256)) for lo in range(u, u + n)]
-            if ab == "S":
-                op("S", "A" + cn, [dep], lambda a=a, b=b, src=src: act.activation(T.AB[:, a:b], src, F.Abs))
-            else:
-                ts("A" + cn, [dep], T.AB[:, a:b], src, 0.0, A.max, 2.0, A.mult)
-                mm("kd" + cn, [dep, "Zm", "k" + s], [(pK, sel(T.Zm, lo), T.DD[:, c], False, False) for lo, c in unit])
-                ks.append("kd" + cn)
-            mm("ka" + cn, ["A" + cn, "Zk", "k" + s] + (ks if end else []), [(pK, sel(T.Zk, lo), T.AB[:, c], False, lo == 15) for lo, c in unit])
-            ks.append("ka" + cn)
-            u += n
-        key = ks[-1]
-        rej, rejT = cut(T.rej, t, 256), cut(T.rejT, t, 256)
-        tt("rej" + s, [key, "lim" + s], rej, pK, cut(T.lim, t, 256), A.is_ge)
-        mm("n" + s, ["rej" + s, "Ib"] + (["fr" + s] if t else []),
-           [(T.pN[:, 0:16], T.Ib[:], T.rej[:, t * 256 + k:(t + 1) * 256:16], k == 0, k == 15) for k in range(16)])
-        op("V", "scan" + s, [key, "seg"], lambda t=t, pK=pK: vec.tensor_tensor_scan(cut(T.scan, t, 256), T.seg[:], pK, 0.0, A.add, A.min))
-        ts("pI" + s, ["scan" + s], cut(T.pI, t, 16), T.scan[:, t * 256 + 15:(t + 1) * 256:16], NF - 1, A.bitwise_and)
-        copy("V", "pL" + s, ["pI" + s], cut(T.pL, t, 16), cut(T.pI, t, 16))
-        copy("V", "nL" + s, ["n" + s], cut(T.nL, t, 16), T.pN[:, 0:16])
-        acc = None if last else T.rsum[:, t:t + 1]
-        op("S", "sg" + s, ["nL" + s], lambda t=t, acc=acc: act.activation(cut(T.sg, t, 16), T.pN[:, 0:16], F.Sign, bias=-9.5, accum_out=acc))
-        best = cut(T.pL, t, 16)
-        parts = PARTS[t]
-        for j, n in enumerate(parts):
-            a, p = sum(parts[:j]), s + "ab"[j]
-            cols, lists = slice(t * 256 + a, t * 256 + a + n), slice(t * 16 + a // 16, t * 16 + (a + n) // 16)
-            pv_ = (T.pS1 if j else T.pX)[:, 0:n]
-            xme = T.XN[:, q * V + t + 2 * a:q * V + t + 2 * (a + n) - 1:2] if t < 2 else T.XT[:, (t - 1) * 1024 + q * 256 + a:(t - 1) * 1024 + q * 256 + a + n]
-            mm("v" + p, ["m8th", "one", "Ib"] + xdep + (bank[1] if j else xnames(t - 1)[:1]),
-               [(pv_, row["m8th"], T.rows[0:1, 0:n], True, False)] + [(pv_, T.Ib[:], xme, False, False)] * 2, xext)
-            tt("h" + p, ["pL" + s, "x3_" + s], T.hh[:, cols], cut(T.YG, t, 4096).indirect(T.pL[:, lists]), T.x3[:, cols], A.subtract)
-            tt("q" + p, ["h" + p, "nL" + s, "AT"], T.qq[:, cols], T.AT[:, 0:32].indirect(T.nL[:, lists]), T.hh[:, cols], A.mult)
-            mm("vq" + p, ["v" + p, "q" + p, "Ib", "magic"],
-               [(pv_, T.Ib[:], T.qq[:, cols], False, False), (pv_, row["magic"], T.rows[0:1, 0:n], False, True)])
-            xdst = T.xout[:, 1:V:2] if last else T.XT[:, (t + 1) * 1024 + q * 256 + a:(t + 1) * 1024 + q * 256 + a + n]
-            op("S", "xn" + p, ["vq" + p] + (["xe2"] if last else []), lambda xdst=xdst, pv_=pv_: act.activation(xdst, pv_, F.Abs, bias=-MAGIC))
-            if j:
-                bank[1] = ["xn" + p]
+                ts("rej" + e, [], rej, pK, 256.0 * 2049, A.is_ge, bank=bank)
+            pN = T.pN[:, h0:h0 + nh]
+            mm("n" + e, ["rej" + e, "Ib"], ["pN"] + [(pN, T.Ib[:], T.rej[:, t * 256 + 16 * h0 + k:t * 256 + 16 * h0 + uw:16], k == 0, k == 15) for k in range(16)])
+            ts("pI" + e, ["scan" + e], cut(T.pI, t, 16, h0, nh), T.scan[:, t * 256 + 16 * h0 + 15:t * 256 + 16 * h0 + uw:16], 255, A.bitwise_and)
+            ts("pL" + e, ["pI" + e, "pf4", "pf8"], cut(T.pL, t, 16, h0, nh), cut(T.pI, t, 16, h0, nh), lo256 if nh == 16 else lo128, A.add, 240.0 * h0, A.add)
+            copy("V", "nL" + e, ["n" + e], cut(T.nL, t, 16, h0, nh), pN, bank="pN")
+            acc = None if last else T.rsum[:, 2 * t + p:2 * t + p + 1]
+            op("S", "sg" + e, [], lambda: act.activation(cut(T.sg, t, 16, h0, nh), pN, F.Sign, bias=-9.5, accum_out=acc), bank="pN")
+
+        def part(n, h0, nh):
+            return [n + s + p[1] for p in pieces(KEYS[t]) if p[2] < h0 + nh and p[2] + p[3] > h0]
+
+        def features(j, sp, h0, nh):
+            e, a, n = s + sp, 16 * h0, 16 * nh
+            bank = "pK1" if j else "pX" if KEYS[t] == 1 else "pK0"
+            pv = T[bank][:, 256:256 + n]
+            xme, xdep, xext = ownx(t, a, n)
+            hh, qq = cut(T.hh, t, 256, a, n), cut(T.qq, t, 256, a, n)
+            if last:
+                pu, ones = T.pK1[:, 0:n], T.rows[0:1, 0:n]
+                copy("S", "h" + e, part("pL", h0, nh), hh, cut(T.YG, t, 4096).indirect(cut(T.pL, t, 16, h0, nh)))
+                copy("S", "q" + e, part("nL", h0, nh) + ["PT"], qq, T.PT[:, 0:32].indirect(cut(T.nL, t, 16, h0, nh)))
+                mm("u" + e, ["Im"] + xdep, ["pK1", (pu, T.Im[:], xme, True, False)])
+                mm("v" + e, ["m8th", "one", "Ihalf"] + xdep, [bank, (pv, row["m8th"], ones, True, False), (pv, T.Ihalf[:], xme, False, False)])
+                mm("uh" + e, ["u" + e, "h" + e], ["pK1", (pu, T.Ib[:], hh, False, False)])
+                mm("vh" + e, ["v" + e, "h" + e, "magic", "back"],
+                   [bank, (pv, T.Ihalf[:], hh, False, False), (pv, row["magic"], ones, False, False), (pv, row["back"], ones, False, False)])
+                mm("uq" + e, ["uh" + e, "q" + e], ["pK1", (pu, T.Ib[:], qq, False, True)])
+                mm("vq" + e, ["vh" + e, "q" + e], [bank, (pv, T.Ib[:], qq, False, True)])
+                op("S", "xu" + e, [], lambda: act.activation(T.uu[:, a:a + n], pu, F.Abs, bias=-1024.0), bank="pK1")
+                tt("xn" + e, ["xu" + e, "xe2"], T.xout[:, 2 * a + 1:2 * (a + n):2], pv, T.uu[:, a:a + n], A.min, bank=bank)
+                op("Y", "st_x" + sp, ["xn" + e], lambda: g.sync.dma_start(T.yx[:, 2 * a:2 * (a + n)], T.xout[:, 2 * a:2 * (a + n)]).then_inc(T.sem.stored, 16))
+                return
+            mm("v" + e, ["m8th", "one", "Ib"] + xdep, [bank, (pv, row["m8th"], T.rows[0:1, 0:n], True, False)] + [(pv, T.Ib[:], xme, False, False)] * 2, xext)
+            tt("h" + e, part("pL", h0, nh) + ["x3_" + s], hh, cut(T.YG, t, 4096).indirect(cut(T.pL, t, 16, h0, nh)), cut(T.x3, t, 256, a, n), A.subtract)
+            tt("q" + e, ["h" + e, "AT"] + part("nL", h0, nh), qq, T.AT[:, 0:32].indirect(cut(T.nL, t, 16, h0, nh)), hh, A.mult)
+            mm("vq" + e, ["v" + e, "q" + e, "Ib", "magic"], [bank, (pv, T.Ib[:], qq, False, False), (pv, row["magic"], T.rows[0:1, 0:n], False, True)])
+            xdst = own(T.XT, 2 - t, a, n)
+            op("S", "xn" + e, [], lambda: act.activation(xdst, pv, F.Abs, bias=-MAGIC), bank=bank)
+            send("sx" + n1 + sp, ["xn" + e], xdst, others, eng, T.sem["xa" + n1])
+
+        def casts(j, sp, h0, nh, t=t):
+            e, a, n = s + sp, 16 * h0, 16 * nh
+            cme, cdep = ownc(t, a, n)
+            onehot = T.OH[:, 0:4096].indirect(cut(T.pL, t, 16, h0, nh))
+            tt("selc" + e, part("pL", h0, nh) + ["oh1", "oh2", "oh3"] + cdep, T.sel[:, t, 0, a:a + n], onehot, cme, A.mult)
+            tt("self" + e, part("pL", h0, nh) + ["oh1", "oh2", "oh3", "fJ" + s], T.sel[:, t, 1, :] if t < 2 else T.selF[:, t - 2:V:2], onehot, cut(T.fJ, t, 256), A.mult)
+            sg, sgd, pA = cut(T.sg, t, 16), part("sg", h0, nh), T.pN[:, 128:129]
             if not last:
-                send("sx" + n1 + "ab"[j], ["xn" + p], xdst, others, eng, T.sem["xa" + n1])
+                count = [(pA, T.w[:], T.rsum[:, 2 * t + p:2 * t + p + 1], p == 0, False) for p in range(KEYS[t])] + [(pA, T.w[0:1, :], T.wk[0:1, :], False, True)]
+                mm("a" + s, ["w", "wk"] + sgd, ["pN"] + count)
+            if t < 2:
+                sums = [(T.pN[:, 32:64], sel(T.Z1, lo), T.sel[:, t, :, lo:256:16], lo == 0, lo == 15) for lo in range(16)]
+                mm("b" + e, ["selc" + e, "self" + e, "Z1", "Ik"] + sgd, ["pN"] + sums[:15] + [(T.pN[:, 48:64], T.Ik[:], sg, False, False)] + sums[15:])
+                tt("zE" + e, ["e1_" + s], cut(T.zA, t, 32), T.pN[:, 32:64], cut(T.W, t, 32), A.max, bank="pN")
+                ts("zI" + e, ["zE" + e], T.zI[:, t, :, :], cut(T.zA, t, 32), NS - 1, A.bitwise_and)
+                copy("V", "zL" + e, ["zI" + e], cut(T.zL, t, 32), T.zI[:, t, :, :])
+            else:
+                bank, pc_ = ("pL2", T.pL2[:, 0, 0:2, :]) if last else ("pN", T.pN[:, 32:48])
+                mm("b" + e, ["selc" + e], [bank] + [(pc_, sel(T.Z1, lo), T.sel[:, t, 0, lo:256:16], lo == 0, lo == 15) for lo in range(16)])
+                copy("V", "zL" + e, [], cut(T.zL, t, 32, 0, 16), pc_, bank=bank)
+            if not last:
+                ts("fl" + n1, [], T.fl[:, t + 1:t + 2], pA, 2.0 ** 39 - 32768, A.add, 2.0 ** 39 + 524288, A.subtract, bank="pN")
+                if KEYS[t + 1] == 2:
+                    copy("S", "c1_" + n1, [], T.c1[:, t + 1:t + 2], pA, bank="pN")
+            b0, nb = h0 // 2, nh // 2
+            op("V", "rT" + e, part("rej", h0, nh), lambda: vec.transpose(T.rejT[:, t * 8 + b0:t * 8 + b0 + nb, :, :], cut(T.rej, t, 256, a, n)))
+            pM, pC = T.pM[:, b0:b0 + nb, :, :], T.pM[:, 8 + b0:8 + b0 + nb, :, :]
+            mm("m" + e, ["rT" + e, "Gm0", "Gm1"], ["pM"] + [(T.pM[:, b0:b0 + nb, h, :], shift("Gm", h, w), T.rejT[:, t * 8 + b0:t * 8 + b0 + nb, w, :], w == 0, w == 1)
+                                                           for h in range(2) for w in range(2)])
+            mk, t1 = cut(T.mk, t, 256, a, n), cut(T.t1, t, 256, a, n)
+            op("S", "mk" + e, [], lambda: act.activation(mk, pM, F.Sign, bias=-6.5), bank="pM")
+            bank, pC = ("pS1", T.pS1[:, 0:n]) if last else ("pM", pC)
+            calls = [(pC, T.Ib[:], cme, True, False), (pC, row["kilo"], T.rows[0:1, 0:n], False, False), (pC, T.Ik2[:], mk, False, True)]
+            if last:
+                mm("mb" + e, cdep, [bank] + calls[:2])
+            mm("mc" + e, ["mk" + e, "Ib", "Ik2", "one", "kilo"] + cdep + ["mb" + e] * last, [bank] + calls[2 * last:])
+            conv = ["cv" + s + k for k in "abcd"] if t else []
+            came = [] if t else [ld("cas")] + [("ca0_%d" % r, len(eng)) for r in range(len(T.cores)) if r != q]
+            tt("t1" + e, ["zL" + e, "mk" + e] + conv, t1, T.CT[:, 0:4 * V].indirect(cut(T.zL, t, 32, h0, nh)), mk, A.mult, came)
+            tt("cn" + e, ["t1" + e] + (["ce2"] if last else []), T.cout[:, 2 * a + 1:2 * (a + n):2] if last else own(T.CH, t, a, n), pC, t1, A.max, bank=bank)
+            if last:
+                op("Y", "st_c" + sp, ["cn" + e], lambda: g.sync.dma_start(T.yc[:, 2 * a:2 * (a + n)], T.cout[:, 2 * a:2 * (a + n)]).then_inc(T.sem.stored, 16))
+
+        for p in pieces(KEYS[t]):
+            keys(*p)
+        for p in pieces(FEATS[t]):
+            features(*p)
+        for p in pieces(CASTS[t]):
+            casts(*p)
+        if t == 1:
+            op("V", "eT1", ["zI0a", "zI1a"], lambda: vec.transpose(T.eT[:], T.zI[:, :, 1, :]))
+            copy("V", "eH1", ["eT1"], T.eH[:], T.eT[:])
+            mm("ef1", ["eH1", "G0", "G1"], ["pN"] + [(T.pN[:, 64 + p:96:2], shift("G", p, w), cut(T.eH, w, 16), w == 0, w == 1) for p in range(2) for w in range(2)])
+            copy("S", "eu1", [], T.eU[:], T.pN[:, 64:96], bank="pN")
         if last:
-            op("Y", "st_x", xnames(t) + ["xe2"], lambda: g.sync.dma_start(T.yx[:], T.xout[:]).then_inc(T.sem.stored, 16))
+            op("V", "sT3", letters("sg", 2, KEYS) + letters("sg", 3, KEYS), lambda: vec.transpose(T.sT[:], T.sg[:, 32:64]))
+            mm("be3", ["self2a", "self3a", "sT3", "Gk0", "Gk1"],
+               ["pS0"] + [(T.pS0[:, 0:32], sel(T.Z1, hi), cut(T.selF, hi, 32), hi == 0, False) for hi in range(16)]
+               + [(T.pS0[:, p:32:2], shift("Gk", p, w), cut(T.sT, w, 16), False, p + w == 2) for p in range(2) for w in range(2)])
+            tt("zE3a", ["eu1"], cut(T.zA, 3, 32), T.pS0[:, 0:32], T.eU[:], A.max, bank="pS0")
+            ts("zI3a", ["zE3a"], T.eT[:], cut(T.zA, 3, 32), NS - 1, A.bitwise_and)
+            scale("eo3", ["zI3a"], T.eout[:], T.eT[:], 1.0)
+            op("Y", "st_e", ["eo3"], lambda: g.sync.dma_start(T.ye[:], T.eout[:]).then_inc(T.sem.stored, 16))
         else:
             ygather(t + 1)
-        onehot = T.OH[:, 0:4096].indirect(best)
-        tt("selc" + s, ["pL" + s, "OH6"] + cdep, T.sel[:, t * 512:t * 512 + 256], onehot, cme, A.mult, [("oh", 48)])
-        tt("self" + s, ["pL" + s, "OH6", "fJ" + s], T.sel[:, t * 512 + 256:(t + 1) * 512], onehot, cut(T.fJ, t, 256), A.mult, [("oh", 48)])
-        scene, sdep, sg = T.zI[:, t * 32 + 16:(t + 1) * 32], "zI" + s, cut(T.sg, t, 16)
-        if last:
-            for n, out, a in (("bc", T.pB[:, 0:16], 0), ("be", T.pK[:, 256:272], 256)):
-                mm(n + s, ["selc" + s, "eo2"] if a == 0 else ["self" + s, "scan" + s, "rej" + s],
-                   [(out, sel(T.Z1, lo), T.sel[:, t * 512 + a + lo:t * 512 + a + 256:16], lo == 0, False) for lo in range(16)])
-                mm(n + "j" + s, [n + s, "sg" + s], [(out, T.Ik[:], sg, False, True)])
-            tt("zA" + s, ["bcj" + s, "Wc"], T.zc[:], T.pB[:, 0:16], T.Wc[:], A.min)
-            ts("zL" + s, ["zA" + s], T.zL[:, t * 32:t * 32 + 16], T.zc[:], 4096.0, A.add)
-            tt("zE" + s, ["bej" + s, "e1_" + s], T.zA[:, t * 32 + 16:(t + 1) * 32], T.pK[:, 256:272], T.W[:, 48:64], A.max)
-            ts("zI" + s, ["zE" + s], scene, T.zA[:, t * 32 + 16:(t + 1) * 32], NS - 1, A.bitwise_and)
-        else:
-            sums = [(T.pB[:, 0:32], sel(T.Z1, lo), T.sel[:, t * 512 + lo:(t + 1) * 512:16], lo == 0, lo == 15) for lo in range(16)]
-            jump = [(T.pB[:, 0:16], T.Imk[:], sg, False, False), (T.pB[:, 16:32], T.Ik[:], sg, False, False)]
-            mm("b" + s, ["selc" + s, "self" + s, "Z1", "sg" + s, "Ik", "Imk"] + (prev("zA") or ["eL", "e1_0", "e1_1"]), sums[:15] + jump + sums[15:])
-            tt("zA" + s, ["b" + s, "Wn%d" % (t & 1), "e1_" + s], cut(T.zA, t, 32), T.pB[:, 0:32], cut(T.W, t & 1, 32), A.max)
-            ts("zI" + s, ["zA" + s], cut(T.zI, t, 32), cut(T.zA, t, 32), NS - 1, A.bitwise_and)
-            copy("V", "zL" + s, ["zI" + s], cut(T.zL, t, 32), cut(T.zI, t, 32))
-        op("V", "rT" + s, ["rej" + s], lambda rej=rej, rejT=rejT: vec.transpose(rejT, rej))
-        calls = []
-        for hi in range(16):
-            for w in range(2):
-                blk, half = hi // 2, hi % 2
-                off = 16 + 16 * (half - w)
-                calls.append((T.pM[:, 16 * hi:16 * hi + 16], T["G%d" % half][:, off:off + 128],
-                              T.rejT[:, t * 256 + 32 * blk + 16 * w:t * 256 + 32 * blk + 16 * w + 16], w == 0, w == 1))
-        mm("m" + s, ["rT" + s, "G0", "G1"] + [["TH", "lim0"], ["fOff2"], ["fOff3"], ["t22"]][t], calls)
-        conv = ["cv" + s + k for k in "abcd"] if t else []
-        came = [] if t else [ld("cas")] + [("ca0_%d" % r, len(eng)) for r in range(len(T.cores)) if r != q]
-        table, conv = (T.CT[:, 0:4 * V + 256], conv + ["cc2"]) if last else (T.CT[:, 0:4 * V], conv)
-        tt("t1" + s, ["zL" + s] + conv + cdep, cut(T.t1, t, 256), table.indirect(T.zL[:, t * 32:t * 32 + 16]), cme, A.subtract, came)
-        tt("t2" + s, ["t1" + s, "m" + s] + prev("cn") + ([] if last else ["cOff" + n1]), pC, pM, cut(T.t1, t, 256), A.mult)
-        tt("cn" + s, ["t2" + s] + (["ce2"] if last else []), T.cout[:, 1:V:2] if last else own(T.CH, t), pC, cme, A.add)
-        if last:
-            op("Y", "st_c", ["cn" + s, "ce2"], lambda: g.sync.dma_start(T.yc[:], T.cout[:]).then_inc(T.sem.stored, 16))
-        else:
-            send_casts(t + 1, ["cn" + s], own(T.CH, t))
-            widen(t + 1, ["cn" + s, "t1" + s])
-            pA = T.pN[:, 128:129]
-            mm("a" + s, ["sg" + s, "w", "one", "half"],
-               [(pA, T.w[:], T.rsum[:, t:t + 1], True, False), (pA, row["half"], T.rows[0:1, 0:1], False, True)])
-            ts("fl" + n1, ["a" + s], T.fl[:, t:t + 1], pA, MAGIC, A.add, MAGIC, A.subtract)
-            ts("fr" + n1, ["fl" + n1], T.fr[:, t:t + 1], pA, T.fl[:, t:t + 1], A.subtract, 256.0 * 4096, A.mult)
-            lin("lim" + n1, ["fr" + n1, "TH"], cut(T.lim, t + 1, 256), T.TH[:], 1.0, T.fr[:, t:t + 1])
+            send_casts(t + 1, ["cn" + s + "a"], own(T.CH, t))
+            widen(t + 1, ["cn" + s + "a", "t1" + s + "a"])
         if t < 2:
-            ts("e1_" + n2, [sdep], T.W[:, t * 32 + 16:(t + 1) * 32], scene, 1.0, A.add)
-            prepare(t + 2, ["cn" + s])
-        else:
-            p = t & 1
-            ts("eH" + s, [sdep], cut(T.eH, p, 16), scene, 1.0, A.mult)
-            mm("ef" + s, ["eH" + s, "zA" + s, "Ib"],
-               [(T.pB[0:8, 256 + lo:512:16], T.Ib[:, lo:128:16], cut(T.eH, p, 16), True, True) for lo in range(16)])
-            copy("S", "eo" + s, ["ef" + s] + (["eo2"] if last else []), T.eout[0:8, p:V:2], T.pB[0:8, 256:512])
+            prepare(t + 2)
         if t == 2:
-            gcopy("xe2", xnames(2), T.xout[:, 0:V:2], own(T.XT, 3), 256)
-            gcopy("ce2", ["cn2"], T.cout[:, 0:V:2], own(T.CH, 2), 256)
-            gcopy("cc2", ["cn1"], T.CT[:, 4 * V:4 * V + 256], own(T.CH, 1), 256)
-            lin("Wc", ["Wn0"], T.Wc[:], T.W[:, 0:16], 0.5, -2048.0 - q * 256)
-    op("Y", "st_e", ["eo2", "eo3"], lambda: g.sync.dma_start(T.ye[:], T.eout[0:8, :]).then_inc(T.sem.stored, 16))
+            gcopy("xe2", letters("xn", 2, FEATS), T.xout[:, 0:V:2], own(T.XT, 0), 256)
+            gcopy("ce2", ["cn2a"], T.cout[:, 0:V:2], own(T.CH, 2), 256)
     return ops, sent[0]
 
 
@@ -425,7 +603,8 @@ def hand_on(g, core, rank_core, T, topo):
 
 def arrange(ops):
     order = {e: [n for n in ops if ops[n][0] == e] for e in "VSPGY"}
-    for e, (first, each, final) in (ORDER or {}).items():
+    order["Y"].sort(key=lambda n: STORES.index(n) if n in STORES else -1)
+    for e, (first, each, final) in ORDER.items():
         names = first.split()
         for r in range(RO):
             for tok in (final if r == RO - 1 else each).split():
@@ -470,7 +649,7 @@ def emit(g, T, ops, order, sent):
             if name in count:
                 ins.then_inc(T.sem[counter[e]], 1)
     g.wait_ge(T.sem.sent, sent)
-    g.sync.wait_ge(T.sem.stored, 48)
+    g.sync.wait_ge(T.sem.stored, 16 * len([n for n in ops if n.startswith("st_")]))
 
 
 def rank_program(g, core, T, topo):

from concourse.bass import DstId, RemoteDMATransfer
from concourse.mybir import AluOpType, ActivationFunctionType

V, NF, NS, RO = 512, 4096, 2048, 4
H, B, F4, I4, U2 = "float16", "bfloat16", "float32", "int32", "uint16"
MAGIC = 12582912.0


def sb(n, dt):
    return ("sbuf", [128, n], dt)


SCRATCH = {
    "XN": sb(4 * V, B), "XT": sb(4 * 1024, B), "CN": sb(V, H), "CH": sb(3 * 1024, H), "CT": sb(4 * V + 256, I4), "Wc": sb(16, F4), "zc": sb(16, F4),
    "frms": sb(NF, B), "rols": sb(NS + 16, I4), "selF": sb(V, H), "eU": sb(32, F4), "sT": sb(32, B), "Gk0": sb(160, B), "Gk1": sb(160, B), "scs": sb(32, I4), "sc8": sb(V, I4), "sc8h": sb(V, H), "ths": sb(4, I4), "thf": sb(1, F4),
    "YG": sb(RO * 4096, B), "DD": sb(RO * 4096, B), "AB": sb(RO * 4096, B),
    "fOff": sb(RO * 256, U2), "cOff": sb(RO * 256, U2), "fJ": sb(RO * 256, H), "mh": sb(RO * 256, H), "x3": sb(RO * 256, H),
    "turn": sb(16, U2), "scan": sb(RO * 256, I4), "rej": sb(RO * 256, B), "rejT": ("sbuf", [128, RO * 8, 2, 16], B),
    "hh": sb(RO * 256, H), "qq": sb(RO * 256, H), "t1": sb(RO * 256, H), "mk": sb(RO * 256, H), "sel": ("sbuf", [128, RO, 2, 256], H),
    "pI": sb(RO * 16, I4), "pL": sb(RO * 16, U2), "nL": sb(RO * 16, U2), "sg": sb(RO * 16, B),
    "W": sb(64, F4), "zA": sb(RO * 32, I4), "zI": ("sbuf", [128, 2, 2, 16], I4), "zL": sb(RO * 32, U2), "eL": sb(32, U2), "eC": sb(32, H), "eD": sb(32, H), "PT": sb(32, B), "Ihalf": sb(128, B), "uu": sb(256, H),
    "eH": sb(32, H), "eT": sb(32, I4), "rsum": sb(2 * RO, F4), "fl": sb(RO, F4), "c1": sb(RO, F4),
    "xout": sb(V, B), "cout": sb(V, F4), "eout": sb(32, F4),
    "J": sb(256, B), "J16": sb(160, B), "Gb": sb(160, B), "Gc": sb(160, B), "Ik2": sb(128, B), "Jm": sb(256, B), "pc": sb(4, I4), "pa": sb(4, I4), "pf": sb(12, F4), "Ga": sb(160, B),
    "iq": sb(16, I4), "io2": sb(16, I4), "Zk": sb(144, B),
    "Z1": sb(144, B), "Zm": sb(144, B), "Z8": sb(144, B), "G0": sb(160, B), "G1": sb(160, B), "Gm0": sb(160, B), "Gm1": sb(160, B),
    "BD": sb(128, B), "Ib": sb(128, B), "Im": sb(128, B), "Ik": sb(128, B), "Imk": sb(128, B), "Ih": sb(128, H),
    "Ia": sb(128, B), "w": sb(128, F4), "wk": sb(1, F4), "rows": sb(5 * 256, B), "seg": sb(256, F4), "OH": sb(4096, B),
    "thd": sb(256, H), "TH": sb(256, F4), "AT": sb(32, B),
    "pM": ("psum", [128, 16, 2, 16], F4), "pL2": ("psum", [128, 4, 16, 8], F4),
}
for n in ("pK0", "pK1", "pN", "pX", "pS0", "pS1"):
    SCRATCH[n] = ("psum", [128, 512], F4)
LOADS = ["x0", "sc", "th", "end", "cas", "rol", "frm"]
SEMAPHORES = (["cV", "cS", "cP", "cG", "sent", "left0", "stored"] + ["ld_" + n for n in LOADS]
              + ["handed"] + ["xa%d" % t for t in range(RO)] + ["ca%d_%d" % (t, r) for t in range(RO) for r in range(4)])

STORES = ["st_ca", "st_xa", "st_e"]
DIRECT = 1
KEYS = [1, 1, 1, 1]
FEATS = [2, 2, 2, 1]
CASTS = [1, 1, 1, 1]
CHUNKS = [["S2 S2 S2 S1 V4 V3 V1 V1"]] * 4
YCH = ["V4 V4 S4 S4"] + ["S3 S3 S3 S3 S2 V2"] * 3
ON_S = ["x3_2", "x3_3"]
ORDER = {
    "V": ("one pa2 pa0 m8th pa1 pf3 pf w Z1 G1a wk io2 magic Z8 turn AT Ib x3_1 s8h0 thf eC1 s8h1 BD cs x3_0 OH4 eC0 mh1 cOff0 eL fOff1 fOff0 seg0 fJ0 seg Y0_1 Y0_0",
          "X#a4 X#a5 A#a4 A#a5 X#a6 X#a7 mh#@1 fOff#@1 A#a6 A#a7 scan#a rej#a pI#a rT#a pL#a h#a nL#a h#b q#a q#b e1_#@1 self#a selc#a Y#_5@1 cOff#@1 zA#a zI#a fJ#@1 zL#a fl#@1 t1#a fJ#@2 cn#a",
          "X#a4 X#a5 A#a4 A#a5 X#a6 X#a7 A#a7 A#a6 rej#a scan#a rT#a pI#a pL#a nL#a selc#a self#a h#a zA#a q#a zE#a zL#a zI#a t1#a eT# cn#a eH#"),
    "S": ("pf5 Im pf6 Ia Ih Zm pf9 Ik G0 thd TH G1 Gm0 e1_0 Imk pf7 Wn0 Zk pf8 Wn1 Gm1 e1_1 Wc pf4 Y0_2 Y0_3",
          "X#a0 X#a1 A#a0 X#a3 X#a2 x3_#@1 A#a1 A#a2 A#a3 Y#_1@1 Y#_0@1 sg#a xn#a xn#b mk#a Y#_3@1 Y#_2@1 Y#_4@1",
          "X#a0 X#a1 A#a0 X#a2 A#a1 X#a3 A#a2 A#a3 sg#a mk#a xn#a eo#"),
    "P": ("e0 thm k0a co1 my0a0 my0a2 my0a3 my0a1",
          "ft#@1 mx#a0 kd#a4 mx#a1 ka#a0 kd#a5 mx#a3 ka#a4 mx#a2 ka#a5 ka#a1 kd#a7 kd#a6 ka#a2 ka#a6 ka#a3 ka#a7 v#b v#a n#a m#a vq#a vq#b co#@1 b#a a# my#a1@1 my#a2@1 my#a3@1 my#a0@1 k#a@1",
          "mx#a0 kd#a4 mx#a1 ka#a0 kd#a5 mx#a2 ka#a4 ka#a5 mx#a3 ka#a1 kd#a6 kd#a7 ka#a2 ka#a3 ka#a6 ka#a7 v#a n#a m#a bc#a bcj#a be#a bej#a vq#a ef#"),
    "G": ("pc J iq Jm J16 sx0 sc0 OH5 OH6 oh1 sd0 oh2 oh3 xo sx1a sx1b",
          "sc#@1 cv#a@1 cc#@1 xe# ce# cv#b@1 cv#c@1 cv#d@1 sx#a@2 sx#b@2", ""),
}


CHUNKS2 = [["S2 S2 S1 V2 M2 V3 M2 V1 V1"]] * 4
YCH2 = ["V4 V4 S4 S4"] + ["S4 S4 S4 S3 V1"] * 3
ORDER2 = dict({
    "V": ("m8th pf3 magic wk one pa0 pa1 pa2 pf G1a io2 Ib turn Z1 w Z8 OH4 s8h1 x3_0 thf BD eC1 cs s8h0 AT mh1 cOff0 x3_1 eL seg0 eC0 fOff1 fOff0 seg fJ0 Y0_1 Y0_0",
          "e1_#@1 X#a3 X#a4 A#a3 X#a5 X#a6 A#a5 fOff#@1 X#a7 X#a8 A#a7 A#a8 mh#@1 rej#a scan#a pI#a rT#a pL#a nL#a h#a q#a h#b q#b self#a selc#a fJ#@1 Y#_4@1 zA#a zI#a zL#a fl#@1 t1#a fJ#@2 cn#a cOff#@1",
          "X#a3 X#a5 A#a3 A#a5 X#a4 X#a6 X#a8 X#a7 A#a7 A#a8 rej#a scan#a rT#a pI#a pL#a nL#a selc#a self#a h#a q#a zA#a zE#a zL#a zI#a t1#a eT# cn#a eH#"),
    "S": ("pf5 pf6 pf7 Zk Wn0 Ih Ik G1 Imk pf9 Zm thd TH G0 Wc Gm0 Im pf8 Ia Wn1 e1_1 Gm1 e1_0 pf4 Y0_2 Y0_3",
          "x3_#@1 X#a0 X#a2 X#a1 A#a0 A#a1 A#a4 A#a2 A#a6 Y#_0@1 Y#_1@1 xn#a mk#a sg#a xn#b Y#_3@1 Y#_2@1",
          "X#a0 X#a2 X#a1 A#a0 A#a1 A#a2 A#a4 A#a6 sg#a mk#a xn#a eo#"),
    "P": ("thm e0 co1 k0a my0a2 my0a1 my0a0",
          "ft#@1 mx#a0 kd#a3 mx#a1 mx#a2 ka#a3 ka#a0 kd#a5 ka#a1 ka#a4 ka#a5 ka#a2 kd#a7 ka#a6 kd#a8 ka#a7 ka#a8 v#a n#a m#a vq#a v#b my#a0@1 vq#b a# b#a co#@1 my#a2@1 my#a1@1 k#a@1",
          "mx#a0 kd#a3 mx#a2 mx#a1 kd#a5 ka#a5 ka#a1 ka#a2 ka#a3 ka#a0 ka#a4 kd#a8 ka#a6 kd#a7 ka#a7 ka#a8 v#a n#a m#a bc#a bcj#a be#a bej#a vq#a ef#"),
})
YCH = ["V4 V4 S4 S4"] + ["S4 S3 S3 S3 V1 V1 V1"] * 3
ORDER.update({
    "V": ("magic m8th kilo w wk pf3 pa1 pa2 pa0 pf G1a one io2 Ib Z1 Z8 AT turn OH4 x3_0 thf s8h1 BD Gb Gc s8h0 eC0 cOff0 eC1 cs seg0 fOff0 fOff1 eL mh1 x3_1 fJ0 seg Y0_1 Y0_0",
          "X#a4 X#a5 A#a4 A#a5 X#a6 fOff#@1 X#a7 A#a6 A#a7 Y#_6@1 scan#a rej#a pI#a rT#a pL#a mh#@1 h#a nL#a h#b q#a q#b self#a selc#a Y#_5@1 Y#_4@1 zL#a zE#a fl#@1 zI#a fJ#@1 t1#a zS#@2 e1_#@2 cOff#@1 cn#a fJ#@2",
          "X#a4 X#a5 A#a4 X#a7 A#a5 A#a7 X#a6 A#a6 rej#a scan#a rT#a pI#a pL#a nL#a selc#a self#a h#a zL#a q#a zE#a t1#a zI#a eT# cn#a eH#"),
    "S": ("pf5 pf6 G1 pf8 pf9 Im pf7 Ik G0 thd Gm1 TH Zk pf4 Zm Ih Ik2 Imk Gm0 e1_1 e1_0 Ia Y0_2 Y0_3",
          "X#a0 X#a1 A#a0 X#a3 X#a2 A#a3 A#a1 A#a2 Y#_1@1 Y#_0@1 sg#a x3_#@1 mk#a xn#a xn#b Y#_3@1 Y#_2@1",
          "X#a0 X#a1 A#a0 X#a2 X#a3 A#a1 A#a2 A#a3 sg#a mk#a xn#a eo#"),
    "P": ("thm k0a e0 co1 my0a2 my0a0 my0a3 my0a1",
          "ft#@1 mx#a0 kd#a4 mx#a1 ka#a0 kd#a5 mx#a3 ka#a4 mx#a2 kd#a6 ka#a3 ka#a5 ka#a1 kd#a7 ka#a6 ka#a2 ka#a7 v#a v#b n#a m#a vq#a a# vq#b b#a mc#a co#@1 my#a3@1 my#a2@1 k#a@1 my#a1@1 my#a0@1",
          "mx#a0 kd#a4 mx#a1 ka#a0 kd#a5 mx#a2 ka#a4 kd#a7 mx#a3 ka#a5 ka#a1 ka#a2 kd#a6 ka#a6 ka#a3 ka#a7 v#a n#a m#a bc#a b#a mc#a vq#a ef#"),
})
CHUNKS = [["S2 S2 S2 V3 M1 V3 V2 V1"]] * 4
YCH = ["V4 V4 S4 S4"] + ["S4 S4 S3 S3 V1 V1"] * 3
ON_S = ["x3_2", "x3_3", "fJ1", "fJ2", "fJ3"]
ORDER.update({
    "V": ("magic m8th kilo w wk pf3 pa1 pa2 pa0 pf G1a one io2 Ib Z1 Z8 AT turn OH4 x3_0 thf s8h1 BD Gb Gc s8h0 eC0 cOff0 eC1 cs seg0 fOff0 fOff1 eL mh1 x3_1 fJ0 seg Y0_1 Y0_0",
          "X#a3 X#a4 A#a3 X#a5 X#a6 fOff#@1 A#a5 X#a7 A#a6 A#a7 mh#@1 scan#a rej#a pI#a pL#a rT#a h#a nL#a h#b q#a q#b self#a selc#a Y#_4@1 Y#_5@1 zE#a zL#a fl#@1 zI#a t1#a e1_#@2 zS#@2 cOff#@1 cn#a",
          "X#a3 X#a4 A#a3 X#a5 X#a6 A#a5 X#a7 A#a6 A#a7 rej#a scan#a rT#a pI#a pL#a nL#a selc#a self#a h#a zL#a q#a zE#a t1#a zI#a eT# cn#a eH#"),
    "S": ("pf5 pf6 G1 pf8 pf9 Im pf7 Ik G0 thd Gm1 TH Zk pf4 Zm Ih Ik2 Imk Gm0 e1_1 e1_0 Ia Y0_2 Y0_3",
          "X#a0 X#a1 A#a0 X#a2 A#a1 A#a4 A#a2 Y#_0@1 fJ#@1 Y#_1@1 sg#a mk#a xn#a xn#b Y#_2@1 Y#_3@1 fJ#@2 x3_#@1",
          "X#a0 X#a1 A#a0 X#a2 A#a1 A#a4 A#a2 mk#a sg#a xn#a eo#"),
    "P": ("thm k0a e0 co1 my0a0 my0a1 my0a2",
          "ft#@1 mx#a0 kd#a3 mx#a1 ka#a0 ka#a3 mx#a2 kd#a5 ka#a1 ka#a4 kd#a6 ka#a2 ka#a5 kd#a7 ka#a6 ka#a7 v#a v#b n#a k#a@1 m#a vq#a vq#b mc#a a# b#a co#@1 my#a0@1 my#a2@1 my#a1@1",
          "mx#a0 kd#a3 mx#a1 ka#a0 ka#a3 mx#a2 kd#a5 ka#a1 ka#a4 kd#a6 ka#a5 ka#a2 kd#a7 ka#a6 ka#a7 n#a m#a v#a bc#a b#a mc#a vq#a ef#"),
})
CHUNKS = [["S2 S2 S2 V3 M1 V3 V2 V1"]] * 3 + [["S2 S2 S2 S1 V3 V3 V2 V1"]]
ON_S = ["x3_2", "x3_3", "fJ0", "fJ1", "fJ2", "fJ3", "cs", "s8h0", "s8h1"]
ORDER.update({
    "V": ("magic pa2 pa0 pa1 pf3 pf Ib G1a w io2 Z1 one turn x3_0 Z8 thf OH4 m8th Gb BD cOff0 wk x3_1 Gc AT eC1 eC0 eL mh1 fOff0 kilo seg0 fOff1 seg Y0_1 Y0_0",
          "X#a3 X#a4 A#a3 X#a5 X#a6 fOff#@1 A#a5 X#a7 A#a6 A#a7 scan#a rej#a pI#a mh#@1 pL#a rT#a h#a nL#a h#b q#a q#b selc#a self#a Y#_4@1 Y#_5@1 zE#a zL#a fl#@1 zI#a t1#a e1_#@2 zS#@2 cOff#@1 cn#a",
          "X#a4 X#a5 A#a4 A#a5 X#a6 X#a7 A#a6 A#a7 rej#a scan#a rT#a pI#a pL#a nL#a selc#a self#a h#a zL#a q#a zE#a t1#a zI#a eT# cn#a eH#"),
    "S": ("pf5 pf6 pf8 pf4 pf7 Ih Ik Imk Ia Ik2 Zk s8h1 s8h0 thd pf9 cs G0 TH Zm Im Gm1 e1_0 e1_1 G1 fJ0 Gm0 Y0_2 Y0_3",
          "X#a0 X#a1 X#a2 A#a0 A#a1 A#a4 A#a2 fJ#@1 Y#_0@1 Y#_1@1 sg#a mk#a xn#a xn#b Y#_2@1 Y#_3@1 fJ#@2 x3_#@1",
          "X#a0 X#a1 A#a0 X#a2 X#a3 A#a1 A#a3 A#a2 mk#a sg#a xn#a eo#"),
    "P": ("e0 thm co1 my0a2 k0a my0a0 my0a1",
          "ft#@1 mx#a0 kd#a3 mx#a1 ka#a3 mx#a2 ka#a0 kd#a5 ka#a1 kd#a6 ka#a4 ka#a2 ka#a5 kd#a7 ka#a6 ka#a7 v#a n#a v#b m#a my#a0@1 vq#a vq#b a# mc#a b#a co#@1 my#a1@1 my#a2@1 k#a@1 my#a3@1",
          "mx#a0 kd#a4 mx#a1 ka#a0 kd#a5 ka#a4 mx#a2 mx#a3 ka#a5 ka#a1 kd#a6 kd#a7 ka#a3 ka#a6 ka#a2 ka#a7 v#a n#a m#a bc#a b#a mc#a vq#a ef#"),
})
KEYS = [2, 2, 2, 1]
CHUNKS = [["S4 S3 V5 V4", "S4 S3 V4 V3 V2"]] * 3 + [["S2 S2 S2 S1 V3 V3 V2 V1"]]
ON_S = ["x3_2", "x3_3", "cs", "s8h0", "s8h1"]
ORDER.update({
    "V": ("pa0 pa1 pa2 pf3 pf Ib io2 wk kilo OH4 thf w x3_1 magic Z8 AT Z1 G1a eC0 BD one m8th Gb turn x3_0 Gc eL eC1 mh1 fJ0 seg0 fJ1 fOff0 seg Y0_0 cOff0 Y0_1 fOff1",
          "X#a2 X#a3 A#a2 A#a3 X#b2 X#b3 rej#a fOff#@1 scan#a X#b4 pI#a A#b2 pL#a A#b3 nL#a h#a A#b4 q#a scan#b rej#b pI#b pL#b rT#a h#b nL#b mh#@1 q#b self#a selc#a Y#_4@1 Y#_5@1 zE#a zL#a fl#@1 zI#a t1#a zS#@2 e1_#@2 fJ#@2 cOff#@1 cn#a",
          "X#a4 X#a5 A#a4 A#a5 X#a6 X#a7 A#a6 A#a7 rej#a scan#a rT#a pI#a pL#a nL#a selc#a self#a h#a zL#a q#a zE#a t1#a zI#a eT# cn#a eH#"),
    "S": ("pf5 pf7 pf8 Ik2 pf6 Ia Imk pf9 s8h0 s8h1 Im thd cs pf4 TH G0 Zm e1_1 Zk Gm1 Ik Gm0 G1 Ih e1_0 Y0_3 Y0_2",
          "x3_#@1 X#a0 X#a1 A#a0 A#a1 X#b0 X#b1 A#b0 A#b1 Y#_0@1 sg#a xn#a Y#_1@1 sg#b xn#b mk#a Y#_2@1 c1_#@1 Y#_3@1",
          "X#a0 X#a1 A#a0 X#a2 X#a3 A#a1 A#a3 A#a2 mk#a sg#a xn#a eo#"),
    "P": ("e0 thm k0a ft0 co0 my0a0 ft1 my0a1 k0b my0b0",
          "ft#@1 mx#a0 kd#a2 mx#a1 kd#a3 ka#a2 ka#a0 ka#a1 ka#a3 my#b1 mx#b0 kd#b2 mx#b1 kd#b3 n#a ka#b0 ka#b2 ka#b1 ka#b3 kd#b4 ka#b4 v#a vq#a n#b m#a my#a0@1 v#b vq#b k#a@1 a# b#a co#@1 mc#a my#a3@1 my#b0@1 k#b@1 my#a1@1 my#a2@1",
          "mx#a0 kd#a4 mx#a1 ka#a0 kd#a5 ka#a4 mx#a2 mx#a3 ka#a5 ka#a1 kd#a6 kd#a7 ka#a3 ka#a6 ka#a2 ka#a7 v#a n#a m#a bc#a b#a mc#a vq#a ef#"),
})
YCH = ["V4 V4 S4 S4"] + ["S4 S3 S3 S3 V1 V2"] * 3
ORDER.update({
    "V": ("pa0 pa2 pa1 pf3 pf w Ib kilo io2 Z8 turn wk G1a m8th Gb OH4 x3_0 thf BD eC0 Gc Z1 one x3_1 eL eC1 magic AT fJ0 seg0 fJ1 seg fOff0 mh1 cOff0 Y0_0 Y0_1 fOff1",
          "X#a2 X#a3 A#a2 A#a3 fOff#@1 X#b2 X#b3 rej#a scan#a X#b4 pI#a A#b2 pL#a A#b3 A#b4 h#a nL#a q#a scan#b rej#b pI#b mh#@1 pL#b rT#a h#b nL#b q#b selc#a self#a Y#_5@1 Y#_4@1 zE#a zL#a fl#@1 zI#a t1#a zS#@2 e1_#@2 cOff#@1 fJ#@2 cn#a",
          "X#a4 X#a5 A#a4 A#a5 X#a6 X#a7 A#a6 A#a7 rej#a scan#a pI#a rT#a pL#a nL#a selc#a self#a h#a zL#a q#a zE#a t1#a zI#a eT# cn#a eH#"),
    "S": ("pf5 pf8 pf7 pf6 Ia Ih pf9 Ik s8h0 s8h1 Im Imk thd cs Ik2 TH G1 pf4 G0 e1_0 Gm0 Gm1 Zk Zm e1_1 Y0_2 Y0_3",
          "x3_#@1 X#a0 X#a1 A#a0 A#a1 X#b0 X#b1 A#b0 A#b1 Y#_0@1 sg#a xn#a Y#_1@1 sg#b xn#b mk#a Y#_2@1 Y#_3@1 c1_#@1",
          "X#a0 X#a1 A#a0 X#a2 X#a3 A#a1 A#a3 A#a2 sg#a mk#a xn#a eo#"),
    "P": ("e0 thm ft0 co0 k0b my0b0 ft1 k0a my0a0 my0a1",
          "ft#@1 mx#a0 kd#a2 mx#a1 kd#a3 my#b1 ka#a2 ka#a0 ka#a1 ka#a3 mx#b0 kd#b2 mx#b1 kd#b3 n#a kd#b4 ka#b0 ka#b2 ka#b1 ka#b3 ka#b4 v#a vq#a n#b m#a v#b vq#b k#a@1 a# b#a co#@1 mc#a my#a1@1 my#a0@1 my#a3@1 my#b0@1 my#a2@1 k#b@1",
          "mx#a0 kd#a4 mx#a1 ka#a0 kd#a5 ka#a4 mx#a2 mx#a3 ka#a5 kd#a6 ka#a1 kd#a7 ka#a3 ka#a6 ka#a2 ka#a7 n#a v#a m#a bc#a b#a mc#a vq#a ef#"),
})
ON_S = ["cs"]
ORDER.update({
    "V": ("pa0 pa2 pa1 pf3 pf w Ib G1a kilo wk eC0 eC1 m8th eD Gb OH4 x3_0 thf BD Gc Z1 one x3_1 eL magic back AT PT fJ0 seg0 fJ1 seg fOff0 mh1 Y0_0 cOff0 Y0_1 fOff1",
          "X#a2 X#a3 A#a2 A#a3 fOff#@1 X#b2 X#b3 rej#a scan#a X#b4 pI#a A#b2 pL#a A#b3 A#b4 h#a nL#a q#a scan#b rej#b pI#b mh#@1 pL#b rT#a h#b nL#b q#b selc#a self#a Y#_5@1 Y#_4@1 zE#a zL#a fl#@1 zI#a c1_#@1 t1#a zS#@2 e1_#@2 cOff#@1 fJ#@2 cn#a x3_#@1",
          "X#a4 X#a5 A#a4 A#a5 X#a6 X#a7 A#a6 A#a7 rej#a scan#a pI#a rT#a pL#a nL#a selc#a self#a zL#a zE#a t1#a zI#a xn#a eT# cn#a eH#"),
    "S": ("pf8 pf7 pf6 pf9 G1 G0 Ia Ih Ik Im Imk thd cs Ik2 TH pf4 e1_0 Gm0 Gm1 Zk Zm e1_1 Ihalf Y0_2 Y0_3",
          "X#a0 X#a1 A#a0 A#a1 X#b0 X#b1 A#b0 A#b1 Y#_0@1 sg#a xn#a Y#_1@1 sg#b xn#b mk#a Y#_2@1 Y#_3@1",
          "X#a0 X#a1 A#a0 X#a2 X#a3 A#a1 A#a3 A#a2 h#a sg#a q#a mk#a xu#a eo#"),
    "P": ("e0 thm ft0 co0 k0b my0b0 ft1 k0a my0a0 my0a1",
          "ft#@1 mx#a0 kd#a2 mx#a1 kd#a3 my#b1 ka#a2 ka#a0 ka#a1 ka#a3 mx#b0 kd#b2 mx#b1 kd#b3 n#a kd#b4 ka#b0 ka#b2 ka#b1 ka#b3 ka#b4 v#a vq#a n#b m#a v#b vq#b k#a@1 a# b#a co#@1 mc#a my#a1@1 my#a0@1 my#a3@1 my#b0@1 my#a2@1 k#b@1",
          "mx#a0 kd#a4 mx#a1 ka#a0 kd#a5 ka#a4 mx#a2 mx#a3 ka#a5 kd#a6 ka#a1 kd#a7 ka#a3 ka#a6 ka#a2 ka#a7 u#a n#a v#a m#a bc#a uh#a vh#a b#a uq#a vq#a mc#a ef#"),
    "G": ("pc J Jm J16 sx0 sc0 OH5 OH6 oh1 sd0 oh2 oh3 xo sx1a sx1b",
          "sc#@1 cv#a@1 xe# ce# cv#b@1 cv#c@1 cv#d@1 sx#a@2 sx#b@2", ""),
})
ORDER.update({
    "V": ("kilo m8th pa2 pa0 pa1 pf magic wk pf3 Ib G1a eC0 thf PT AT x3_0 w eC1 Z1 back x3_1 OH4 eD one Gb eL BD mh1 Gc fJ0 seg0 fJ1 seg fOff0 Y0_0 cOff0 Y0_1 fOff1",
          "X#a2 X#a3 A#a2 A#a3 X#b2 X#b3 rej#a fOff#@1 scan#a A#b3 pI#a A#b2 pL#a X#b4 h#a nL#a A#b4 q#a x3_#@1 scan#b rej#b pI#b rT#a pL#b mh#@1 h#b nL#b q#b selc#a self#a Y#_5@1 zL#a zE#a Y#_4@1 zI#a fl#@1 t1#a zS#@2 c1_#@1 e1_#@2 cOff#@1 fJ#@2 cn#a",
          "X#a4 X#a5 A#a4 A#a5 X#a6 A#a6 X#a7 A#a7 scan#a rej#a pI#a pL#a rT#a selc#a nL#a self#a zL#a t1#a zE#a zI#a eT# xn#a eH# cn#a"),
    "S": ("pf6 pf7 pf4 pf9 Ik G1 G0 Ih Im Ik2 cs thd Imk Zm TH Ihalf Gm1 Zk pf8 Gm0 e1_0 Ia e1_1 Y0_3 Y0_2",
          "X#a0 X#a1 A#a0 A#a1 X#b0 X#b1 A#b0 A#b1 Y#_0@1 sg#a xn#a Y#_1@1 sg#b xn#b Y#_2@1 mk#a Y#_3@1",
          "X#a1 X#a3 X#a0 X#a2 A#a0 A#a1 A#a2 A#a3 h#a sg#a mk#a q#a xu#a eo#"),
    "P": ("e0 thm ft0 co0 ft1 my0a1 my0a0 my0b0 k0a k0b",
          "ft#@1 mx#a0 kd#a2 mx#a1 kd#a3 ka#a0 ka#a2 my#b1 ka#a1 ka#a3 mx#b0 kd#b2 mx#b1 kd#b3 n#a ka#b0 ka#b3 ka#b1 kd#b4 ka#b2 ka#b4 v#a vq#a n#b m#a v#b vq#b k#a@1 a# b#a co#@1 mc#a my#a1@1 my#a0@1 my#b0@1 my#a2@1 k#b@1 my#a3@1",
          "mx#a1 mx#a3 kd#a4 mx#a0 kd#a5 ka#a4 mx#a2 ka#a5 ka#a0 kd#a6 ka#a1 ka#a6 ka#a2 kd#a7 ka#a3 ka#a7 v#a u#a n#a m#a bc#a uh#a b#a uq#a vh#a vq#a mc#a ef#"),
})
ON_S = ["cs", "x3_2", "fJ2", "fJ3", "eo3"]
CHUNKS = [["S4 S3 V5 V4", "S4 S3 V5 V4"]] * 3 + [["S2 S2 S2 S1 V3 V3 V2 V1"]]
ORDER.update({
    "V": ("back magic one pf3 w pa0 pa1 Ib pa2 wk pf G1a Z1 kilo OH4 x3_1 eC0 AT eC1 Gb m8th eD thf x3_0 BD Gc eL PT cOff0 fJ0 fJ1 seg0 mh1 seg fOff0 Y0_0 Y0_1",
          "X#a2 X#a3 A#a2 A#a3 eT#@-1 X#b2 eH#@-1 X#b3 fOff#@1 rej#a scan#a A#b2 pI#a A#b3 pL#a nL#a h#a q#a scan#b rej#b pI#b mh#@1 pL#b rT#a h#b nL#b q#b selc#a self#a Y#_4@1 zE#a fl#@1 zI#a Y#_5@1 zL#a cOff#@1 t1#a cn#a",
          "X#a4 X#a5 A#a4 A#a5 X#a6 A#a6 X#a7 A#a7 scan#a rej#a pI#a pL#a rT#a selc#a nL#a self#a zL#a sT# t1#a zE#a cn#a zI#a xn#a"),
    "S": ("Ia Imk Ik pf6 Ik2 pf9 G1 Ih G0 pf8 cs Zm Zk thd pf7 Gm1 TH Im W0 e1_0 Gm0 Ihalf pf4 e1_1 Y0_3 Y0_2",
          "X#a0 X#a1 A#a0 A#a1 eu#@-1 X#b0 X#b1 A#b0 A#b1 Y#_0@1 sg#a x3_#@1 xn#a Y#_1@1 sg#b xn#b Y#_2@1 mk#a Y#_3@1 c1_#@1 fJ#@2",
          "X#a3 X#a1 X#a0 X#a2 A#a3 A#a0 A#a1 A#a2 Gk0 Gk1 h#a sg#a mk#a q#a xu#a eo#"),
    "P": ("e0 co0 thm k0a ft0 ft1 k0b my0b0 my0a1 my0a0",
          "ft#@1 mx#a0 kd#a2 mx#a1 kd#a3 ka#a0 ef#@-1 ka#a2 ka#a1 my#b1 ka#a3 mx#b0 kd#b2 mx#b1 kd#b3 n#a ka#b0 ka#b1 ka#b2 ka#b3 v#a vq#a n#b v#b m#a my#a0@1 vq#b a# b#a co#@1 mc#a my#a3@1 k#b@1 my#a2@1 my#b0@1 k#a@1 my#a1@1",
          "mx#a3 mx#a1 kd#a4 mx#a0 kd#a5 ka#a4 mx#a2 ka#a3 ka#a5 ka#a0 kd#a6 ka#a1 ka#a6 ka#a2 kd#a7 ka#a7 u#a v#a n#a m#a b#a uh#a mc#a be# uq#a vh#a vq#a"),
})
ORDER.update({
    "V": ("m8th w pa1 pa0 pa2 pf3 pf Ib AT PT G1a kilo Z1 one eC0 eC1 Gb eD thf BD back OH4 Gc wk mh1 eL cOff0 magic x3_0 fJ0 fJ1 seg0 fOff0 x3_1 seg Y0_0 fOff1 Y0_1",
          "eT#@-1 X#a2 eH#@-1 X#a3 A#a2 A#a3 X#b2 X#b3 fOff#@1 rej#a scan#a A#b3 pI#a A#b2 pL#a nL#a h#a mh#@1 q#a scan#b rej#b pI#b pL#b rT#a h#b nL#b q#b selc#a self#a Y#_5@1 zE#a fl#@1 zI#a zL#a Y#_4@1 t1#a cOff#@1 cn#a",
          "X#a4 X#a5 A#a4 A#a5 X#a6 X#a7 A#a6 A#a7 scan#a rej#a pI#a rT#a pL#a selc#a nL#a self#a zL#a sT# t1#a cn#a zE#a xn#a zI#a"),
    "S": ("pf6 pf9 Im G1 Zk G0 cs W0 pf7 Ik thd Imk pf4 Gm0 Gm1 pf8 TH Zm e1_1 e1_0 Ik2 Ih Ia Ihalf Y0_3 Y0_2",
          "X#a0 X#a1 A#a0 eu#@-1 A#a1 X#b0 X#b1 A#b0 A#b1 Y#_0@1 sg#a x3_#@1 xn#a Y#_1@1 sg#b xn#b mk#a Y#_2@1 Y#_3@1 fJ#@2 c1_#@1",
          "X#a3 X#a1 X#a0 X#a2 A#a0 A#a3 A#a1 A#a2 Gk0 Gk1 h#a sg#a mk#a q#a xu#a eo#"),
    "P": ("e0 co0 k0a thm ft0 ft1 my0a1 my0a0 my0b0 k0b",
          "ft#@1 mx#a0 ef#@-1 kd#a2 mx#a1 kd#a3 ka#a0 ka#a2 my#b1 ka#a1 ka#a3 mx#b0 kd#b2 mx#b1 kd#b3 n#a ka#b0 ka#b1 ka#b2 ka#b3 v#a vq#a n#b m#a v#b my#a1@1 vq#b a# b#a co#@1 mc#a my#b0@1 k#a@1 my#a0@1 my#a3@1 my#a2@1 k#b@1",
          "mx#a3 kd#a4 mx#a1 mx#a0 kd#a5 ka#a4 mx#a2 ka#a5 ka#a0 kd#a6 ka#a3 ka#a1 kd#a7 ka#a6 ka#a2 ka#a7 v#a u#a mb#a n#a m#a b#a uh#a mc#a be# vh#a uq#a vq#a"),
})
ORDER.update({
    "V": ("kilo one pa1 pa0 pa2 wk pf m8th pf3 Z1 back G1a w Ib OH4 magic thf eC1 eC0 Gb eD AT Gc BD x3_0 eL x3_1 PT mh1 cOff0 fJ0 fJ1 seg0 fOff0 seg Y0_0 Y0_1 fOff1",
          "eT#@-1 X#a2 X#a3 A#a2 eH#@-1 A#a3 X#b2 X#b3 rej#a fOff#@1 scan#a A#b3 pI#a A#b2 pL#a nL#a h#a q#a scan#b rej#b pI#b pL#b rT#a h#b nL#b mh#@1 q#b selc#a self#a Y#_5@1 zE#a zI#a Y#_4@1 zL#a fl#@1 t1#a cOff#@1 cn#a",
          "X#a4 X#a5 A#a4 A#a5 X#a6 A#a6 X#a7 A#a7 scan#a rej#a pI#a pL#a rT#a selc#a nL#a self#a zL#a sT# t1#a cn#a xn#a zE#a zI#a"),
    "S": ("W0 pf6 pf7 Zm pf9 pf8 G0 Ik2 G1 cs Imk thd Zk Ihalf e1_1 Im Ih TH e1_0 Gm1 Gm0 Ik Ia pf4 Y0_2 Y0_3",
          "X#a0 X#a1 A#a0 A#a1 X#b0 X#b1 eu#@-1 A#b0 A#b1 Y#_0@1 sg#a x3_#@1 xn#a Y#_1@1 sg#b xn#b mk#a Y#_2@1 Y#_3@1 c1_#@1 fJ#@2",
          "X#a1 X#a3 X#a0 A#a3 X#a2 A#a0 A#a1 A#a2 Gk1 Gk0 h#a mk#a sg#a q#a xu#a eo#"),
    "P": ("e0 co0 thm ft0 k0b my0a0 ft1 my0b0 my0a1 k0a",
          "ft#@1 mx#a0 kd#a2 mx#a1 kd#a3 my#b1 ka#a2 ka#a1 ef#@-1 ka#a0 ka#a3 mx#b0 kd#b2 mx#b1 kd#b3 n#a ka#b0 ka#b1 ka#b2 ka#b3 v#a vq#a n#b m#a my#a1@1 v#b vq#b a# b#a co#@1 mc#a my#b0@1 k#b@1 my#a2@1 my#a0@1 my#a3@1 k#a@1",
          "mx#a1 mx#a3 kd#a4 mx#a0 kd#a5 ka#a3 ka#a4 mx#a2 ka#a5 ka#a0 kd#a6 ka#a1 ka#a6 ka#a2 kd#a7 ka#a7 v#a mb#a u#a n#a m#a b#a uh#a vh#a uq#a mc#a vq#a be#"),
})


def pieces(n):
    return [(j, "ab"[j], 16 // n * j, 16 // n) for j in range(n)]


def build(g, core, T, topo):
    A, F = AluOpType, ActivationFunctionType
    q = T.rank_of(core)
    vec, act, pe = g.vector, g.scalar, g.tensor
    ops, turn = {}, {}

    def op(eng, name, deps, fn, ext=(), bank=None):
        assert name not in ops
        deps = list(deps)
        if bank:
            who, now, before = turn.get(bank, (eng, [], []))
            turn[bank] = (eng, now + [name], before) if who == eng else (eng, [name], now)
            deps += turn[bank][2]
        ops[name] = (eng, fn, deps, list(ext))

    def mm(name, deps, calls, ext=()):
        op("P", name, deps, lambda: [pe.matmul(*c) for c in calls[1:]][-1], ext, calls[0])

    def copy(eng, name, deps, out, src, ext=(), bank=None):
        op(eng, name, deps, (lambda: act.activation(out, src, F.Copy)) if eng == "S" else (lambda: vec.tensor_copy(out, src)), ext, bank)

    def gcopy(name, deps, out, src, n, ext=()):
        op("G", name, deps, lambda: g.affine_select(out, src, [[0, n]], A.is_ge, 0.0, 0, 0), ext)

    def tt(name, deps, out, a, b, alu, ext=(), bank=None):
        op("V", name, deps, lambda: vec.tensor_tensor(out, a, b, alu), ext, bank)

    def ts(name, deps, out, a, s1, o1, s2=None, o2=None, ext=(), bank=None):
        if o2 is None:
            op("V", name, deps, lambda: vec.tensor_scalar(out, a, s1, None, o1), ext, bank)
        else:
            op("V", name, deps, lambda: vec.tensor_scalar(out, a, s1, s2, o1, o2), ext, bank)

    def lin(name, deps, out, a, scale, bias=0.0, ext=(), bank=None):
        op("S", name, deps, lambda: act.activation(out, a, F.Identity, bias=bias, scale=scale), ext, bank)

    def scale(name, deps, out, a, k, bias=0.0, ext=()):
        if name in ON_S:
            lin(name, deps, out, a, k, bias, ext)
        else:
            ts(name, deps, out, a, k, A.mult, bias, A.add, ext)

    def fill(name, deps, out, k):
        op("V", name, deps, lambda: vec.memset(out, k))

    def ld(n):
        return ("ld_" + n, 16)

    def cut(buf, t, n, a=0, m=None):
        return buf[:, t * n + a:t * n + (n if m is None else a + m)]

    def own(buf, slot, a=0, m=256):
        return cut(buf, 4 * slot + q, 256, a, m)

    def sel(z, i):
        return z[:, 15 - i:143 - i]

    def shift(G, h, w):
        return T[G + str(h)][:, 16 + 16 * (h - w):144 + 16 * (h - w)]

    def listed(t, use, lo):
        return T.pL2[:, 2 * use:2 * use + 2, lo, :] if KEYS[t] == 2 else T.pL2[:, 2 * use + lo // 8, 2 * (lo % 8):2 * (lo % 8) + 2, :]

    def letters(n, t, table):
        return [n + str(t) + p[1] for p in pieces(table[t])] if t >= 0 else []

    def ynames(t, a, b):
        out, u = [], 0
        for j, c in enumerate(YCH[t].split()):
            if u < b and u + 256 * int(c[1:]) > a:
                out.append("Y%d_%d" % (t, j))
            u += 256 * int(c[1:])
        return out

    def ygather(t):
        u = 0
        for j, c in enumerate(YCH[t].split()):
            n = int(c[1:])
            copy(c[0], "Y%d_%d" % (t, j), ["fOff%d" % t], cut(T.YG, t, 4096, u * 256, n * 256),
                 T.frms[:, 0:NF].indirect(cut(T.fOff, t, 256, u * 16, n * 16)), [ld("frm")])
            u += n

    minex, minec = cut(T.XN, q, V), cut(T.CT, q, V)
    into = {"x0": (minex, T.x0[:]), "sc": (T.scs[:], T.sc0[:]), "th": (T.ths[:, 0:1], T.th[:]),
            "cas": (minec, T.cas[:]), "rol": (T.rols[:, 9:9 + NS], T.rol[:]), "end": (T.rols[:, 7:9], T.rol[:, NS - 2:NS]), "frm": (T.frms[:], T.frm[:])}
    for n in LOADS:
        op("Y", "ld_" + n, [], lambda n=n: g.sync.dma_start(*into[n]).then_inc(T.sem["ld_" + n], 16))

    def ownx(t, a=0, m=256):
        if t < 2:
            return T.XN[:, q * V + t + 2 * a:q * V + t + 2 * (a + m) - 1:2], [], [ld("x0")]
        return own(T.XT, 4 - t, a, m), letters("xn", t - 2, FEATS), []

    def ownc(t, a=0, m=256, step=1):
        if t < 2:
            return T.CN[:, t + 2 * a:t + 2 * (a + m) - 1:2 * step], ["cs"]
        return T.CH[:, (t - 2) * 1024 + q * 256 + a:(t - 2) * 1024 + q * 256 + a + m:step], letters("cn", t - 2, CASTS)

    others = [T.cores[(q + k) % len(T.cores)] for k in range(1, len(T.cores))]
    eng = out_engines(topo, core, others)
    arrive = len(eng) * len(others)
    sent = [0]

    def send(name, dep, part, dsts, engs, sem, ext=()):
        first = name in ("sc0", "sd0")
        sent[0] += 0 if first else len(engs)
        op("G", name, dep, lambda: write(g, topo, part, dsts, engs, sem, T.sem.left0 if first else T.sem.sent), ext)

    def send_casts(t, dep, part, ext=()):
        if t:
            send("sc%d" % t, dep, part, others, eng, T.sem["ca%d_%d" % (t, q)], ext)
        else:
            h = helper(topo, core)
            send("sc0", dep, part, [h], [e for e in topo.engines(core, h) if e not in eng], T.sem.handed, ext)
            send("sd0", dep, part, others[:DIRECT], eng, T.sem["ca0_%d" % q], list(ext) + [("sent", len(eng))])

    def widen(t, dep):
        for k in range(len(T.cores)):
            r = (q - k) % len(T.cores)
            came = [("ca%d_%d" % (t, r), len(eng))] if k else [("left0", 2 * len(eng))]
            gcopy("cv%d" % t + "abcd"[k], dep, T.CT[:, r * V + (t - 1) % 2:(r + 1) * V:2], cut(T.CH, 4 * (t - 1) + r, 256), 256, came)

    op("G", "J", [], lambda: g.iota(T.J[:], [[1, 256]], 0, 0, allow_small_or_imprecise_dtypes=True))
    op("G", "pc", [], lambda: g.iota(T.pc[:, 0:1], [[1, 1]], 0, 1))
    send("sx0", [], minex, others, eng, T.sem.xa0, [ld("x0")])
    op("G", "J16", [], lambda: g.iota(T.J16[:], [[16, 10], [0, 16]], -16, 0, allow_small_or_imprecise_dtypes=True))
    op("G", "Jm", [], lambda: g.iota(T.Jm[:], [[0, 16], [1, 16]], 0, 0, allow_small_or_imprecise_dtypes=True))
    for j, m in enumerate((112, 15, 16)):
        ts("pa%d" % j, ["pc"], T.pa[:, j:j + 1], T.pc[:, 0:1], m, A.bitwise_and)
    copy("V", "pf", ["pa0", "pa1", "pa2"], T.pf[:, 0:3], T.pa[:, 0:3])
    copy("V", "pf3", ["pc"], T.pf[:, 3:4], T.pc[:, 0:1])
    gp, lo1, bit4, pp, lo256, p16, bit, nobit4, lo128, nobit = [T.pf[:, j:j + 1] for j in range(10)]
    lin("pf4", ["pf"], lo256, lo1, 256.0)
    lin("pf6", ["pf"], bit, bit4, 1.0 / 16)
    lin("pf8", ["pf"], lo128, lo1, 128.0)
    lin("pf9", ["pf6"], nobit, bit, -1.0, 1.0)
    ts("Z1", ["J", "pf"], T.Z1[:], T.J[:, 0:144], gp, A.subtract, 15.0, A.is_equal)
    ts("Ib", ["J", "pf3"], T.Ib[:], T.J[:, 0:128], pp, A.is_equal)
    ts("G1a", ["J", "pf3"], T.Ga[:], T.J[:, 0:160], pp, A.subtract, 16.0, A.is_equal)
    lin("G1", ["G1a", "pf6"], T.G1[:], T.Ga[:], bit)
    lin("G0", ["G1a", "pf9"], T.G0[:], T.Ga[:], nobit)
    for n, src, k in (("Zk", "Z1", 256.0), ("Zm", "Z1", -256.0), ("Im", "Ib", -1.0), ("Ik", "Ib", 4096.0),
                      ("Imk", "Ib", -2048.0), ("Ia", "Ib", 1024.0), ("Ih", "Ib", -2047.0), ("Ik2", "Ib", -1024.0), ("Ihalf", "Ib", 0.5),
                      ("Gk0", "G0", 4096.0), ("Gk1", "G1", 4096.0)):
        lin(n, [src], T[n][:], T[src][:], k)
    ts("BD", ["J16", "pf"], T.BD[:], T.J16[:, 16:144], gp, A.is_equal, -256.0, A.mult)
    ts("Gb", ["J16", "pf"], T.Gb[:], T.J16[:], gp, A.is_equal, 1.0 / 16, A.mult)
    tt("Gc", ["Gb", "G1a"], T.Gc[:], T.Ga[:], T.Gb[:], A.subtract)
    lin("Gm1", ["Gc", "pf"], T.Gm1[:], T.Gc[:], bit4)
    lin("pf7", ["pf"], nobit4, bit4, -1.0, 16.0)
    lin("Gm0", ["Gc", "pf7"], T.Gm0[:], T.Gc[:], nobit4)
    ts("AT", ["J"], T.AT[:], T.J[:, 0:32], 9.5, A.is_lt, 0.5, A.max)
    ts("PT", ["J"], T.PT[:], T.J[:, 0:32], 9.5, A.is_lt, 1024.0, A.mult)
    fill("w", [], T.w[:], 128.0)
    fill("wk", [], T.wk[:], 2048.0 + 2.0 * 2049 - 1.0 / 256)
    row = {}
    for j, (n, k, width) in enumerate((("one", 1.0, 256), ("m8th", -0.125, 128), ("magic", MAGIC, 128), ("kilo", -1024.0, 128), ("back", -MAGIC, 128))):
        row[n] = T.rows[0:1, j * 256:j * 256 + width]
        fill(n, [], row[n], k)
    ts("OH4", ["Jm", "pf"], T.OH[:, 0:256], T.Jm[:], lo1, A.is_equal)
    for j in (4, 5):
        gcopy("OH%d" % (j + 1), ["OH%d" % j], T.OH[:, 16 << j:32 << j], T.OH[:, 0:16 << j], 16 << j)
    for j in (1, 2, 3):
        gcopy("oh%d" % j, ["OH6"], cut(T.OH, j, 1024), cut(T.OH, 0, 1024), 1024)
    ts("thf", [], T.thf[:], T.ths[:, 0:1], 2048.0, A.subtract, ext=[ld("th")])
    lin("thd", ["thf", "OH4"], T.thd[:], T.OH[:, 0:256], T.thf[:, 0:1])
    mm("thm", ["thd", "BD"], ["pK1", (T.pK1[:, 0:256], T.BD[:], T.thd[:], True, True)])
    copy("S", "TH", ["thm"], T.TH[:], T.pK1[:, 0:256], bank="pK1")
    tt("seg0", ["TH"], T.seg[:, 1:256], T.pK1[:, 1:256], T.TH[:, 0:255], A.subtract, bank="pK1")
    fill("seg", ["seg0"], T.seg[:, 0:256:16], 2.0 ** 25)

    scale("cs", [], T.CN[:], minec, 1.0, ext=[ld("cas")])
    send_casts(0, [], minec, [ld("cas")])
    for p in range(2):
        copy("V", "eC%d" % p, [], cut(T.eC, p, 16), T.scs[:, p:32:2], [ld("sc")])
    op("V", "eD", ["eC0", "eC1"], lambda: vec.transpose(T.eD[:], T.eC[:]))
    mm("e0", ["eD", "G0", "G1"], ["pN"] + [(cut(T.pN, p, 16), shift("G", p, w), cut(T.eD, w, 16), w == 0, w == 1) for p in range(2) for w in range(2)])
    ts("eL", ["e0"], T.eL[:], T.pN[:, 0:32], 1.0, A.add, bank="pN")
    lin("W0", ["J"], T.W[:], T.J[:, 0:64], 0.0)
    for p in range(2):
        lin("e1_%d" % p, ["W0"], cut(T.W, p, 32, 16), cut(T.pN, p, 16), 1.0, 2.0, bank="pN")
    mm("co0", ["Ib", "cs"], ["pL2"] + [(listed(0, 1, lo), T.Ib[:], ownc(0, lo, 256 - lo, 16)[0], True, True) for lo in range(16)])
    copy("V", "cOff0", ["co0"], cut(T.cOff, 0, 256), T.pL2[:, 2:4, :, :], bank="pL2")

    def frames(t, ts_):
        for r in ts_:
            lst, dep = (cut(T.eL, r, 16), ["eL"]) if r < 2 else (cut(T.zL, r - 2, 32, 16), ["zL%da" % (r - 2)])
            scale("fJ%d" % r, dep, cut(T.fJ, r, 256), T.rols[:, 8:9 + NS].indirect(lst), 1.0, -2047.0 - r // 2, ext=[ld("rol"), ld("end")])
        for r in ts_:
            mm("ft%d" % r, ["fJ%d" % r, "Ib"], ["pL2"] + [(listed(r, r - t, lo), T.Ib[:], T.fJ[:, r * 256 + lo:(r + 1) * 256:16], True, True) for lo in range(16)])
        ts("fOff%d" % t, [], T.fOff[:, t * 256:(t + len(ts_)) * 256], T.pL2[:, 0:2 * len(ts_), :, :], 2047.0 + t // 2, A.add, bank="pL2")

    def prepare(t):
        s = str(t)
        x, xd, xe = ownx(t)
        if t < RO - 1:
            scale("x3_" + s, xd, cut(T.x3, t, 256), x, 3.0, ext=xe)
        frames(t, [t])
        c, cd = ownc(t)
        if t:
            scale("mh" + s, cd, cut(T.mh, t, 256), c, 0.5, 1024.75)
            calls = ["pL2"]
            for lo in range(16):
                o, m = listed(t, 1, lo), T.mh[:, t * 256 + lo:(t + 1) * 256:16]
                calls += [(o, T.Ia[:], ownc(t, lo, 256 - lo, 16)[0], True, False)]
                calls += [(o, T.Ih[:], m, False, True)] if t % 2 else [(o, T.Imk[:], m, False, False), (o, T.Im[:], m, False, True)]
            mm("co" + s, ["mh" + s, "Ia", "Imk", "Im", "Ih"] + cd, calls)
            k = (1.0, 2047.0 * 1025) if t % 2 else (-1.0, 1024.0 - 2049.0 * 1025)
            ts("cOff" + s, ["co" + s], cut(T.cOff, t, 256), T.pL2[:, 2:4, :, :], k[0], A.mult, k[1], A.add, bank="pL2")

    prepare(0)
    prepare(1)
    ygather(0)
    gcopy("xo", [], cut(T.XT, 3, 1024), T.XN[:, 1:4 * V:2], 1024, [ld("x0"), ("xa0", arrive)])

    for t in range(RO):
        s, n1, n2 = str(t), str(t + 1), str(t + 2)
        nS, spare = [0], ["pS0", "pS1"] + (["pK1", "pX"] if KEYS[t] == 1 else ["pX"])
        last = t == RO - 1
        tab_x = letters("xn", t - 1, FEATS) + (["xo"] if t == 1 else [])
        xa = [ld("x0")] + [("xa%d" % k, arrive * (FEATS[k - 1] if k else 1)) for k in range(t + 1)]
        table = T.XT[:, (3 - t) * 1024:(5 - t) * 1024] if t else T.XN[:, 0:4 * V]

        def keys(p, sp, h0, nh, t=t):
            e, uw, bank = s + sp, 16 * nh, "pK%d" % p
            pK = T[bank][:, 0:uw]
            mm("k" + e, ["J", "one", "BD", "thd"], [bank, (pK, T.rows[0:1, 0:128], T.J[0:1, 16 * h0:16 * h0 + uw], True, False), (pK, T.BD[:], T.thd[:, 0:uw], False, False)])
            u, ks = 0, []
            for ci, c in enumerate(CHUNKS[t][p].split()):
                n, cn = int(c[1:]), e + str(ci)
                a, m = 256 * h0 + u * uw, n * uw
                ys, dd, ab, yg = ynames(t, a, a + m), cut(T.DD, t, 4096, a, m), cut(T.AB, t, 4096, a, m), cut(T.YG, t, 4096, a, m)
                gat = table.indirect(cut(T.cOff, t, 256, a // 16, m // 16))
                unit = [(lo, a + (lo - u) * uw) for lo in range(u, u + n)]
                if c[0] == "M":
                    tt("X" + cn, ["cOff" + s] + tab_x + ys, dd, gat, yg, A.subtract, xa)
                    op("S", "A" + cn, ["X" + cn], lambda ab=ab, dd=dd: act.activation(ab, dd, F.Abs))
                elif c[0] == "V":
                    tt("X" + cn, ["cOff" + s] + tab_x + ys, dd, gat, yg, A.subtract, xa)
                    ts("A" + cn, ["X" + cn], ab, dd, 0.0, A.max, 2.0, A.mult)
                    mm("kd" + cn, ["X" + cn, "Zm", "k" + e], [bank] + [(pK, sel(T.Zm, lo), cut(T.DD, t, 4096, b, uw), False, False) for lo, b in unit])
                    ks.append("kd" + cn)
                else:
                    pS = spare[nS[0] % len(spare)]
                    nS[0] += 1
                    copy("S", "X" + cn, ["cOff" + s] + tab_x, dd, gat, xa)
                    mm("my" + cn, ys + ["Im"], [pS, (T[pS][:, 0:m], T.Im[:], yg, True, False)])
                    mm("mx" + cn, ["my" + cn, "X" + cn, "Ib"], [pS, (T[pS][:, 0:m], T.Ib[:], dd, False, True)])
                    op("S", "A" + cn, ["mx" + cn], lambda ab=ab, src=T[pS][:, 0:m]: act.activation(ab, src, F.Abs), bank=pS)
                mm("ka" + cn, ["A" + cn, "Zk", "k" + e] + (ks if u + n == 16 else []),
                   [bank] + [(pK, sel(T.Zk, lo), cut(T.AB, t, 4096, b, uw), False, lo == 15) for lo, b in unit])
                ks.append("ka" + cn)
                u += n
            rej = cut(T.rej, t, 256, 16 * h0, uw)
            op("V", "scan" + e, ["seg"], lambda: vec.tensor_tensor_scan(cut(T.scan, t, 256, 16 * h0, uw), T.seg[:, 0:uw], pK, 0.0, A.add, A.min), bank=bank)
            if t:
                limit, dep = (T.c1[:, t:t + 1], ["c1_" + s]) if KEYS[t] == 2 else (T.pN[:, 128:129], [])
                ts("rej" + e, ["fl" + s] + dep, rej, pK, T.fl[:, t:t + 1], A.add, limit, A.is_ge, bank=bank)
            else:
                ts("rej" + e, [], rej, pK, 256.0 * 2049, A.is_ge, bank=bank)
            pN = T.pN[:, h0:h0 + nh]
            mm("n" + e, ["rej" + e, "Ib"], ["pN"] + [(pN, T.Ib[:], T.rej[:, t * 256 + 16 * h0 + k:t * 256 + 16 * h0 + uw:16], k == 0, k == 15) for k in range(16)])
            ts("pI" + e, ["scan" + e], cut(T.pI, t, 16, h0, nh), T.scan[:, t * 256 + 16 * h0 + 15:t * 256 + 16 * h0 + uw:16], 255, A.bitwise_and)
            ts("pL" + e, ["pI" + e, "pf4", "pf8"], cut(T.pL, t, 16, h0, nh), cut(T.pI, t, 16, h0, nh), lo256 if nh == 16 else lo128, A.add, 240.0 * h0, A.add)
            copy("V", "nL" + e, ["n" + e], cut(T.nL, t, 16, h0, nh), pN, bank="pN")
            acc = None if last else T.rsum[:, 2 * t + p:2 * t + p + 1]
            op("S", "sg" + e, [], lambda: act.activation(cut(T.sg, t, 16, h0, nh), pN, F.Sign, bias=-9.5, accum_out=acc), bank="pN")

        def part(n, h0, nh):
            return [n + s + p[1] for p in pieces(KEYS[t]) if p[2] < h0 + nh and p[2] + p[3] > h0]

        def features(j, sp, h0, nh):
            e, a, n = s + sp, 16 * h0, 16 * nh
            bank = "pK1" if j else "pX" if KEYS[t] == 1 else "pK0"
            pv = T[bank][:, 256:256 + n]
            xme, xdep, xext = ownx(t, a, n)
            hh, qq = cut(T.hh, t, 256, a, n), cut(T.qq, t, 256, a, n)
            if last:
                pu, ones = T.pK1[:, 0:n], T.rows[0:1, 0:n]
                copy("S", "h" + e, part("pL", h0, nh), hh, cut(T.YG, t, 4096).indirect(cut(T.pL, t, 16, h0, nh)))
                copy("S", "q" + e, part("nL", h0, nh) + ["PT"], qq, T.PT[:, 0:32].indirect(cut(T.nL, t, 16, h0, nh)))
                mm("u" + e, ["Im"] + xdep, ["pK1", (pu, T.Im[:], xme, True, False)])
                mm("v" + e, ["m8th", "one", "Ihalf"] + xdep, [bank, (pv, row["m8th"], ones, True, False), (pv, T.Ihalf[:], xme, False, False)])
                mm("uh" + e, ["u" + e, "h" + e], ["pK1", (pu, T.Ib[:], hh, False, False)])
                mm("vh" + e, ["v" + e, "h" + e, "magic", "back"],
                   [bank, (pv, T.Ihalf[:], hh, False, False), (pv, row["magic"], ones, False, False), (pv, row["back"], ones, False, False)])
                mm("uq" + e, ["uh" + e, "q" + e], ["pK1", (pu, T.Ib[:], qq, False, True)])
                mm("vq" + e, ["vh" + e, "q" + e], [bank, (pv, T.Ib[:], qq, False, True)])
                op("S", "xu" + e, [], lambda: act.activation(T.uu[:, a:a + n], pu, F.Abs, bias=-1024.0), bank="pK1")
                tt("xn" + e, ["xu" + e, "xe2"], T.xout[:, 2 * a + 1:2 * (a + n):2], pv, T.uu[:, a:a + n], A.min, bank=bank)
                op("Y", "st_x" + sp, ["xn" + e], lambda: g.sync.dma_start(T.yx[:, 2 * a:2 * (a + n)], T.xout[:, 2 * a:2 * (a + n)]).then_inc(T.sem.stored, 16))
                return
            mm("v" + e, ["m8th", "one", "Ib"] + xdep, [bank, (pv, row["m8th"], T.rows[0:1, 0:n], True, False)] + [(pv, T.Ib[:], xme, False, False)] * 2, xext)
            tt("h" + e, part("pL", h0, nh) + ["x3_" + s], hh, cut(T.YG, t, 4096).indirect(cut(T.pL, t, 16, h0, nh)), cut(T.x3, t, 256, a, n), A.subtract)
            tt("q" + e, ["h" + e, "AT"] + part("nL", h0, nh), qq, T.AT[:, 0:32].indirect(cut(T.nL, t, 16, h0, nh)), hh, A.mult)
            mm("vq" + e, ["v" + e, "q" + e, "Ib", "magic"], [bank, (pv, T.Ib[:], qq, False, False), (pv, row["magic"], T.rows[0:1, 0:n], False, True)])
            xdst = own(T.XT, 2 - t, a, n)
            op("S", "xn" + e, [], lambda: act.activation(xdst, pv, F.Abs, bias=-MAGIC), bank=bank)
            send("sx" + n1 + sp, ["xn" + e], xdst, others, eng, T.sem["xa" + n1])

        def casts(j, sp, h0, nh, t=t):
            e, a, n = s + sp, 16 * h0, 16 * nh
            cme, cdep = ownc(t, a, n)
            onehot = T.OH[:, 0:4096].indirect(cut(T.pL, t, 16, h0, nh))
            tt("selc" + e, part("pL", h0, nh) + ["oh1", "oh2", "oh3"] + cdep, T.sel[:, t, 0, a:a + n], onehot, cme, A.mult)
            tt("self" + e, part("pL", h0, nh) + ["oh1", "oh2", "oh3", "fJ" + s], T.sel[:, t, 1, :] if t < 2 else T.selF[:, t - 2:V:2], onehot, cut(T.fJ, t, 256), A.mult)
            sg, sgd, pA = cut(T.sg, t, 16), part("sg", h0, nh), T.pN[:, 128:129]
            if not last:
                count = [(pA, T.w[:], T.rsum[:, 2 * t + p:2 * t + p + 1], p == 0, False) for p in range(KEYS[t])] + [(pA, T.w[0:1, :], T.wk[0:1, :], False, True)]
                mm("a" + s, ["w", "wk"] + sgd, ["pN"] + count)
            if t < 2:
                sums = [(T.pN[:, 32:64], sel(T.Z1, lo), T.sel[:, t, :, lo:256:16], lo == 0, lo == 15) for lo in range(16)]
                mm("b" + e, ["selc" + e, "self" + e, "Z1", "Ik"] + sgd, ["pN"] + sums[:15] + [(T.pN[:, 48:64], T.Ik[:], sg, False, False)] + sums[15:])
                tt("zE" + e, ["e1_" + s], cut(T.zA, t, 32), T.pN[:, 32:64], cut(T.W, t, 32), A.max, bank="pN")
                ts("zI" + e, ["zE" + e], T.zI[:, t, :, :], cut(T.zA, t, 32), NS - 1, A.bitwise_and)
                copy("V", "zL" + e, ["zI" + e], cut(T.zL, t, 32), T.zI[:, t, :, :])
            else:
                bank, pc_ = ("pL2", T.pL2[:, 0, 0:2, :]) if last else ("pN", T.pN[:, 32:48])
                mm("b" + e, ["selc" + e], [bank] + [(pc_, sel(T.Z1, lo), T.sel[:, t, 0, lo:256:16], lo == 0, lo == 15) for lo in range(16)])
                copy("V", "zL" + e, [], cut(T.zL, t, 32, 0, 16), pc_, bank=bank)
            if not last:
                ts("fl" + n1, [], T.fl[:, t + 1:t + 2], pA, 2.0 ** 39 - 32768, A.add, 2.0 ** 39 + 524288, A.subtract, bank="pN")
                if KEYS[t + 1] == 2:
                    copy("S", "c1_" + n1, [], T.c1[:, t + 1:t + 2], pA, bank="pN")
            b0, nb = h0 // 2, nh // 2
            op("V", "rT" + e, part("rej", h0, nh), lambda: vec.transpose(T.rejT[:, t * 8 + b0:t * 8 + b0 + nb, :, :], cut(T.rej, t, 256, a, n)))
            pM, pC = T.pM[:, b0:b0 + nb, :, :], T.pM[:, 8 + b0:8 + b0 + nb, :, :]
            mm("m" + e, ["rT" + e, "Gm0", "Gm1"], ["pM"] + [(T.pM[:, b0:b0 + nb, h, :], shift("Gm", h, w), T.rejT[:, t * 8 + b0:t * 8 + b0 + nb, w, :], w == 0, w == 1)
                                                           for h in range(2) for w in range(2)])
            mk, t1 = cut(T.mk, t, 256, a, n), cut(T.t1, t, 256, a, n)
            op("S", "mk" + e, [], lambda: act.activation(mk, pM, F.Sign, bias=-6.5), bank="pM")
            bank, pC = ("pS1", T.pS1[:, 0:n]) if last else ("pM", pC)
            calls = [(pC, T.Ib[:], cme, True, False), (pC, row["kilo"], T.rows[0:1, 0:n], False, False), (pC, T.Ik2[:], mk, False, True)]
            if last:
                mm("mb" + e, cdep, [bank] + calls[:2])
            mm("mc" + e, ["mk" + e, "Ib", "Ik2", "one", "kilo"] + cdep + ["mb" + e] * last, [bank] + calls[2 * last:])
            conv = ["cv" + s + k for k in "abcd"] if t else []
            came = [] if t else [ld("cas")] + [("ca0_%d" % r, len(eng)) for r in range(len(T.cores)) if r != q]
            tt("t1" + e, ["zL" + e, "mk" + e] + conv, t1, T.CT[:, 0:4 * V].indirect(cut(T.zL, t, 32, h0, nh)), mk, A.mult, came)
            tt("cn" + e, ["t1" + e] + (["ce2"] if last else []), T.cout[:, 2 * a + 1:2 * (a + n):2] if last else own(T.CH, t, a, n), pC, t1, A.max, bank=bank)
            if last:
                op("Y", "st_c" + sp, ["cn" + e], lambda: g.sync.dma_start(T.yc[:, 2 * a:2 * (a + n)], T.cout[:, 2 * a:2 * (a + n)]).then_inc(T.sem.stored, 16))

        for p in pieces(KEYS[t]):
            keys(*p)
        for p in pieces(FEATS[t]):
            features(*p)
        for p in pieces(CASTS[t]):
            casts(*p)
        if t == 1:
            op("V", "eT1", ["zI0a", "zI1a"], lambda: vec.transpose(T.eT[:], T.zI[:, :, 1, :]))
            copy("V", "eH1", ["eT1"], T.eH[:], T.eT[:])
            mm("ef1", ["eH1", "G0", "G1"], ["pN"] + [(T.pN[:, 64 + p:96:2], shift("G", p, w), cut(T.eH, w, 16), w == 0, w == 1) for p in range(2) for w in range(2)])
            copy("S", "eu1", [], T.eU[:], T.pN[:, 64:96], bank="pN")
        if last:
            op("V", "sT3", letters("sg", 2, KEYS) + letters("sg", 3, KEYS), lambda: vec.transpose(T.sT[:], T.sg[:, 32:64]))
            mm("be3", ["self2a", "self3a", "sT3", "Gk0", "Gk1"],
               ["pS0"] + [(T.pS0[:, 0:32], sel(T.Z1, hi), cut(T.selF, hi, 32), hi == 0, False) for hi in range(16)]
               + [(T.pS0[:, p:32:2], shift("Gk", p, w), cut(T.sT, w, 16), False, p + w == 2) for p in range(2) for w in range(2)])
            tt("zE3a", ["eu1"], cut(T.zA, 3, 32), T.pS0[:, 0:32], T.eU[:], A.max, bank="pS0")
            ts("zI3a", ["zE3a"], T.eT[:], cut(T.zA, 3, 32), NS - 1, A.bitwise_and)
            scale("eo3", ["zI3a"], T.eout[:], T.eT[:], 1.0)
            op("Y", "st_e", ["eo3"], lambda: g.sync.dma_start(T.ye[:], T.eout[:]).then_inc(T.sem.stored, 16))
        else:
            ygather(t + 1)
            send_casts(t + 1, ["cn" + s + "a"], own(T.CH, t))
            widen(t + 1, ["cn" + s + "a", "t1" + s + "a"])
        if t < 2:
            prepare(t + 2)
        if t == 2:
            gcopy("xe2", letters("xn", 2, FEATS), T.xout[:, 0:V:2], own(T.XT, 0), 256)
            gcopy("ce2", ["cn2a"], T.cout[:, 0:V:2], own(T.CH, 2), 256)
    return ops, sent[0]


def out_engines(topo, core, dsts):
    return [e for e in topo.engines(core, dsts[0]) if all(e in topo.engines(core, c) for c in dsts)]


def helper(topo, core):
    return [c for c in topo.cores_of(core) if topo.die(c) != topo.die(core)][0]


def write(g, topo, part, dsts, engs, sem, left):
    ids = [DstId(rid=topo.addr(c)[0], pnc=topo.addr(c)[1]) for c in dsts]
    return g.remote_dma_fused([RemoteDMATransfer(dst_ids=ids, dma_engine_mask=sum(1 << e for e in engs), remote_sem=sem,
                                                 srcs=[part], dsts=[part] * len(ids))], local_sem=left)


def hand_on(g, core, rank_core, T, topo):
    q = T.rank_of(rank_core)
    others = [T.cores[(q + k) % len(T.cores)] for k in range(1, len(T.cores))]
    eng = out_engines(topo, core, others)
    came = len([e for e in topo.engines(rank_core, core) if e not in out_engines(topo, rank_core, others)])
    g.wait_ge(T.sem.handed, came)
    write(g, topo, T.CT[:, q * V:(q + 1) * V], others[DIRECT:], eng, T.sem["ca0_%d" % q], T.sem.sent)
    g.wait_ge(T.sem.sent, len(eng))


def arrange(ops):
    order = {e: [n for n in ops if ops[n][0] == e] for e in "VSPGY"}
    order["Y"].sort(key=lambda n: STORES.index(n) if n in STORES else -1)
    for e, (first, each, final) in ORDER.items():
        names = first.split()
        for r in range(RO):
            for tok in (final if r == RO - 1 else each).split():
                n, d = (tok + "@0").split("@")[:2]
                n = n.replace("#", str(r + int(d)))
                if n in order[e] and n not in names:
                    names.append(n)
        assert sorted(names) == sorted(order[e]), (e, sorted(set(names) ^ set(order[e])))
        order[e] = names
    return order


def emit(g, T, ops, order, sent):
    queue = {"V": g.vector, "S": g.scalar, "P": g.tensor, "G": g, "Y": g.sync}
    counter = {"V": "cV", "S": "cS", "P": "cP", "G": "cG"}
    needed = set(d for o in ops.values() for d in o[2] if not (o[0] == "P" and ops[d][0] == "P"))
    count = {}
    for e, names in order.items():
        k = 0
        for name in names:
            if name in needed:
                k += 1
                count[name] = k
    for e, names in order.items():
        seen = {}
        for name in names:
            _, fn, deps, ext = ops[name]
            want = {}
            for d in deps:
                if e == "P" and ops[d][0] == "P":
                    assert names.index(d) < names.index(name)
                    continue
                k = counter[ops[d][0]]
                want[k] = max(want.get(k, 0), count[d])
            for k, v in ext:
                want[k] = max(want.get(k, 0), v)
            for k, v in want.items():
                if seen.get(k, 0) < v:
                    queue[e].wait_ge(T.sem[k], v)
                    seen[k] = v
            ins = fn()
            if name in count:
                ins.then_inc(T.sem[counter[e]], 1)
    g.wait_ge(T.sem.sent, sent)
    g.sync.wait_ge(T.sem.stored, 16 * len([n for n in ops if n.startswith("st_")]))


def rank_program(g, core, T, topo):
    if T.rank_of(core) is not None:
        ops, sent = build(g, core, T, topo)
        emit(g, T, ops, arrange(ops), sent)
    else:
        for c in T.cores:
            if helper(topo, c) == core:
                hand_on(g, core, c, T, topo)
